import numpy as np, ml_dtypes
CORES = [242,247,114,119]
N = 4
BF = ml_dtypes.bfloat16
def gentries(a):
    return np.ascontiguousarray(a.reshape(8, 16, -1).transpose(0, 2, 1)).reshape(8, -1)
def gtable(e):
    e = np.asarray(e); return np.ascontiguousarray(e.reshape(8, -1, 16).transpose(0, 2, 1)).reshape(128, -1).astype(np.int32)
W, UN, P, SH, MS = 4096, 128, 32, 6, (2, 1)
def parts(rng):
    e = (0.5 + 2.5 * rng.random((N, 8, 16, 1))).astype(np.float32)
    sh = np.minimum(np.floor(256 * rng.random((N, 8, 16, W), dtype=np.float32) ** e), 255)
    return sh, rng.integers(0, W, (N, 8, UN, P))
def pack(sh, un):
    return {"shelf": np.ascontiguousarray(sh.reshape(N, 128, W)).astype(np.float32).astype(BF), "units": np.stack([gtable(a.reshape(8, -1)) for a in un])}
def setup_inputs(rng):
    sh, un = parts(rng)
    return pack(sh, un)
def setup_inputs_ties(rng):
    sh, un = parts(rng)
    sh = (rng.random((N, 8, 16, W)) < 0.03) * rng.choice(np.array([1, 7, 255]), (1, 8, 1, 1))
    sh[:, rng.integers(0, 8)] = 9
    return pack(sh, un)
def setup_inputs_alike(rng):
    sh, un = parts(rng)
    un[:, 0] = un[0, 0].copy()
    un[:, 1] = rng.choice(np.array([0, 1, W - 1, W // 2]), (N, UN, P))
    un[:, 2] = un[:, 2, :1].copy()
    un[:, 3] = un[:, 3, :, :1].copy()
    un[:, 4] = 0
    un[:, 5, 1::2] = un[:, 5, ::2].copy()
    un[:, 6, :, P // 2:] = un[:1, 6, :1, P // 2:].copy()
    return pack(sh, un)
def setup_inputs_ends(rng):
    sh, un = parts(rng)
    sh[:, :7] = sh[:1, :7].copy(); x = rng.integers(1, W, (N, 7, UN)); un[:, :7] = 0
    for g, e in enumerate((0, P - 1, P // 2 - 1, P // 2, 1, P - 2, int(rng.integers(0, P)))): un[:, g, :, e] = x[:, g]
    return pack(sh, un)
def setup_inputs_rare(rng):
    sh, un = parts(rng)
    few = W // (8 * P) * np.array([1, 2, 3, 4, 2, 3])[:, None, None]
    hit = np.argsort(rng.random((N, 6, 1, W)), axis=-1) < few
    v = rng.integers(1, 256, (N, 6, 16, W)); v[:, 0] = 1; v[:, 1] = 255
    v = np.where(hit, v, 0); v[:, 4:] = 255 - v[:, 4:]
    sh[:, :6] = v
    sh[:, 6] = rng.choice(np.array([0, 1, 2, 253, 254, 255]), (N, 16, W))
    sh[:, 7] = np.clip(rng.integers(-64, 320, (N, 16, W)), 0, 255)
    sh = np.where((sh == 0) & (rng.random(sh.shape, dtype=np.float32) < 0.5), np.float32(-0.0), sh)
    return pack(sh, un)
def setup_inputs_spread(rng):
    sh, un = parts(rng)
    k = np.exp2(8 * rng.random((N, 8, 1, W))) * (rng.random((N, 8, 1, W)) > 0.0625)
    sh = np.minimum(np.floor(rng.random((N, 8, 16, W)) * k), 255)
    un = np.minimum((W * rng.random((N, 8, UN, P)) ** rng.choice(np.array([1, 2, 4, 8]), (N, 8, 1, 1))).astype(np.int64), W - 1)
    return pack(sh, un)
def check_inputs(d):
    bad = []; v = np.asarray(d["shelf"]).astype(np.float32)
    if not np.all((v >= 0) & (v <= 255) & (v == np.floor(v))): bad.append("values of shelf")
    if np.min(d["units"]) < 0 or np.max(d["units"]) > W - 1: bad.append("range of units")
    return bad
def reference(shelf, units):
    tab = np.ascontiguousarray(shelf.astype(np.float32).astype(np.int16).reshape(N, 8, 16, W).transpose(0, 1, 3, 2))
    un = np.stack([gentries(a) for a in units]).astype(np.int64).reshape(N, 8, UN, P)
    A = np.zeros((N, 8), np.int64); rank = np.arange(N); place = np.arange(P)
    n3, g3 = rank[:, None, None], np.arange(8)[None, :, None]
    def measure(x):
        z = (A[:, :, None, None] + np.add.accumulate(x, axis=3)) & 4095
        c = ((z * z >> SH) + x) & (W - 1)
        b = tab[n3[..., None], g3[..., None], c]
        return np.sum((np.max(b, axis=3) - np.min(b, axis=3)).astype(np.int64), axis=3)
    for m in MS:
        mate = rank ^ m; low = (rank < mate)[:, None, None]
        q = measure(un)
        order = np.argsort(np.where(low, -q, q), axis=2, kind="stable")
        own = un[n3, g3, order]; qo = q[n3, g3, order]; far = own[mate]; qf = qo[mate]
        s0 = np.where(low, qo > qf, qf > qo)
        first = np.zeros((N, 8, UN), np.int64); n = P
        while n > 1:
            n = n // 2
            swapped = (place >= first[..., None]) & (place < first[..., None] + n)
            a = measure(np.where(swapped, far, own)); b = a[mate]
            s = np.where(low, a > b, b > a)
            first = np.where(s != s0, first, first + n)
        takes = np.where(low, qo < qf, qo <= qf)
        new = np.where(takes[..., None] & (place == first[..., None]), far, own)
        un = np.zeros_like(un); un[n3, g3, order] = new
        A = np.sum(first, axis=2)
    return {"yu": np.stack([gtable(a.reshape(8, -1)) for a in un]).astype(np.float32), "yq": q.astype(np.float32)}

@@ -1,0 +1,576 @@
+from concourse.bass import DstId, RemoteDMATransfer
+from concourse.mybir import dt, AluOpType as OP, AxisListType, ActivationFunctionType as AF
+
+NC, CU = 4, 32
+US, USM = 32, 24
+BIG = 786432.0
+HS = (16, 8, 4, 2, 1)
+SFROM = 5
+GR, VF, SFX, PEC, WAKE, ITERS = 1.56, 12.0, 65.0, 0.71, 110.0, 1
+LB = 1200.0
+SB = {"ga": -800.0, "mx": -800.0, "mn": -800.0, "mk": -800.0, "md": -800.0, "x": -800.0, "t": 800.0, "of": -800.0}
+
+F32M = ["mrow", "sm", "im", "idf", "le", "same", "pmt", "e1", "e2"]
+B16M = (["ineg", "i64b", "m16", "sameb", "ones", "sdp0", "sdn0", "sdp1", "sdn1", "lp0", "lp1", "ln0", "ln1"] + ["idh%d" % h for h in HS]
+        + ["dg%d" % t for t in range(1, 6)] + ["lk%d" % s for s in range(8)] + ["ql%d" % q for q in range(4)])
+H16M = ["tri", "onesb", "i64h", "idd", "pm0", "pm1", "dm0", "dm1"]
+COLF = ["pcf", "ps", "pi", "b1", "b2", "nb1", "nb2", "asum", "lam0", "lam1", "px0", "px1", "psx0", "psx1", "th0", "th1", "nl0", "nl1",
+        "va", "vb", "vv", "vt", "colr", "fc", "scl2", "ad0", "ad1", "scl1", "ad2"] + ["dc%d" % t for t in range(1, 6)]
+COLI = ["pc", "psi", "ii", "odd", "bit0", "bit1"] + ["fi%d" % h for h in (8, 4, 2, 1)]
+SCRATCH = {"cc": ("sbuf", [128, 8, 128], "bfloat16"), "st": ("dram", [512, 1024], "bfloat16"), "su": ("dram", [512, 64], "int32"),
+           "lsh": ("dram", [512, 1024], "bfloat16"), "lu": ("dram", [512, 64], "int32")}
+for _d, _l in (("float32", (("kf", 128 * len(F32M)), ("cf", len(COLF)), ("row8", 8), ("ind", 8), ("r2t", 8), ("r2f", 8), ("sq", 256), ("md", 256),
+                            ("pf", 128), ("nw", 256), ("kc", 8), ("src", 384), ("win", 384), ("ou", 256), ("sto", 256), ("lr", 256), ("yo", 256),
+                            ("qo", 128), ("lq", 512))),
+               ("bfloat16", (("kb", 128 * len(B16M)), ("r1", 4), ("r2", 8), ("negv", 512), ("cl", 128), ("cr", 128), ("mmx", 1024), ("mmn", 1024),
+                             ("sh0", 4096), ("shs", 4096), ("y", 256), ("ga", 4096), ("mx", 4096), ("mn", 4096), ("mk", 256), ("sp", 1280),
+                             ("sg", 256), ("nt", 256), ("dd", 128), ("dl", 512))),
+               ("float16", (("kh", 128 * len(H16M)), ("xo", 256), ("x", 256), ("wh", 384))),
+               ("int32", (("ci", len(COLI)), ("un0", 256), ("uns", 256), ("t3", 256), ("sf", 256))),
+               ("uint16", (("of", 256), ("po", 24)))):
+    for _n, _w in _l:
+        SCRATCH[_n] = ("sbuf", [128, _w], _d)
+for _i in range(4):
+    SCRATCH["pa%d" % _i] = ("psum", [128, 512], "float32")
+    SCRATCH["pb%d" % _i] = ("psum", [128, 512], "float32")
+LANE = "pw px y py sq t sf of ga gv mx mn pd sp pg pc mk md x pD sg nt nw pf dd".split()
+ONE = ("vk gk srcu xo pkc kc pk0 pk1 pk3 pkr0 pkr1 pkr3 cv cs pq sq_ pl po poq scat scq whq red un1 un2 dst dsu dun dsh dut douq dou "
+       "au ad aq loc").split()
+SEMAPHORES = [s + str(c) for s in LANE for c in range(NC)] + ONE + [s + str(q) for s in ("ash", "bs", "al") for q in range(4)]
+
+
+def vd(n, rate=1.0):
+    return max(64.0, n * rate) * 0.83 + VF
+
+
+def sd(n, rate=1.0):
+    return max(64.0, n * rate) * 0.83 + SFX
+
+
+def pe(n):
+    return n * (64 * PEC) + 10.0
+
+
+def rank_program(g, core, T, topo):
+    r = T.rank_of(core)
+    if r is None:
+        return
+    cores = list(T.cores)
+    others = [q for q in range(4) if q != r]
+    V, S, P = g.vector, g.scalar, g.tensor
+    tasks, lastw, readers, bank, count = [], {}, {}, {}, {}
+
+    def add(eng, sem, fn, reads=(), writes=(), banks=(), dur=60.0, lat=0.0, n=1, inc=1, extra=()):
+        i = len(tasks)
+        deps, soft = set(extra), set()
+        for k in list(reads) + list(writes):
+            if k in lastw:
+                deps.add(lastw[k])
+        for k in writes:
+            deps.update(readers.get(k, ()))
+        for b in banks:
+            st = bank.setdefault(b, {})
+            for e in [e for e in st if e != eng]:
+                deps.update(st.pop(e))
+            if eng in st:
+                soft.add(st[eng][-1])
+            st.setdefault(eng, []).append(i)
+        for k in reads:
+            readers.setdefault(k, []).append(i)
+        for k in writes:
+            lastw[k] = i
+            readers[k] = []
+        count[sem] = count.get(sem, 0) + n * inc
+        tasks.append(dict(eng=eng, sem=sem, val=count[sem], inc=inc, fn=fn, deps=deps, soft=soft - deps, dur=dur, lat=lat))
+        return i
+
+    def mats(buf, names):
+        return {n: buf[:, 128 * i:128 * i + 128] for i, n in enumerate(names)}
+    kf, kb, kh = mats(T.kf, F32M), mats(T.kb, B16M), mats(T.kh, H16M)
+    cf = {n: T.cf[:, i:i + 1] for i, n in enumerate(COLF)}
+    ci = {n: T.ci[:, i:i + 1] for i, n in enumerate(COLI)}
+    ob = B16M.index("ones") * 128
+    ones1, onesrow, ones8 = T.kb[:, ob:ob + 1], T.kb[0:1, ob:ob + 128], T.kb[0:1, ob:ob + 8]
+
+    def rows(q):
+        return slice(32 * q, 32 * q + 32)
+
+    def big(q):
+        return slice(128 * q, 128 * q + 128)
+    add("S", "dun", lambda: [S.dma_start(T.un0[:, :], T.units[:, :])], (), ["un0"], dur=100, lat=2000, inc=16)
+    add("Y", "dst", lambda: [g.sync.dma_start(T.st[big(q), :], T.shelf[rows(q), :]) for q in others], (), ["st"], dur=300, lat=4000, n=3, inc=16)
+    add("S", "dsu", lambda: [S.dma_start(T.su[big(q), :], T.units[rows(q), :]) for q in others], (), ["su"], dur=300, lat=2000, n=3, inc=16)
+    add("Y", "dsh", lambda: [g.sync.dma_start(T.sh0[:, :], T.shelf[:, :])], (), ["sh0"], dur=100, lat=7000, inc=16)
+    add("Y", "bs%d" % r, lambda: [g.sync.dma_start(T.shs[rows(r), :], T.shelf[rows(r), :])], (), ["shs%d" % r], dur=100, lat=8000, inc=16)
+
+    def split(p):
+        oth = [q for q in range(4) if q != p]
+        away = [q for q in oth if (topo.host(cores[q]), topo.chip(cores[q])) != (topo.host(cores[p]), topo.chip(cores[p]))]
+        offe = topo.engines(cores[p], cores[away[0]])
+        w = len(offe) // len(away)
+        res = {q: offe[k * w:k * w + w] for k, q in enumerate(away)}
+        for q in oth:
+            if q not in away:
+                res[q] = [e for e in topo.engines(cores[p], cores[q]) if e not in offe]
+        return res, away
+    eng_of, off = split(r)
+    near = [q for q in others if q not in off]
+
+    def send(reads, src_of, dst, sem):
+        def fn():
+            tr = []
+            for q in others:
+                rid, pid = topo.addr(cores[q], core)
+                tr.append(RemoteDMATransfer(dst_ids=[DstId(rid=rid, pnc=pid)], dma_engine_mask=sum(1 << e for e in eng_of[q]),
+                                            remote_sem=T.sem[sem], src=src_of(q), dst=dst))
+            g.remote_dma_fused(tr, local_sem=T.sem["loc"])
+            return []
+        return add("G", "loc", fn, reads, (), dur=1500, n=sum(len(eng_of[q]) for q in others))
+
+    def arrive(sem, qs, key, like, lat):
+        add("R", sem, None, (), [key], dur=0.0, lat=lat, n=sum(len(split(q)[0][r]) for q in qs), extra=[like])
+
+    prev = {}
+
+    def const(eng, sem, fn, reads, key, dur):
+        prev[sem] = add(eng, sem, lambda: [fn()], reads, [key], dur=dur, extra=[prev[sem]] if sem in prev else [])
+
+    def iota(key, out, pattern, cm, n, **kw):
+        const("G", "gk", lambda: g.iota(out, pattern, 0, cm, **kw), [], key, 130 + 1.66 * n)
+
+    def ts(key, out, in0, rk, s1, op0, s2=None, op1=None, n=128):
+        a = (out, in0, s1, None, op0) if op1 is None else (out, in0, s1, s2, op0, op1)
+        const("V", "vk", lambda: V.tensor_scalar(*a), rk.split(), key, vd(n))
+
+    def tc(name, in0, rk, *a):
+        ts(name, cf[name] if name in cf else ci[name], (cf[in0] if in0 in cf else ci[in0]), in0 + " " + rk, *a, n=1)
+
+    def tt(key, out, a, b, rk, op):
+        const("V", "vk", lambda: V.tensor_tensor(out, a, b, op), rk.split(), key, vd(256))
+
+    def ms(key, ap, v, n):
+        const("V", "vk", lambda: V.memset(ap, v), [], key, vd(n, 0.5))
+
+    def diag(name, out, v, rk=""):
+        ts(name, out, kf["mrow"], "mrow pcf " + rk, cf["pcf"], OP.is_equal, v, OP.mult)
+    small = dict(allow_small_or_imprecise_dtypes=True)
+    iota("pc", ci["pc"], [[0, 1]], 1, 1)
+    iota("mrow", kf["mrow"], [[1, 128]], 0, 128, **small)
+    iota("sm", kf["sm"], [[1, 8], [0, 16]], 0, 128, **small)
+    iota("im", kf["im"], [[0, 8], [1, 16]], 0, 128, **small)
+    ms("cl", T.cl[:, :], -512.0, 128)
+    ms("cr", T.cr[:, 0:64], 0.0, 64)
+    ms("cr", T.cr[:, 64:128], 256.0, 64)
+    tc("pcf", "pc", "", 1.0, OP.mult)
+    tc("psi", "pc", "", 4, OP.arith_shift_right)
+    tc("ii", "pc", "", 15, OP.bitwise_and)
+    tc("odd", "pc", "", 1, OP.bitwise_and)
+    tc("ps", "psi", "", 1.0, OP.mult)
+    tc("pi", "ii", "", 1.0, OP.mult)
+    tc("b1", "odd", "", -2048.0, OP.mult, BIG + 2048.0 - 2047.5, OP.add)
+    tc("b2", "odd", "", -2048.0, OP.mult, BIG + 2048.0, OP.add)
+    ts("same", kf["same"], kf["sm"], "sm ps", cf["ps"], OP.is_equal)
+    ts("le", kf["le"], kf["im"], "im pi", cf["pi"], OP.is_ge)
+    tt("tri", kh["tri"], kf["same"], kf["le"], "same le", OP.mult)
+    ts("onesb", kh["onesb"], kf["sm"], "sm ps", cf["ps"], OP.is_equal)
+    xok = ["xo%d" % c for c in range(NC)]
+    add("V", "xo", lambda: [V.tensor_scalar(T.xo[:, :], T.un0[:, :], -2048.0, None, OP.add)], ["un0"], xok, dur=vd(256))
+    diag("ineg", kb["ineg"], -1.0)
+    diag("i64h", kh["i64h"], 64.0)
+    ms("mmx", T.mmx[:, :], 0.0, 1024)
+    ms("mmx", T.mmx[:, 0:1024:32], -512.0, 32)
+    ms("mmn", T.mmn[:, :], 0.0, 1024)
+    ms("mmn", T.mmn[:, 0:1024:32], 512.0, 32)
+
+    s_u = send(["su"], lambda q: T.su[big(q), :], T.lu[big(r), :], "au")
+    s_s = send(["st"], lambda q: T.st[big(q), :], T.lsh[big(r), :], "ash%d" % r)
+    iota("row8", T.row8[:, :], [[1, 8]], 0, 8, **small)
+    iota("negv", T.negv[0:1, :], [[0, 4], [-1, 128]], 0, 512, **small)
+    arrive("au", others, "lu", s_u, 3500.0)
+    add("Y", "dut", lambda: [g.sync.dma_start(T.uns[rows(q), :], T.units[rows(r), :] if q == r else T.lu[big(q), :]) for q in range(4)],
+        ["lu"], ["uns"], dur=400, lat=2000, n=4, inc=16)
+
+    def bounce(q):
+        arrive("ash%d" % q, [q], "lsh%d" % q, s_s, 6000.0 if q in near else 10000.0)
+        add("Y", "bs%d" % q, lambda: [g.sync.dma_start(T.shs[rows(q), :], T.lsh[big(q), :])], ["lsh%d" % q], ["shs%d" % q], dur=100, lat=3000, inc=16)
+    for q in near + off:
+        bounce(q)
+    slots = ["shs%d" % q for q in range(4)]
+
+    def measure(c, xb, xkey, shelf, skeys, b1, b2, us):
+        a, bk, b, o, v = T["pa%d" % c], ["pa%d" % c], T["pb%d" % c], 64 * c, 1024 * c
+        X, X0, X1, XY = a[:, 0:128], a[:, 0:64], a[:, 64:128], b[:, 384:448]
+        C = str(c)
+        w, wo = slice(o, o + 64), slice(o, o + 64, 2)
+        add("P", "pw" + C, lambda: [P.matmul(XY, kh["tri"], xb[:, w], True, False), P.matmul(b[:, 385:448:2], kh["onesb"], xb[:, wo], False, True)],
+            [xkey, "tri", "onesb"], (), ["pb" + C], dur=pe(2), n=2)
+        add("V", "y" + C, lambda: [V.tensor_scalar(T.y[:, w], XY, cf[b1], None, OP.add)], [b1], ["y" + C], ["pb" + C], dur=vd(64))
+        add("P", "px" + C, lambda: [P.matmul(X, T.cl[0:1, :], T.cr[0:1, :], True, False), P.matmul(X1, kh["i64h"], xb[:, w], False, False),
+                                    P.matmul(X0, kh["tri"], xb[:, w], False, False), P.matmul(a[:, 1:64:2], kh["onesb"], xb[:, wo], False, False)],
+            [xkey, "tri", "onesb", "cl", "cr", "i64h"], (), bk, dur=pe(5), n=4)
+        add("P", "py" + C, lambda: [P.matmul(X0, kb["ineg"], T.y[:, w], False, True)], ["y" + C, "ineg"], (), bk, dur=pe(1))
+        add("S", "sq" + C, lambda: [S.activation(T.sq[:, w], X0, AF.Square, bias=cf[b2])], [b2], ["sq" + C], bk, dur=sd(64))
+        add("V", "t" + C, lambda: [V.tensor_tensor(T.t3[:, w], T.sq[:, w], X1, OP.add)], ["sq" + C], ["t3" + C], bk, dur=vd(64))
+        add("V", "sf" + C, lambda: [V.tensor_scalar(T.sf[:, w], T.t3[:, w], 6, 4095, OP.arith_shift_right, OP.bitwise_and)], ["t3" + C], ["sf" + C],
+            dur=vd(64))
+        add("V", "of" + C, lambda: [V.tensor_copy(T.of[:, w], T.sf[:, w])], ["sf" + C], ["of" + C], dur=vd(64))
+        m = v + 32 * us
+        add("S", "ga" + C, lambda: [S.activation(T.ga[:, v:m], shelf[:, :].indirect(T.of[:, o:o + 2 * us]), AF.Copy)],
+            ["of" + C] + skeys, ["gas" + C], dur=sd(32 * us, GR))
+        gk = ["gas" + C]
+        if us < CU:
+            gk.append("gav" + C)
+            add("V", "gv" + C, lambda: [V.tensor_copy(T.ga[:, m:v + 1024], shelf[:, :].indirect(T.of[:, o + 2 * us:o + 64]))],
+                ["of" + C] + skeys, ["gav" + C], dur=50 + vd(32 * (CU - us), GR))
+        z = slice(v, v + 1024)
+        gr = ["gas" + C, "gav" + C]
+        add("V", "mx" + C, lambda: [V.tensor_tensor_scan(T.mx[:, z], T.mmx[:, :], T.ga[:, z], 0.0, OP.add, OP.max)], gr + ["mmx"], ["mx" + C],
+            dur=vd(1024, 0.5))
+        add("V", "mn" + C, lambda: [V.tensor_tensor_scan(T.mn[:, z], T.mmn[:, :], T.ga[:, z], 0.0, OP.add, OP.min)], gr + ["mmn"], ["mn" + C],
+            dur=vd(1024, 0.5))
+
+    def ext(buf, c):
+        return buf[:, 1024 * c + 31:1024 * c + 1024:32]
+
+    def measure_all(shelf, skeys, b1, b2):
+        for c in range(NC):
+            measure(c, T.xo, "xo%d" % c, shelf, skeys, b1, b2, USM)
+            add("V", "dd%d" % c, (lambda c: lambda: [V.tensor_tensor(T.dd[:, 32 * c:32 * c + 32], ext(T.mx, c), ext(T.mn, c), OP.subtract)])(c),
+                ["mx%d" % c, "mn%d" % c], ["dd%d" % c], dur=vd(64))
+    measure_all(T.sh0, ["sh0"], "b1", "b2")
+
+    ms("ones", kb["ones"], 1.0, 128)
+    ts("ind", T.ind[:, :], T.row8[:, :], "row8 ps", cf["ps"], OP.is_equal, 128.0, OP.mult, n=8)
+    ts("r1", T.r1[:, 0:2], T.ind[:, 2 * r:2 * r + 2], "ind", 1.0, OP.mult, n=2)
+    ts("r1", T.r1[:, 2:4], T.ind[:, 2 * r:2 * r + 2], "ind", -1.0, OP.mult, n=2)
+    for b in (0, 1):
+        ts("lp%d" % b, kb["lp%d" % b], kf["mrow"], "mrow ind", 0.0, OP.mult, T.ind[:, 2 * r + b:2 * r + b + 1], OP.add)
+        ts("ln%d" % b, kb["ln%d" % b], kb["lp%d" % b], "lp%d" % b, -1.0, OP.mult)
+    tc("va", "ps", "", float(2 * r), OP.is_ge)
+    tc("vb", "ps", "", float(2 * r + 1), OP.is_le)
+    tc("vv", "va", "vb", cf["vb"], OP.mult)
+    tc("vt", "ps", "", float(100 - 2 * r), OP.add)
+    tc("colr", "vt", "vv", cf["vv"], OP.mult, -100.0, OP.add)
+    for q in range(4):
+        ts("ql%d" % q, kb["ql%d" % q], kf["sm"], "sm colr", float(2 * q), OP.subtract, cf["colr"], OP.is_equal)
+    tc("fc", "ps", "", float(SFROM), OP.is_ge)
+    tc("scl2", "fc", "", -1.0, OP.mult, 2.0, OP.add)
+    tc("ad0", "fc", "", 127.0, OP.mult)
+    tc("ad1", "fc", "", 127.0, OP.mult, 1.0, OP.add)
+    tc("scl1", "fc", "", -0.5, OP.mult, 1.0, OP.add)
+    tc("ad2", "fc", "", 63.5, OP.mult)
+    ms("win", T.win[:, 0:256], 0.0, 512)
+    ms("winq", T.win[:, 256:384], 0.0, 256)
+    for k, sh in ((0, 6), (1, 5)):
+        tc("bit%d" % k, "pc", "", sh, OP.arith_shift_right, 1, OP.bitwise_and)
+        tc("lam%d" % k, "bit%d" % k, "", -2.0, OP.mult, 1.0, OP.add)
+    diag("idf", kf["idf"], 1.0)
+    diag("idd", kh["idd"], 1.0)
+
+    def round_consts(k):
+        K = str(k)
+        tc("px" + K, "lam" + K, "pcf", (64.0, 32.0)[k], OP.mult, cf["pcf"], OP.add)
+        ts("pm" + K, kh["pm" + K], kf["mrow"], "mrow px" + K, cf["px" + K], OP.is_equal)
+        ts("pmt", kf["pmt"], kf["mrow"], "mrow px" + K, cf["px" + K], OP.is_equal)
+        tt("dm" + K, kh["dm" + K], kf["pmt"], kf["idf"], "idf pmt", OP.subtract)
+        tc("nl" + K, "lam" + K, "", -1.0, OP.mult)
+        tc("th" + K, "lam" + K, "", 0.5, OP.mult)
+        tc("psx" + K, "lam" + K, "ps", (4.0, 2.0)[k], OP.mult, cf["ps"], OP.add)
+        ts("e1", kf["e1"], kf["sm"], "sm ps lam" + K, cf["ps"], OP.is_equal, cf["lam" + K], OP.mult)
+        ts("e2", kf["e2"], kf["sm"], "sm psx%s lam%s" % (K, K), cf["psx" + K], OP.is_equal, cf["lam" + K], OP.mult)
+        tt("sdp" + K, kb["sdp" + K], kf["e1"], kf["e2"], "e1 e2", OP.add)
+        ts("sdn" + K, kb["sdn" + K], kb["sdp" + K], "sdp" + K, -1.0, OP.mult)
+    round_consts(0)
+    diag("m16", kb["m16"], -16.0)
+    for t in range(1, 6):
+        h = HS[t] if t < 5 else 1
+        if t < 5:
+            tc("fi%d" % h, "pc", "", 16 - h, OP.bitwise_and)
+        tc("dc%d" % t, "fi%d" % h, "", -1.0, OP.mult, 16.0 - h if t < 5 else 15.5, OP.add)
+        diag("dg%d" % t, kb["dg%d" % t], cf["dc%d" % t], "dc%d" % t)
+        diag("idh%d" % HS[t - 1], kb["idh%d" % HS[t - 1]], float(HS[t - 1]))
+    diag("i64b", kb["i64b"], 64.0)
+
+    dkeys = ["dd%d" % c for c in range(NC)]
+    s_d = send(dkeys, lambda q: T.dd[:, :], T.dl[:, big(r)], "ad")
+    arrive("ad", others, "dl", s_d, 3500.0)
+    add("V", "srcu", lambda: [V.tensor_scalar(T.src[:, 128 * e:128 * e + 128], T.uns[:, e:256:2], -2048.0, None, OP.add) for e in (0, 1)],
+        ["uns"], ["srcA", "srcB"], dur=2 * vd(128), n=2)
+
+    def order(k):
+        pa2 = T.pa2
+        dq = [T.dd[:, :] if q == r or k else T.dl[:, big(q)] for q in range(4)]
+        dk = dkeys + ([] if k else ["dl"])
+        lks = ["lk%d" % s for s in range(8)] if k else ["lp0", "lp1", "ln0", "ln1"]
+
+        def lk(s):
+            return kb["lk%d" % s] if k else kb[("lp%d" if s < 4 else "ln%d") % (s % 2)]
+
+        def kcol():
+            o = [P.matmul(pa2[:, 0:8], T.negv[0:1, 0:128], ones8, True, False)]
+            if k:
+                return o + [P.matmul(pa2[:, 0:8], T.dd[:, :], T.r2[:, :], False, True)]
+            for q in range(4):
+                w = 0 if q < 2 else 2
+                o.append(P.matmul(pa2[:, 2 * q:2 * q + 2], dq[q], T.r1[:, w:w + 2], False, q == 3))
+            return o
+        places = [("pa0", list(range(0, 4))), ("pa1", list(range(SFROM, 8))), ("pa3", list(range(4, SFROM)))]
+
+        def kconst(bn, n):
+            add("P", "pk" + bn[2], lambda: [P.matmul(T[bn][:, 0:128 * n], onesrow, T.negv[0:1, 0:128 * n], True, False)], ["negv", "ones"], (), [bn],
+                dur=pe(2 * n))
+
+        def krow(bn, ss):
+            add("P", "pkr" + bn[2], lambda: [P.matmul(T[bn][:, big(j)], lk(s), dq[s // 2], False, j == len(ss) - 1) for j, s in enumerate(ss)],
+                dk + lks, (), [bn], dur=pe(2 * len(ss)), n=len(ss))
+
+        def compare(bn, j, s):
+            src, out = T[bn][:, big(j)], T.cc[:, :, 16 * s:16 * s + 16]
+            if bn == "pa1":
+                add("S", "cs", lambda: [S.activation(out, src, AF.Sign, bias=T.kc[:, s:s + 1], scale=-1.0)], ["kc"], ["cc%d" % s], [bn], dur=sd(128))
+            else:
+                add("V", "cv", lambda: [V.tensor_scalar(out, src, T.kc[:, s:s + 1], None, OP.is_lt)], ["kc"], ["cc%d" % s], [bn], dur=vd(128))
+        for bn, ss in places:
+            kconst(bn, len(ss))
+        add("P", "pkc", kcol, dk + ["negv", "ones", "r2" if k else "r1"], (), ["pa2"], dur=pe(3), n=2 if k else 5)
+        add("V", "kc", lambda: [V.tensor_copy(T.kc[:, :], pa2[:, 0:8])], (), ["kc"], ["pa2"], dur=vd(8))
+        for bn, ss in places:
+            krow(bn, ss)
+        for bn, ss in places:
+            for j, s in enumerate(ss):
+                compare(bn, j, s)
+        qr = T.pb0[:, 0:128]
+        if k:
+            add("P", "pq", lambda: [P.matmul(qr, kb["sameb"], T.dd[:, :], True, True)], dk + ["sameb"], (), ["pb0"], dur=pe(2))
+        else:
+            add("P", "pq", lambda: [P.matmul(qr, kb["ql%d" % q], dq[q], q == 0, q == 3) for q in range(4)], dk + ["ql%d" % q for q in range(4)], (),
+                ["pb0"], dur=pe(8), n=4)
+        sq = add("S", "sq_", lambda: [S.activation(T.src[:, 256:384], qr, AF.Identity, bias=-2048.0)], (), ["srcq"], ["pb0"], dur=sd(128))
+        if k:
+            add("S", "sq_", lambda: [S.activation(T.qo[:, :], qr, AF.Copy)], (), ["qo"], ["pb0"], dur=sd(128), extra=[sq])
+        add("P", "pl", lambda: [P.matmul(pa2[:, 8 + j:9 + j], T.cc[:, j, :], ones1, True, True) for j in range(8)],
+            ["cc%d" % s for s in range(8)] + ["ones"], (), ["pa2"], dur=pe(8), n=8)
+
+        def lists(sem, key, js, ab):
+            add("V", sem, lambda: [V.tensor_scalar(T.po[:, 8 * j:8 * j + 8], pa2[:, 8:16], cf[a], cf[b], OP.mult, OP.add) for j, (a, b) in zip(js, ab)],
+                [x for y in ab for x in y], [key], ["pa2"], dur=len(js) * vd(8), n=len(js))
+        lists("po", "po", (0, 1), [("scl2", "ad0"), ("scl2", "ad1")])
+        add("V", "scat", lambda: [V.tensor_copy(T.win[:, 0:256].indirect(T.po[:, 0:16]), T.src[:, 0:256])], ["po", "srcA", "srcB"], ["win"],
+            dur=50 + vd(256, 3.0))
+        for c in range(NC):
+            add("V", "nw%d" % c, (lambda w: lambda: [V.tensor_copy(T.wh[:, w], T.win[:, w])])(slice(64 * c, 64 * c + 64)), ["win"], ["wh%d" % c], dur=vd(64))
+        lists("poq", "poq", (2,), [("scl1", "ad2")])
+        add("V", "scq", lambda: [V.tensor_copy(T.win[:, 256:384].indirect(T.po[:, 16:24]), T.src[:, 256:384])], ["poq", "srcq"], ["winq"],
+            dur=50 + vd(128, 3.0))
+        add("V", "whq", lambda: [V.tensor_copy(T.wh[:, 256:384], T.win[:, 256:384])], ["winq"], ["whq"], dur=vd(128))
+
+    def spap(c, t, st=1):
+        return T.sp[:, 320 * c + 64 * (t - 1):320 * c + 64 * t:st]
+
+    def pre_g(c, t):
+        C, w, b = str(c), slice(64 * c, 64 * c + 64), T["pb%d" % c]
+        G = b[:, 64:128]
+
+        def fn():
+            o = [P.matmul(G, kb["dg%d" % t], T.sg[:, w], True, False),
+                 P.matmul(b[:, 65:128:2], kb["m16"], T.sg[:, 64 * c + 1:64 * c + 64:2], False, False)]
+            for u in range(1, t):
+                o.append(P.matmul(G, kb["idh%d" % HS[u - 1]], spap(c, u), False, False))
+            if t == 5:
+                o.append(P.matmul(G, kb["i64b"], T.nt[:, w], False, False))
+            return o
+        n = t + 1 + (1 if t == 5 else 0)
+        add("P", "pg" + C, fn, ["sg" + C, "dg%d" % t, "m16"] + ["sp%d_%d" % (c, u) for u in range(1, t)] + ["idh%d" % HS[u - 1] for u in range(1, t)]
+            + (["i64b", "nt" + C] if t == 5 else []), (), ["pb" + C], dur=pe(n), n=n)
+
+    def first(k, c):
+        b, bk, o, W, C, K = T["pb%d" % c], ["pb%d" % c], 64 * c, T.wh, str(c), str(k)
+        add("P", "pD" + C, lambda: [P.matmul(b[:, 256:320:2], kh["pm" + K], W[:, o:o + 64:2], True, True),
+                                    P.matmul(b[:, 257:320:2], kh["idd"], W[:, o + 1:o + 64:2], True, True)],
+            ["wh" + C, "pm" + K, "idd"], (), bk, dur=pe(2), n=2)
+        add("V", "x" + C, lambda: [V.tensor_copy(T.x[:, o:o + 64], b[:, 256:320])], (), ["x" + C], bk, dur=vd(64))
+
+    def rest_of(k, c):
+        b, bk, o, W, C, K = T["pb%d" % c], ["pb%d" % c], 64 * c, T.wh, str(c), str(k)
+        dm, idd, dqp, w, qw = kh["dm" + K], kh["idd"], b[:, 320:384], slice(64 * c, 64 * c + 64), slice(256 + 32 * c, 288 + 32 * c)
+        add("P", "pD" + C, lambda: [P.matmul(b[:, 128:192], dm, W[:, w], True, True), P.matmul(b[:, 192:256], idd, W[:, w], True, True),
+                                    P.matmul(b[:, 320:384:2], dm, W[:, qw], True, True), P.matmul(b[:, 321:384:2], dm, W[:, qw], True, True)],
+            ["wh" + C, "whq", "dm" + K, "idd"], (), bk, dur=pe(4), n=4)
+        add("S", "sg" + C, lambda: [S.activation(T.sg[:, w], dqp, AF.Sign, bias=-0.5, scale=cf["nl" + K])], ["nl" + K], ["sg" + C], bk, dur=sd(64))
+        add("V", "nt" + C, lambda: [V.tensor_scalar(T.nt[:, w], dqp, cf["th" + K], None, OP.is_le)], ["th" + K], ["nt" + C], bk, dur=vd(64))
+
+    def trial(k, c, t, b1, b2):
+        b, bk, a, o, C, K = T["pb%d" % c], ["pb%d" % c], T["pa%d" % c], 64 * c, str(c), str(k)
+        w, w3, sp, h = slice(o, o + 64), slice(32 * c, 32 * c + 32), "sp%d_%d" % (c, t), "idh%d" % HS[t - 1]
+        measure(c, T.x, "x" + C, T.shs, slots, b1, b2, US)
+        if t == 1:
+            rest_of(k, c)
+        pre_g(c, t)
+        add("P", "pd" + C, lambda: [P.matmul(a[:, 128 + e:192:2], kb[n + K], ext(m, c), n == "sdp", n == "sdn")
+                                    for e in (0, 1) for n, m in (("sdp", T.mx), ("sdn", T.mn))],
+            ["mx" + C, "mn" + C, "sdp" + K, "sdn" + K], (), ["pa" + C], dur=pe(4), n=4)
+        add("V", "sp" + C, lambda: [V.tensor_scalar(spap(c, t), a[:, 128:192], 0.0, -0.5, OP.is_gt, OP.add)], (), [sp], ["pa" + C], dur=vd(64))
+        add("P", "pc" + C, lambda: [P.matmul(b[:, 64:128], kb[h], spap(c, t), False, True)], [sp, h], (), bk, dur=pe(1))
+        add("V", "mk" + C, lambda: [V.tensor_scalar(T.mk[:, w], b[:, 64:128], 0.0, None, OP.is_equal)], (), ["mk" + C], bk, dur=vd(64))
+        add("V", "md" + C, lambda: [V.tensor_tensor(T.md[:, w], T.mk[:, w], b[:, 128:192], OP.mult)], ["mk" + C], ["md" + C], bk, dur=vd(64))
+        nm, dst = ("x", T.x) if t < 5 else ("nw", T.nw)
+        add("V", nm + C, lambda: [V.tensor_tensor(dst[:, w], T.md[:, w], b[:, 192:256], OP.add)], ["md" + C],
+            [("x" if t < 5 else "new") + C], bk, dur=vd(64))
+        if t == 5 and k == 0:
+            add("P", "pD" + C, lambda: [P.matmul(b[:, 448:480], kb["idh%d" % HS[u - 1]], spap(c, u, 2), u == 1, u == 5) for u in range(1, 6)],
+                ["sp%d_%d" % (c, u) for u in range(1, 6)], (), bk, dur=pe(5), n=5)
+            add("V", "pf" + C, lambda: [V.tensor_tensor(T.pf[:, w3], T.sg[:, o:o + 64:2], b[:, 448:480], OP.mult)], ["sg" + C], ["pf" + C], bk, dur=vd(32))
+
+    def trials(k, b1, b2):
+        for c in range(NC):
+            first(k, c)
+        for t in range(1, 6):
+            for c in range(NC):
+                trial(k, c, t, b1, b2)
+    order(0)
+    trials(0, "b1", "b2")
+    ts("r2t", T.r2t[:, :], T.row8[:, :], "row8 ps lam1", cf["ps"], OP.is_equal, cf["lam1"], OP.mult, n=8)
+    ts("r2f", T.r2f[:, :], T.r2t[:, :], "r2t", 128.0, OP.mult, n=8)
+    ts("r2", T.r2[:, :], T.r2t[:, :], "r2t", 128.0, OP.mult, n=8)
+    for s in range(8):
+        ts("lk%d" % s, kb["lk%d" % s], kf["mrow"], "mrow r2f", 0.0, OP.mult, T.r2f[:, s:s + 1], OP.add)
+    ts("sameb", kb["sameb"], kf["sm"], "sm ps", cf["ps"], OP.is_equal)
+    round_consts(1)
+    nwk = ["new%d" % c for c in range(NC)] + ["po"]
+    add("S", "un1", lambda: [S.activation(T.src[:, 0:128], T.nw[:, :].indirect(T.po[:, 0:8]), AF.Copy)], nwk, ["srcA"], dur=sd(128, GR))
+    add("V", "un2", lambda: [V.tensor_copy(T.src[:, 128:256], T.nw[:, :].indirect(T.po[:, 8:16]))], nwk, ["srcB"], dur=50 + vd(128, GR))
+    add("V", "xo", lambda: [V.tensor_copy(T.xo[:, e:256:2], T.src[:, 128 * e:128 * e + 128]) for e in (0, 1)], ["srcA", "srcB"], xok, dur=2 * vd(128), n=2)
+    add("V", "red", lambda: [V.tensor_reduce(cf["asum"], T.pf[:, :], AxisListType.X, OP.add)], ["pf%d" % c for c in range(NC)], ["asum"], dur=vd(128))
+    add("V", "red", lambda: [V.tensor_scalar(cf["nb" + e], cf["asum"], cf["b" + e], 1984.0, OP.add, OP.add) for e in "12"], ["asum", "b1", "b2"],
+        ["nb1", "nb2"], dur=2 * vd(1), n=2)
+    measure_all(T.shs, slots, "nb1", "nb2")
+    order(1)
+    s_q = send(["qo"], lambda q: T.qo[:, :], T.lq[:, big(r)], "aq")
+    arrive("aq", others, "lq", s_q, 6000.0)
+
+    def yq():
+        o = []
+        for b in (0, 1):
+            p = 32 * r + 16 * b
+            for q in range(4):
+                s = T.qo[p:p + 1, :] if q == r else T.lq[p:p + 1, big(q)]
+                o.append(g.sync.dma_start(T.yq[2 * q + b:2 * q + b + 1, :], s))
+        return o
+    add("Y", "douq", yq, ["qo", "lq"], ["yq"], dur=800, lat=2000, n=8, inc=16)
+    trials(1, "nb1", "nb2")
+
+    add("S", "un1", lambda: [S.activation(T.ou[:, 0:256:2], T.nw[:, :].indirect(T.po[:, 0:8]), AF.Identity, bias=2048.0)], nwk, ["ouA"], dur=sd(128, GR))
+    add("V", "un2", lambda: [V.tensor_scalar(T.ou[:, 1:256:2], T.nw[:, :].indirect(T.po[:, 8:16]), 2048.0, None, OP.add)], nwk, ["ouB"],
+        dur=50 + vd(128, GR))
+
+    def copies(eng, sem, cps, reads, key):
+        def fn():
+            return [V.tensor_copy(d, s) if eng == "V" else S.activation(d, s, AF.Copy) for d, s in cps]
+        add(eng, sem, fn, reads, [key], dur=(vd(64) if eng == "V" else sd(64)) * len(cps), n=len(cps))
+    blocks = [(T.sto[32 * a:32 * a + 32, 64 * q:64 * q + 64], T.ou[rows(q), 64 * a:64 * a + 64]) for q in others for a in range(4)]
+    copies("V", "x0", blocks[:7], ["ouA", "ouB"], "stoV")
+    copies("S", "sq0", blocks[7:], ["ouA", "ouB"], "stoS")
+    s_o = send(["stoV", "stoS"], lambda q: T.sto[:, 64 * q:64 * q + 64], T.lr[:, 64 * r:64 * r + 64], "al%d" % r)
+    add("Y", "dou", lambda: [g.sync.dma_start(T.yu[rows(r), :], T.ou[rows(r), :])], ["ouA", "ouB"], ["yu"], dur=100, lat=2000, inc=16)
+
+    def back(j, q):
+        arrive("al%d" % q, [q], "lr%d" % q, s_o, 3000.0 + 500.0 * j)
+        cps = [(T.yo[rows(q), 64 * a:64 * a + 64], T.lr[32 * a:32 * a + 32, 64 * q:64 * q + 64]) for a in range(4)]
+        m = 3 if j < 2 else 2
+        copies("V", "x1", cps[:m], ["lr%d" % q], "yoV%d" % q)
+        copies("S", "sq1", cps[m:], ["lr%d" % q], "yoS%d" % q)
+        add("Y", "dou", lambda: [g.sync.dma_start(T.yu[rows(q), :], T.yo[rows(q), :])], ["yoV%d" % q, "yoS%d" % q], ["yu%d" % q], dur=100, lat=2000, inc=16)
+    for j, q in enumerate(near + off):
+        back(j, q)
+    return emit(T, dict(V=V, S=S, P=P, G=g, Y=g.sync), tasks, count)
+
+
+def place(tasks, pred, succ, key, back):
+    n = len(tasks)
+    need, st, busy = [len(p) for p in pred], [0.0] * n, {}
+    pool = set(i for i in range(n) if need[i] == 0)
+    while pool:
+        i = min(pool, key=lambda j: (key[j], j))
+        pool.discard(i)
+        t = tasks[i]
+        s, d = 0.0, t["dur"]
+        for p, hard in pred[i]:
+            s = max(s, st[p] + tasks[p]["dur"] + ((t if back else tasks[p])["lat"] + WAKE if hard else 0.0))
+        if t["eng"] != "R":
+            iv = busy.setdefault(t["eng"], [])
+            j = len(iv)
+            while j and iv[j - 1][1] > s:
+                j -= 1
+            while j < len(iv) and iv[j][0] < s + d - 0.001:
+                s = max(s, iv[j][1])
+                j += 1
+            iv.insert(j, (s, s + d))
+        st[i] = s
+        for q, _ in succ[i]:
+            need[q] -= 1
+            if need[q] == 0:
+                pool.add(q)
+    return st
+
+
+def bias(t):
+    x = t["sem"]
+    y = x.rstrip("0123456789")
+    return SB.get(y, 0.0) + (LB * (3 - int(x[len(y):])) if y != x and len(y) <= 2 and y in LANE else 0.0)
+
+
+def emit(T, E, tasks, count):
+    n = len(tasks)
+    pred, succ, before = [[] for _ in range(n)], [[] for _ in range(n)], {}
+    for i, t in enumerate(tasks):
+        if t["sem"] in before and tasks[before[t["sem"]]]["eng"] == t["eng"]:
+            t["soft"].add(before[t["sem"]])
+        before[t["sem"]] = i
+        for hard, ds in ((1, t["deps"]), (0, t["soft"] - t["deps"])):
+            for d in ds:
+                pred[i].append((d, hard))
+                succ[d].append((i, hard))
+    rest = [0.0] * n
+    for i in range(n - 1, -1, -1):
+        rest[i] = tasks[i]["dur"] + tasks[i]["lat"] + max([rest[j] + WAKE for j, h in succ[i] if h] or [0.0])
+    st = place(tasks, pred, succ, [-x - bias(t) for x, t in zip(rest, tasks)], False)
+    best = (1e18, None)
+    for k in range(ITERS + 1):
+        end = max(s + t["dur"] + t["lat"] for s, t in zip(st, tasks))
+        if end < best[0]:
+            best = (end, st)
+        if k < ITERS:
+            sb = place(tasks, succ, pred, [-(s + t["dur"]) for s, t in zip(st, tasks)], True)
+            st = place(tasks, pred, succ, [-(s + t["dur"]) for s, t in zip(sb, tasks)], False)
+    st, seq = best[1], {}
+    for i in sorted(range(n), key=lambda i: (st[i], i)):
+        seq.setdefault(tasks[i]["eng"], []).append(i)
+    clocks, after = {e: {} for e in E}, [None] * n
+    pos, left = {e: 0 for e in seq}, n
+    while left:
+        was = left
+        for e in seq:
+            while pos[e] < len(seq[e]):
+                i = seq[e][pos[e]]
+                t = tasks[i]
+                if any(after[d] is None for d in t["deps"]):
+                    break
+                ck = clocks.get(e, {})
+                if e != "R":
+                    for d in sorted(t["deps"], key=lambda d: -st[d]):
+                        sem, val = tasks[d]["sem"], tasks[d]["val"]
+                        if ck.get(sem, 0) < val:
+                            E[e].wait_ge(T.sem[sem], int(val))
+                            for s, v in after[d].items():
+                                ck[s] = max(ck.get(s, 0), v)
+                    for ins in t["fn"]():
+                        ins.then_inc(T.sem[t["sem"]], t["inc"])
+                after[i] = dict(ck)
+                after[i][t["sem"]] = max(ck.get(t["sem"], 0), t["val"])
+                pos[e] += 1
+                left -= 1
+        assert left < was
+    last = {t["sem"]: s + t["dur"] + t["lat"] for s, t in zip(st, tasks)}
+    for s in sorted(count, key=lambda s: (last[s], s)):
+        E["P"].wait_ge(T.sem[s], int(count[s]))
+    return seq, st, tasks

@@ -2,53 +2,53 @@ from concourse.bass import DstId, RemoteDMATransfer
 from concourse.mybir import dt, AluOpType as OP, AxisListType, ActivationFunctionType as AF
 
 NC, CU = 4, 32
-US, USM = 32, 24
 BIG = 786432.0
+SHIFT = 53 * 4096.0
 HS = (16, 8, 4, 2, 1)
+MS = (2, 1)
 SFROM = 5
-GR, VF, SFX, PEC, WAKE, ITERS = 1.56, 12.0, 65.0, 0.71, 110.0, 1
-LB = 1200.0
-SB = {"ga": -800.0, "mx": -800.0, "mn": -800.0, "mk": -800.0, "md": -800.0, "x": -800.0, "t": 800.0, "of": -800.0}
+CFG = dict(US=31, USM=28, CUT=0, CUTM=0, YE="V", GR=1.56, VF=12.0, SFX=65.0, PEC=0.6, WAKE=130.0, ITERS=0, Q=1440.0, N=(0, 12, 33, 44, 70),
+           PHI=dict(y=-3280.0, sq=-2500.0, t=-1740.0, sf=-3140.0, of=-2360.0, ga=-800.0, gb=-700.0, gv=300.0, mx=-1700.0, mn=700.0, mx_=900.0, mn_=1100.0,
+                    de=300.0, mi=1780.0))
 
-F32M = ["mrow", "sm", "im", "idf", "le", "same", "pmt", "e1", "e2"]
-B16M = (["ineg", "i64b", "m16", "sameb", "ones", "sdp0", "sdn0", "sdp1", "sdn1", "lp0", "lp1", "ln0", "ln1"] + ["idh%d" % h for h in HS]
-        + ["dg%d" % t for t in range(1, 6)] + ["lk%d" % s for s in range(8)] + ["ql%d" % q for q in range(4)])
-H16M = ["tri", "onesb", "i64h", "idd", "pm0", "pm1", "dm0", "dm1"]
-COLF = ["pcf", "ps", "pi", "b1", "b2", "nb1", "nb2", "asum", "lam0", "lam1", "px0", "px1", "psx0", "psx1", "th0", "th1", "nl0", "nl1",
-        "va", "vb", "vv", "vt", "colr", "fc", "scl2", "ad0", "ad1", "scl1", "ad2"] + ["dc%d" % t for t in range(1, 6)]
-COLI = ["pc", "psi", "ii", "odd", "bit0", "bit1"] + ["fi%d" % h for h in (8, 4, 2, 1)]
-SCRATCH = {"cc": ("sbuf", [128, 8, 128], "bfloat16"), "st": ("dram", [512, 1024], "bfloat16"), "su": ("dram", [512, 64], "int32"),
-           "lsh": ("dram", [512, 1024], "bfloat16"), "lu": ("dram", [512, 64], "int32")}
-for _d, _l in (("float32", (("kf", 128 * len(F32M)), ("cf", len(COLF)), ("row8", 8), ("ind", 8), ("r2t", 8), ("r2f", 8), ("sq", 256), ("md", 256),
-                            ("pf", 128), ("nw", 256), ("kc", 8), ("src", 384), ("win", 384), ("ou", 256), ("sto", 256), ("lr", 256), ("yo", 256),
-                            ("qo", 128), ("lq", 512))),
-               ("bfloat16", (("kb", 128 * len(B16M)), ("r1", 4), ("r2", 8), ("negv", 512), ("cl", 128), ("cr", 128), ("mmx", 1024), ("mmn", 1024),
-                             ("sh0", 4096), ("shs", 4096), ("y", 256), ("ga", 4096), ("mx", 4096), ("mn", 4096), ("mk", 256), ("sp", 1280),
-                             ("sg", 256), ("nt", 256), ("dd", 128), ("dl", 512))),
-               ("float16", (("kh", 128 * len(H16M)), ("xo", 256), ("x", 256), ("wh", 384))),
-               ("int32", (("ci", len(COLI)), ("un0", 256), ("uns", 256), ("t3", 256), ("sf", 256))),
-               ("uint16", (("of", 256), ("po", 24)))):
+F32M = ["mrow", "sm", "im", "idf", "le", "same", "tmp"]
+B16M = (["ineg", "idb", "sameb", "ones", "spr0", "spr1", "lr0", "lr1"] + ["br%d" % t for t in range(2, 6)] + ["dg%d" % t for t in range(1, 7)]
+        + ["lk%d" % s for s in range(8)] + ["w%d_%d" % (k, t) for k in (0, 1) for t in range(1, 7)] + ["ah%d" % t for t in range(1, 6)])
+H16M = ["tri", "onesb", "i64h", "idd"] + [n + k for n in ("pm", "dm", "tp", "op") for k in "01"]
+COLF = ["pcf", "ps", "pi", "k5", "u5", "fc", "ad0", "ad1", "ad2", "sa", "sb"] + [n + k for n in ("mu", "lam", "px", "psx", "spc", "s2_", "s1_", "d5_") for k in "01"]
+COLI = ["pc", "psi", "ii", "odd", "bit0", "bit1", "k5i", "u5i", "sai", "sbi"]
+SCRATCH = {"cc": ("sbuf", [128, 8, 128], "bfloat16"), "st": ("dram", [512, 1024], "bfloat16"), "lsh": ("dram", [512, 1024], "bfloat16")}
+for _d, _l in (("float32", (("kf", 128 * len(F32M)), ("cf", len(COLF)), ("row8", 8), ("ind", 8), ("sq", 256), ("md", 256), ("ee", 256), ("ea", 256),
+                            ("b4", 4), ("nb", 4), ("bf", 4), ("nf", 5), ("cum", 5), ("dc", 5), ("one5", 5), ("urow", 64),
+                            ("nw", 1024), ("kc", 8), ("src", 384), ("win", 384), ("ou", 256), ("qo", 144), ("lq", 576))),
+               ("bfloat16", (("kb", 128 * len(B16M)), ("r2", 8), ("num", 512), ("sg8", 16), ("cl", 128), ("cr", 400), ("mmx", 1024), ("mmn", 1024),
+                             ("sh0", 4096), ("y", 256), ("ga", 4096), ("mx", 4096), ("mn", 4096), ("mk", 256), ("wsp", 16),
+                             ("pat", 132), ("one0", 65), ("del", 64), ("pt", 528), ("tk", 256), ("de", 20 * 66), ("dd", 128), ("ds", 128), ("dl", 512))),
+               ("float16", (("kh", 128 * len(H16M)), ("xo", 256), ("lx", 1024), ("mi", 256), ("wh", 384))),
+               ("int32", (("ci", len(COLI)), ("bi", 4), ("un0", 256), ("t3", 256), ("sf", 256))),
+               ("uint16", (("of", 256), ("po", 48), ("ho", 16)))):
     for _n, _w in _l:
         SCRATCH[_n] = ("sbuf", [128, _w], _d)
 for _i in range(4):
     SCRATCH["pa%d" % _i] = ("psum", [128, 512], "float32")
     SCRATCH["pb%d" % _i] = ("psum", [128, 512], "float32")
-LANE = "pw px y py sq t sf of ga gv mx mn pd sp pg pc mk md x pD sg nt nw pf dd".split()
-ONE = ("vk gk srcu xo pkc kc pk0 pk1 pk3 pkr0 pkr1 pkr3 cv cs pq sq_ pl po poq scat scq whq red un1 un2 dst dsu dun dsh dut douq dou "
-       "au ad aq loc").split()
-SEMAPHORES = [s + str(c) for s in LANE for c in range(NC)] + ONE + [s + str(q) for s in ("ash", "bs", "al") for q in range(4)]
+LANE = "pw px pv py pz y sq t sf of ga gv mx mn pd pe de pg pc mi pt ea md dd".split()
+ONE = ("vk0 vk1 vk2 vk3 sk0 sk1 gk pu su xo pkc kc pk pr0 pr1 pr2 pr3 pr4 pr5 cv cs pq sq_ pl po poq scat scq pA nb un1 un2 ho "
+       "dun dst0 dst1 dst2 dsh dbo douq dou ax ash0 ash1 ash2 ad aq al loc").split()
+SEMAPHORES = [s + str(c) for s in LANE for c in range(NC)] + ONE
+FREE = ("cv", "cs", "loc", "dbo", "dou", "pk")
 
 
 def vd(n, rate=1.0):
-    return max(64.0, n * rate) * 0.83 + VF
+    return max(64.0, n * rate) * 0.83 + CFG["VF"]
 
 
 def sd(n, rate=1.0):
-    return max(64.0, n * rate) * 0.83 + SFX
+    return max(64.0, n * rate) * 0.83 + CFG["SFX"]
 
 
 def pe(n):
-    return n * (64 * PEC) + 10.0
+    return n * (64 * CFG["PEC"] + 8.0)
 
 
 def rank_program(g, core, T, topo):
@@ -56,9 +56,9 @@ def rank_program(g, core, T, topo):
     if r is None:
         return
     cores = list(T.cores)
-    others = [q for q in range(4) if q != r]
-    V, S, P = g.vector, g.scalar, g.tensor
-    tasks, lastw, readers, bank, count = [], {}, {}, {}, {}
+    V, S, P, Y = g.vector, g.scalar, g.tensor, g.sync
+    GR = CFG["GR"]
+    tasks, lastw, readers, bank, count, turn, now = [], {}, {}, {}, {}, {}, [0]
 
     def add(eng, sem, fn, reads=(), writes=(), banks=(), dur=60.0, lat=0.0, n=1, inc=1, extra=()):
         i = len(tasks)
@@ -66,6 +66,8 @@ def rank_program(g, core, T, topo):
         for k in list(reads) + list(writes):
             if k in lastw:
                 deps.add(lastw[k])
+            else:
+                assert k in writes, k
         for k in writes:
             deps.update(readers.get(k, ()))
         for b in banks:
@@ -81,7 +83,9 @@ def rank_program(g, core, T, topo):
             lastw[k] = i
             readers[k] = []
         count[sem] = count.get(sem, 0) + n * inc
-        tasks.append(dict(eng=eng, sem=sem, val=count[sem], inc=inc, fn=fn, deps=deps, soft=soft - deps, dur=dur, lat=lat))
+        kind = sem.rstrip("0123456789")
+        plan = now[0] * CFG["Q"] + CFG["PHI"][kind] if kind in CFG["PHI"] and "win" not in reads else None
+        tasks.append(dict(eng=eng, sem=sem, val=count[sem], inc=inc, fn=fn, deps=deps, soft=soft - deps, dur=dur, lat=lat, plan=plan))
         return i
 
     def mats(buf, names):
@@ -90,85 +94,98 @@ def rank_program(g, core, T, topo):
     cf = {n: T.cf[:, i:i + 1] for i, n in enumerate(COLF)}
     ci = {n: T.ci[:, i:i + 1] for i, n in enumerate(COLI)}
     ob = B16M.index("ones") * 128
-    ones1, onesrow, ones8 = T.kb[:, ob:ob + 1], T.kb[0:1, ob:ob + 128], T.kb[0:1, ob:ob + 8]
+    ones1, onesrow, ones64 = T.kb[:, ob:ob + 1], T.kb[0:1, ob:ob + 128], T.kb[:, ob:ob + 64]
+
+    def part(buf, names, n, a, b):
+        o = 128 * names.index(n)
+        return buf[:, o + a:o + b]
 
     def rows(q):
         return slice(32 * q, 32 * q + 32)
 
     def big(q):
         return slice(128 * q, 128 * q + 128)
-    add("S", "dun", lambda: [S.dma_start(T.un0[:, :], T.units[:, :])], (), ["un0"], dur=100, lat=2000, inc=16)
-    add("Y", "dst", lambda: [g.sync.dma_start(T.st[big(q), :], T.shelf[rows(q), :]) for q in others], (), ["st"], dur=300, lat=4000, n=3, inc=16)
-    add("S", "dsu", lambda: [S.dma_start(T.su[big(q), :], T.units[rows(q), :]) for q in others], (), ["su"], dur=300, lat=2000, n=3, inc=16)
-    add("Y", "dsh", lambda: [g.sync.dma_start(T.sh0[:, :], T.shelf[:, :])], (), ["sh0"], dur=100, lat=7000, inc=16)
-    add("Y", "bs%d" % r, lambda: [g.sync.dma_start(T.shs[rows(r), :], T.shelf[rows(r), :])], (), ["shs%d" % r], dur=100, lat=8000, inc=16)
 
-    def split(p):
-        oth = [q for q in range(4) if q != p]
-        away = [q for q in oth if (topo.host(cores[q]), topo.chip(cores[q])) != (topo.host(cores[p]), topo.chip(cores[p]))]
-        offe = topo.engines(cores[p], cores[away[0]])
-        w = len(offe) // len(away)
-        res = {q: offe[k * w:k * w + w] for k, q in enumerate(away)}
-        for q in oth:
-            if q not in away:
-                res[q] = [e for e in topo.engines(cores[p], cores[q]) if e not in offe]
-        return res, away
-    eng_of, off = split(r)
-    near = [q for q in others if q not in off]
+    def low(k, b):
+        return ((b ^ r) & MS[k]) == 0
 
-    def send(reads, src_of, dst, sem):
+    def far(p, q):
+        return (topo.host(cores[p]), topo.chip(cores[p])) != (topo.host(cores[q]), topo.chip(cores[q]))
+    off = [b for b in (1, 2, 3) if far(r, b ^ r)]
+    near = [b for b in (1, 2, 3) if b not in off]
+    offe = topo.engines(core, cores[off[0] ^ r])
+    neare = [e for e in topo.engines(core, cores[near[0] ^ r]) if e not in offe]
+    share = len(offe) // len(off)
+    eng_of = {b: offe[share * j:share * j + share] for j, b in enumerate(off)}
+    eng_of[near[0]] = neare
+
+    def send(reads, blocks, engines, src_of, dst_of, sem, key, lat):
         def fn():
             tr = []
-            for q in others:
-                rid, pid = topo.addr(cores[q], core)
-                tr.append(RemoteDMATransfer(dst_ids=[DstId(rid=rid, pnc=pid)], dma_engine_mask=sum(1 << e for e in eng_of[q]),
-                                            remote_sem=T.sem[sem], src=src_of(q), dst=dst))
+            for b in blocks:
+                rid, pid = topo.addr(cores[b ^ r], core)
+                tr.append(RemoteDMATransfer(dst_ids=[DstId(rid=rid, pnc=pid)], dma_engine_mask=sum(1 << e for e in engines[b]),
+                                            remote_sem=T.sem[sem], src=src_of(b), dst=dst_of(b)))
             g.remote_dma_fused(tr, local_sem=T.sem["loc"])
             return []
-        return add("G", "loc", fn, reads, (), dur=1500, n=sum(len(eng_of[q]) for q in others))
+        n = sum(len(engines[b]) for b in blocks)
+        i = add("G", "loc", fn, reads, (), dur=800, lat=1000, n=n)
+        return add("R", sem, None, (), [key], dur=0.0, lat=lat, n=n, extra=[i])
 
-    def arrive(sem, qs, key, like, lat):
-        add("R", sem, None, (), [key], dur=0.0, lat=lat, n=sum(len(split(q)[0][r]) for q in qs), extra=[like])
+    span = 128 if r == 0 else 32 * (r & -r)
+    runs = [(slice(p, p + span), slice(p ^ (32 * r), (p ^ (32 * r)) + span)) for p in range(0, 128, span)]
+    add("S", "dun", lambda: [S.dma_start(T.un0[a, :], T.units[b, :]) for a, b in runs], (), ["un0"], dur=100 * len(runs), lat=2000, n=len(runs), inc=16)
 
-    prev = {}
+    def stage(j, b, reads):
+        add("Y", "dst%d" % j, lambda: [Y.dma_start(T.st[big(b), :], T.shelf[rows(b ^ r), :])], reads, ["st%d" % b], dur=100, lat=2500, inc=16)
+    stage(0, off[0], [])
+    i = add("Y", "dsh", lambda: [Y.dma_start(T.sh0[a, :], T.shelf[b, :]) for a, b in runs], (), ["sh0"], dur=100 * len(runs), lat=7000, n=len(runs), inc=16)
+    tasks[i]["soft"].add(i - 1)
+    stage(1, off[1], ["st%d" % off[0]])
+    stage(2, near[0], ["sh0"])
 
-    def const(eng, sem, fn, reads, key, dur):
-        prev[sem] = add(eng, sem, lambda: [fn()], reads, [key], dur=dur, extra=[prev[sem]] if sem in prev else [])
+    def const(eng, fn, reads, key, dur):
+        m = {"V": 4, "S": 2, "G": 1}[eng]
+        turn[eng] = turn.get(eng, 0) + 1
+        add(eng, "gk" if eng == "G" else "%sk%d" % (eng.lower(), turn[eng] % m), lambda: [fn()], reads, [key], dur=dur)
 
-    def iota(key, out, pattern, cm, n, **kw):
-        const("G", "gk", lambda: g.iota(out, pattern, 0, cm, **kw), [], key, 130 + 1.66 * n)
+    def iota(key, out, pattern, base, cm, n, flag=True):
+        kw = dict(allow_small_or_imprecise_dtypes=True) if flag else {}
+        const("G", lambda: g.iota(out, pattern, base, cm, **kw), [], key, 130 + 1.66 * n)
 
     def ts(key, out, in0, rk, s1, op0, s2=None, op1=None, n=128):
         a = (out, in0, s1, None, op0) if op1 is None else (out, in0, s1, s2, op0, op1)
-        const("V", "vk", lambda: V.tensor_scalar(*a), rk.split(), key, vd(n))
+        const("V", lambda: V.tensor_scalar(*a), rk.split(), key, vd(n))
 
     def tc(name, in0, rk, *a):
         ts(name, cf[name] if name in cf else ci[name], (cf[in0] if in0 in cf else ci[in0]), in0 + " " + rk, *a, n=1)
 
-    def tt(key, out, a, b, rk, op):
-        const("V", "vk", lambda: V.tensor_tensor(out, a, b, op), rk.split(), key, vd(256))
+    def tt(key, out, a, b, rk, op, n=256):
+        const("V", lambda: V.tensor_tensor(out, a, b, op), rk.split(), key, vd(n))
 
     def ms(key, ap, v, n):
-        const("V", "vk", lambda: V.memset(ap, v), [], key, vd(n, 0.5))
+        const("V", lambda: V.memset(ap, v), [], key, vd(n, 0.5))
 
-    def diag(name, out, v, rk=""):
-        ts(name, out, kf["mrow"], "mrow pcf " + rk, cf["pcf"], OP.is_equal, v, OP.mult)
-    small = dict(allow_small_or_imprecise_dtypes=True)
-    iota("pc", ci["pc"], [[0, 1]], 1, 1)
-    iota("mrow", kf["mrow"], [[1, 128]], 0, 128, **small)
-    iota("sm", kf["sm"], [[1, 8], [0, 16]], 0, 128, **small)
-    iota("im", kf["im"], [[0, 8], [1, 16]], 0, 128, **small)
+    def sc(key, out, in0, rk, scale):
+        const("S", lambda: S.activation(out, in0, AF.Identity, scale=scale), rk.split(), key, sd(128))
+
+    def diag(name, out, v):
+        ts(name, out, kf["mrow"], "mrow pcf", cf["pcf"], OP.is_equal, v, OP.mult)
+    iota("pc", ci["pc"], [[0, 1]], 0, 1, 1, False)
+    iota("mrow", kf["mrow"], [[1, 128]], 0, 0, 128)
+    iota("sm", kf["sm"], [[1, 8], [0, 16]], 0, 0, 128)
+    iota("im", kf["im"], [[0, 8], [1, 16]], 0, 0, 128)
     ms("cl", T.cl[:, :], -512.0, 128)
-    ms("cr", T.cr[:, 0:64], 0.0, 64)
-    ms("cr", T.cr[:, 64:128], 256.0, 64)
+    for j, v in enumerate((256.0, 512.0, -4.0, 2.0 ** -10)):
+        ms("cr%d" % j, T.cr[:, 64 * j:64 * j + 64], v, 64)
     tc("pcf", "pc", "", 1.0, OP.mult)
     tc("psi", "pc", "", 4, OP.arith_shift_right)
     tc("ii", "pc", "", 15, OP.bitwise_and)
     tc("odd", "pc", "", 1, OP.bitwise_and)
     tc("ps", "psi", "", 1.0, OP.mult)
     tc("pi", "ii", "", 1.0, OP.mult)
-    tc("b1", "odd", "", -2048.0, OP.mult, BIG + 2048.0 - 2047.5, OP.add)
-    tc("b2", "odd", "", -2048.0, OP.mult, BIG + 2048.0, OP.add)
+    ts("b0", T.b4[:, 0:1], ci["odd"], "odd", -2048.0, OP.mult, BIG + 0.5, OP.add, n=1)
+    ts("b1", T.b4[:, 1:2], ci["odd"], "odd", -2048.0, OP.mult, BIG + 2048.0, OP.add, n=1)
     ts("same", kf["same"], kf["sm"], "sm ps", cf["ps"], OP.is_equal)
     ts("le", kf["le"], kf["im"], "im pi", cf["pi"], OP.is_ge)
     tt("tri", kh["tri"], kf["same"], kf["le"], "same le", OP.mult)
@@ -177,316 +194,372 @@ def rank_program(g, core, T, topo):
     add("V", "xo", lambda: [V.tensor_scalar(T.xo[:, :], T.un0[:, :], -2048.0, None, OP.add)], ["un0"], xok, dur=vd(256))
     diag("ineg", kb["ineg"], -1.0)
     diag("i64h", kh["i64h"], 64.0)
-    ms("mmx", T.mmx[:, :], 0.0, 1024)
-    ms("mmx", T.mmx[:, 0:1024:32], -512.0, 32)
-    ms("mmn", T.mmn[:, :], 0.0, 1024)
-    ms("mmn", T.mmn[:, 0:1024:32], 512.0, 32)
+    for name, buf, v in (("mmx", T.mmx, -512.0), ("mmn", T.mmn, 512.0)):
+        ms(name, buf[:, :], 0.0, 1024)
+        ms(name, buf[:, 0:1024:32], v, 32)
 
-    s_u = send(["su"], lambda q: T.su[big(q), :], T.lu[big(r), :], "au")
-    s_s = send(["st"], lambda q: T.st[big(q), :], T.lsh[big(r), :], "ash%d" % r)
-    iota("row8", T.row8[:, :], [[1, 8]], 0, 8, **small)
-    iota("negv", T.negv[0:1, :], [[0, 4], [-1, 128]], 0, 512, **small)
-    arrive("au", others, "lu", s_u, 3500.0)
-    add("Y", "dut", lambda: [g.sync.dma_start(T.uns[rows(q), :], T.units[rows(r), :] if q == r else T.lu[big(q), :]) for q in range(4)],
-        ["lu"], ["uns"], dur=400, lat=2000, n=4, inc=16)
+    send(xok, (1, 2, 3), eng_of, lambda b: T.xo[:, :], lambda b: T.lx[:, 256 * b:256 * b + 256], "ax", "lx", 3000.0)
+    for j, b in enumerate(off + near):
+        send(["st%d" % b], (b,), {b: offe if b in off else neare}, lambda b: T.st[big(b), :], lambda b: T.lsh[big(b), :], "ash%d" % j, "lsh%d" % b, 5000.0)
+    slots = ["sh0", "sh1", "sh2", "sh3"]
 
-    def bounce(q):
-        arrive("ash%d" % q, [q], "lsh%d" % q, s_s, 6000.0 if q in near else 10000.0)
-        add("Y", "bs%d" % q, lambda: [g.sync.dma_start(T.shs[rows(q), :], T.lsh[big(q), :])], ["lsh%d" % q], ["shs%d" % q], dur=100, lat=3000, inc=16)
-    for q in near + off:
-        bounce(q)
-    slots = ["shs%d" % q for q in range(4)]
+    def sums(c, bank_, at, xb, start, stop):
+        o = 64 * c
+        return [P.matmul(bank_[:, at:at + 64], kh["tri"], xb[:, o:o + 64], start, False),
+                P.matmul(bank_[:, at + 1:at + 64:2], kh["onesb"], xb[:, o:o + 64:2], False, stop)]
 
-    def measure(c, xb, xkey, shelf, skeys, b1, b2, us):
-        a, bk, b, o, v = T["pa%d" % c], ["pa%d" % c], T["pb%d" % c], 64 * c, 1024 * c
-        X, X0, X1, XY = a[:, 0:128], a[:, 0:64], a[:, 64:128], b[:, 384:448]
-        C = str(c)
-        w, wo = slice(o, o + 64), slice(o, o + 64, 2)
-        add("P", "pw" + C, lambda: [P.matmul(XY, kh["tri"], xb[:, w], True, False), P.matmul(b[:, 385:448:2], kh["onesb"], xb[:, wo], False, True)],
-            [xkey, "tri", "onesb"], (), ["pb" + C], dur=pe(2), n=2)
-        add("V", "y" + C, lambda: [V.tensor_scalar(T.y[:, w], XY, cf[b1], None, OP.add)], [b1], ["y" + C], ["pb" + C], dur=vd(64))
-        add("P", "px" + C, lambda: [P.matmul(X, T.cl[0:1, :], T.cr[0:1, :], True, False), P.matmul(X1, kh["i64h"], xb[:, w], False, False),
-                                    P.matmul(X0, kh["tri"], xb[:, w], False, False), P.matmul(a[:, 1:64:2], kh["onesb"], xb[:, wo], False, False)],
-            [xkey, "tri", "onesb", "cl", "cr", "i64h"], (), bk, dur=pe(5), n=4)
+    def measure(c, kind, shelf, skeys, bb, bkeys, us, cut):
+        a, b, C, o, v = T["pa%d" % c], T["pb%d" % c], str(c), 64 * c, 1024 * c
+        ak, bk, w, j = ["pa" + C], ["pb" + C], slice(o, o + 64), 2 if kind == "mask" else 0
+        XY, X1, X0 = a[:, 64:128], a[:, 128:192], b[:, 128:192]
+        shift = lambda: P.matmul(X1, T.cl[0:1, :], T.cr[0:1, 0:64], True, False)
+        if kind == "mask":
+            keys, n = ["mi" + C, "wh" + C], (2, 4, 2)
+            fy = lambda: sums(c, a, 64, T.mi, False, True)
+            f0 = lambda: sums(c, b, 128, T.wh, True, False) + sums(c, b, 128, T.mi, False, False)
+            f1 = lambda: [P.matmul(X1, kh["i64h"], T.wh[:, w], True, False), P.matmul(X1, kh["i64h"], T.mi[:, w], False, True)]
+        elif kind == "own":
+            keys, n = ["xo" + C, "tri", "onesb"], (2, 2, 2)
+            fy = lambda: sums(c, a, 64, T.xo, True, True)
+            f0 = lambda: sums(c, b, 128, T.xo, True, False)
+            f1 = lambda: [shift(), P.matmul(X1, kh["i64h"], T.xo[:, w], False, True)]
+        else:
+            K, lo, up = str(kind), T.wh[:, o:o + 64:2], T.wh[:, o + 1:o + 64:2]
+            keys, n = ["wh" + C, "tp" + K, "op" + K, "pm" + K], (3, 3, 3)
+
+            def mixed(bank_, at, stop):
+                return [P.matmul(bank_[:, at:at + 64], kh["tri"], T.wh[:, w], True, False), P.matmul(bank_[:, at:at + 64:2], kh["tp" + K], lo, False, False),
+                        P.matmul(bank_[:, at + 1:at + 64:2], kh["op" + K], lo, False, stop)]
+            fy = lambda: mixed(a, 64, True)
+            f0 = lambda: mixed(b, 128, False)
+            f1 = lambda: [shift(), P.matmul(a[:, 128:192:2], kh["pm" + K], lo, False, False), P.matmul(a[:, 129:192:2], kh["i64h"], up, False, True)]
+        add("P", "px" + C, fy, keys, (), ak, dur=pe(n[0]), n=n[0])
+        add("P", "pv" + C, f0, keys, (), bk, dur=pe(n[1]), n=n[1])
+        if CFG["YE"] == "V":
+            add("V", "y" + C, lambda: [V.tensor_scalar(T.y[:, w], XY, bb[:, j:j + 1], None, OP.add)], bkeys, ["y" + C], ak, dur=vd(64))
+        else:
+            add("S", "y" + C, lambda: [S.activation(T.y[:, w], XY, AF.Identity, bias=bb[:, j:j + 1])], bkeys, ["y" + C], ak, dur=sd(64))
         add("P", "py" + C, lambda: [P.matmul(X0, kb["ineg"], T.y[:, w], False, True)], ["y" + C, "ineg"], (), bk, dur=pe(1))
-        add("S", "sq" + C, lambda: [S.activation(T.sq[:, w], X0, AF.Square, bias=cf[b2])], [b2], ["sq" + C], bk, dur=sd(64))
-        add("V", "t" + C, lambda: [V.tensor_tensor(T.t3[:, w], T.sq[:, w], X1, OP.add)], ["sq" + C], ["t3" + C], bk, dur=vd(64))
+        add("P", "pz" + C, f1, keys + ["cl", "cr0", "i64h"], (), ak, dur=pe(n[2]), n=n[2])
+        add("S", "sq" + C, lambda: [S.activation(T.sq[:, w], X0, AF.Square, bias=bb[:, j + 1:j + 2])], bkeys, ["sq" + C], bk, dur=sd(64))
+        add("V", "t" + C, lambda: [V.tensor_tensor(T.t3[:, w], T.sq[:, w], X1, OP.add)], ["sq" + C], ["t3" + C], ak, dur=vd(64))
         add("V", "sf" + C, lambda: [V.tensor_scalar(T.sf[:, w], T.t3[:, w], 6, 4095, OP.arith_shift_right, OP.bitwise_and)], ["t3" + C], ["sf" + C],
             dur=vd(64))
         add("V", "of" + C, lambda: [V.tensor_copy(T.of[:, w], T.sf[:, w])], ["sf" + C], ["of" + C], dur=vd(64))
-        m = v + 32 * us
-        add("S", "ga" + C, lambda: [S.activation(T.ga[:, v:m], shelf[:, :].indirect(T.of[:, o:o + 2 * us]), AF.Copy)],
-            ["of" + C] + skeys, ["gas" + C], dur=sd(32 * us, GR))
-        gk = ["gas" + C]
-        if us < CU:
-            gk.append("gav" + C)
-            add("V", "gv" + C, lambda: [V.tensor_copy(T.ga[:, m:v + 1024], shelf[:, :].indirect(T.of[:, o + 2 * us:o + 64]))],
-                ["of" + C] + skeys, ["gav" + C], dur=50 + vd(32 * (CU - us), GR))
-        z = slice(v, v + 1024)
-        gr = ["gas" + C, "gav" + C]
-        add("V", "mx" + C, lambda: [V.tensor_tensor_scan(T.mx[:, z], T.mmx[:, :], T.ga[:, z], 0.0, OP.add, OP.max)], gr + ["mmx"], ["mx" + C],
-            dur=vd(1024, 0.5))
-        add("V", "mn" + C, lambda: [V.tensor_tensor_scan(T.mn[:, z], T.mmn[:, :], T.ga[:, z], 0.0, OP.add, OP.min)], gr + ["mmn"], ["mn" + C],
-            dur=vd(1024, 0.5))
+
+        def gather(eng, sem, a, z):
+            out, src = T.ga[:, v + 32 * a:v + 32 * z], shelf[:, :].indirect(T.of[:, o + 2 * a:o + 2 * z])
+            add(eng, sem + C, lambda: [S.activation(out, src, AF.Copy) if eng == "S" else V.tensor_copy(out, src)], ["of" + C] + skeys, [sem + C],
+                dur=(65 if eng == "S" else 50) + 32 * (z - a) * GR * 0.83)
+
+        def scans(tag, a, z, keys):
+            s = slice(v + 32 * a, v + 32 * z)
+            for nm, buf, mask, op in (("mx", T.mx, T.mmx, OP.max), ("mn", T.mn, T.mmn, OP.min)):
+                add("V", nm + tag + C, (lambda buf, mask, op: lambda: [V.tensor_tensor_scan(buf[:, s], mask[:, 0:32 * (z - a)], T.ga[:, s], 0.0, OP.add, op)])(buf, mask, op),
+                    keys + ["m" + nm], [nm + tag + C], dur=vd(32 * (z - a), 0.5))
+        gv = ["gv" + C] if us < CU else []
+        vu = CU - us
+        if vu:
+            gather("V", "gv", 0, vu)
+        if cut:
+            gather("S", "ga", vu, cut)
+            gather("S", "gb", cut, CU)
+            scans("", 0, cut, gv + ["ga" + C])
+            scans("_", cut, CU, ["gb" + C])
+            return ["mx" + C, "mx_" + C], ["mn" + C, "mn_" + C]
+        gather("S", "ga", vu, CU)
+        scans("", 0, CU, gv + ["ga" + C])
+        return ["mx" + C], ["mn" + C]
 
     def ext(buf, c):
         return buf[:, 1024 * c + 31:1024 * c + 1024:32]
 
-    def measure_all(shelf, skeys, b1, b2):
-        for c in range(NC):
-            measure(c, T.xo, "xo%d" % c, shelf, skeys, b1, b2, USM)
-            add("V", "dd%d" % c, (lambda c: lambda: [V.tensor_tensor(T.dd[:, 32 * c:32 * c + 32], ext(T.mx, c), ext(T.mn, c), OP.subtract)])(c),
-                ["mx%d" % c, "mn%d" % c], ["dd%d" % c], dur=vd(64))
-    measure_all(T.sh0, ["sh0"], "b1", "b2")
+    def spread(c, keys, out, key):
+        add("V", "dd%d" % c, lambda: [V.tensor_tensor(out[:, 32 * c:32 * c + 32], ext(T.mx, c), ext(T.mn, c), OP.subtract)],
+            keys[0] + keys[1], [key + str(c)], dur=vd(64))
+    for c in range(NC):
+        now[0] = c
+        spread(c, measure(c, "own", T.sh0, ["sh0"], T.b4, ["b0", "b1"], CFG["USM"], CFG["CUTM"]), T.dd, "dd")
 
+    iota("row8", T.row8[:, :], [[1, 8]], 0, 0, 8)
+    iota("neg", T.num[0:1, 0:256], [[0, 2], [-1, 128]], 0, 0, 256)
+    iota("pos", T.num[0:1, 256:512], [[0, 2], [1, 128]], 0, 0, 256)
+    sgn = [-1 if low(k, 0) else 1 for k in (0, 1)]
+    iota("sg80", T.sg8[0:1, 0:8], [[-2 * sgn[0], 2], [0, 4]], sgn[0], 0, 8)
     ms("ones", kb["ones"], 1.0, 128)
+    ms("one0", T.one0[:, :], 1.0, 65)
+    ms("one0", T.one0[:, 64:65], 0.0, 1)
     ts("ind", T.ind[:, :], T.row8[:, :], "row8 ps", cf["ps"], OP.is_equal, 128.0, OP.mult, n=8)
-    ts("r1", T.r1[:, 0:2], T.ind[:, 2 * r:2 * r + 2], "ind", 1.0, OP.mult, n=2)
-    ts("r1", T.r1[:, 2:4], T.ind[:, 2 * r:2 * r + 2], "ind", -1.0, OP.mult, n=2)
-    for b in (0, 1):
-        ts("lp%d" % b, kb["lp%d" % b], kf["mrow"], "mrow ind", 0.0, OP.mult, T.ind[:, 2 * r + b:2 * r + b + 1], OP.add)
-        ts("ln%d" % b, kb["ln%d" % b], kb["lp%d" % b], "lp%d" % b, -1.0, OP.mult)
-    tc("va", "ps", "", float(2 * r), OP.is_ge)
-    tc("vb", "ps", "", float(2 * r + 1), OP.is_le)
-    tc("vv", "va", "vb", cf["vb"], OP.mult)
-    tc("vt", "ps", "", float(100 - 2 * r), OP.add)
-    tc("colr", "vt", "vv", cf["vv"], OP.mult, -100.0, OP.add)
-    for q in range(4):
-        ts("ql%d" % q, kb["ql%d" % q], kf["sm"], "sm colr", float(2 * q), OP.subtract, cf["colr"], OP.is_equal)
+    ts("r2", T.r2[:, :], T.row8[:, :], "row8 ps", cf["ps"], OP.is_equal, 128.0, OP.mult, n=8)
+    for s in range(8):
+        sc("lk%d" % s, kb["lk%d" % s], kb["ones"], "ones ind", T.ind[:, s:s + 1])
+    sc("sameb", kb["sameb"], kf["same"], "same", 1.0)
     tc("fc", "ps", "", float(SFROM), OP.is_ge)
-    tc("scl2", "fc", "", -1.0, OP.mult, 2.0, OP.add)
     tc("ad0", "fc", "", 127.0, OP.mult)
     tc("ad1", "fc", "", 127.0, OP.mult, 1.0, OP.add)
-    tc("scl1", "fc", "", -0.5, OP.mult, 1.0, OP.add)
     tc("ad2", "fc", "", 63.5, OP.mult)
     ms("win", T.win[:, 0:256], 0.0, 512)
     ms("winq", T.win[:, 256:384], 0.0, 256)
-    for k, sh in ((0, 6), (1, 5)):
-        tc("bit%d" % k, "pc", "", sh, OP.arith_shift_right, 1, OP.bitwise_and)
-        tc("lam%d" % k, "bit%d" % k, "", -2.0, OP.mult, 1.0, OP.add)
     diag("idf", kf["idf"], 1.0)
     diag("idd", kh["idd"], 1.0)
+    tc("k5i", "pc", "", 5, OP.arith_shift_right)
+    tc("k5", "k5i", "", 1.0, OP.mult)
+    tc("u5i", "pc", "", 31, OP.bitwise_and)
+    tc("u5", "u5i", "", 1.0, OP.mult)
+    iota("urow", T.urow[:, :], [[1, 32], [0, 2]], 0, 0, 64)
+    for t in range(2, 6):
+        h = HS[t - 1]
+        iota("br%d" % t, kb["br%d" % t], [[0, 64 // h], [2, 2]] + ([[0, h]] if h > 1 else []), -1, 0, 128)
+    ts("del", T["del"][:, :], T.urow[:, :], "urow u5", cf["u5"], OP.is_equal, n=64)
+    ms("pat", T.pat[:, :], -1.0, 132)
+    ts("pat", T.pat[:, 0:64], T["del"][:, :], "del", -1.0, OP.mult, n=32)
+    ts("pat", T.pat[:, 66:130:2], T["del"][:, 0:64:2], "del", 1.0, OP.mult, n=32)
+    ts("pat", T.pat[:, 67:130:2], T["del"][:, 1:64:2], "del", -1.0, OP.mult, n=32)
+    ms("b2", T.b4[:, 2:3], BIG + SHIFT - 2047.5, 1)
+    ms("b3", T.b4[:, 3:4], BIG + SHIFT, 1)
+    for j in range(4):
+        ts("bi%d" % j, T.bi[:, j:j + 1], ci["pc"], "pc", 3 - j, OP.arith_shift_right, 1, OP.bitwise_and, n=1)
+    bik = " ".join("bi%d" % j for j in range(4))
+    ms("nf", T.nf[:, :], 2048.0, 5)
+    ts("nf", T.nf[:, 1:5], T.bi[:, :], bik, 4096.0, OP.mult, -4096.0, OP.add, n=4)
+    ms("one5", T.one5[:, :], 1.0, 5)
+    const("V", lambda: V.tensor_tensor_scan(T.cum[:, :], T.one5[:, :], T.nf[:, :], 0.0, OP.mult, OP.add), ["nf", "one5"], "cum", vd(5))
+    ts("bf", T.bf[:, :], T.bi[:, :], bik, -4096.0, OP.mult, n=4)
+    tt("dc", T.dc[:, 0:4], T.cum[:, 0:4], T.bf[:, :], "cum bf", OP.add, n=8)
+    for t in range(1, 5):
+        sc("dg%d" % t, kb["dg%d" % t], kf["idf"], "idf dc", T.dc[:, t - 1:t])
 
     def round_consts(k):
-        K = str(k)
-        tc("px" + K, "lam" + K, "pcf", (64.0, 32.0)[k], OP.mult, cf["pcf"], OP.add)
-        ts("pm" + K, kh["pm" + K], kf["mrow"], "mrow px" + K, cf["px" + K], OP.is_equal)
-        ts("pmt", kf["pmt"], kf["mrow"], "mrow px" + K, cf["px" + K], OP.is_equal)
-        tt("dm" + K, kh["dm" + K], kf["pmt"], kf["idf"], "idf pmt", OP.subtract)
-        tc("nl" + K, "lam" + K, "", -1.0, OP.mult)
-        tc("th" + K, "lam" + K, "", 0.5, OP.mult)
-        tc("psx" + K, "lam" + K, "ps", (4.0, 2.0)[k], OP.mult, cf["ps"], OP.add)
-        ts("e1", kf["e1"], kf["sm"], "sm ps lam" + K, cf["ps"], OP.is_equal, cf["lam" + K], OP.mult)
-        ts("e2", kf["e2"], kf["sm"], "sm psx%s lam%s" % (K, K), cf["psx" + K], OP.is_equal, cf["lam" + K], OP.mult)
-        tt("sdp" + K, kb["sdp" + K], kf["e1"], kf["e2"], "e1 e2", OP.add)
-        ts("sdn" + K, kb["sdn" + K], kb["sdp" + K], "sdp" + K, -1.0, OP.mult)
+        K, m = str(k), MS[k]
+        tc("bit" + K, "pc", "", (6, 5)[k], OP.arith_shift_right, 1, OP.bitwise_and)
+        tc("mu" + K, "bit" + K, "", -2.0, OP.mult, 1.0, OP.add)
+        tc("lam" + K, "mu" + K, "", float(-sgn[k]), OP.mult)
+        tc("px" + K, "mu" + K, "pcf", 32.0 * m, OP.mult, cf["pcf"], OP.add)
+        tc("psx" + K, "mu" + K, "ps", 2.0 * m, OP.mult, cf["ps"], OP.add)
+        tc("s2_" + K, "lam" + K, "fc", -2.0, OP.add, cf["fc"], OP.mult)
+        tc("s1_" + K, "s2_" + K, "", 2.0, OP.add, 0.5, OP.mult)
+        tc("s2_" + K, "s2_" + K, "", 2.0, OP.add)
+        ts("pm" + K, kh["pm" + K], kf["mrow"], "mrow px" + K, cf["px" + K], OP.is_equal, 64.0, OP.mult)
+        ts("op" + K, kh["op" + K], kf["sm"], "sm psx" + K, cf["psx" + K], OP.is_equal)
+        tt("tmp", kf["tmp"], kh["op" + K], kf["same"], "same op" + K, OP.subtract)
+        tt("tp" + K, kh["tp" + K], kf["tmp"], kf["le"], "le tmp", OP.mult)
+        ts("tmp", kf["tmp"], kf["mrow"], "mrow px" + K, cf["px" + K], OP.is_equal)
+        tt("dm" + K, kh["dm" + K], kf["tmp"], kf["idf"], "idf tmp", OP.subtract)
+        if k == 0:
+            tc("sai", "psi", "", 3, OP.bitwise_and)
+            tc("spc0", "sai", "", 1.0, OP.mult)
+            iota("spr0", kb["spr0"], [[0, 2], [1, 4], [0, 16]], 0, 0, 128)
+            iota("lr0", kb["lr0"], [[-2 * sgn[0], 2], [0, 64]], sgn[0], 0, 128)
+        else:
+            tc("sai", "psi", "", 1, OP.bitwise_and)
+            tc("sa", "sai", "", 1.0, OP.mult)
+            tc("spc1", "bit0", "sa", 2.0, OP.mult, cf["sa"], OP.add)
+            for a in (0, 1):
+                iota("spr1", part(T.kb, B16M, "spr1", 64 * a, 64 * a + 64), [[0, 2], [1, 2], [0, 16]], 2 * a, 0, 64)
+            iota("lr1", kb["lr1"], [[0, 2], [-2 * sgn[1], 2], [0, 32]], sgn[1], 0, 128)
+            iota("sg81", T.sg8[0:1, 8:16], [[0, 2], [-2 * sgn[1], 2], [0, 2]], sgn[1], 0, 8)
+        ts("wsp" + K, T.wsp[:, 8 * k:8 * k + 4], T.row8[:, 0:4], "row8 spc%s lam%s" % (K, K), cf["spc" + K], OP.is_equal, cf["lam" + K], OP.mult, n=4)
+        ts("wsn" + K, T.wsp[:, 8 * k + 4:8 * k + 8], T.wsp[:, 8 * k:8 * k + 4], "wsp" + K, -1.0, OP.mult, n=4)
+        w1 = "w%d_1" % k
+        ts(w1, kb[w1], kb["spr" + K], "k5 spr" + K, cf["k5"], OP.is_equal, -4096.0, OP.mult, n=64)
+        for t in range(2, 7):
+            row = "br%d" % t if t < 6 else "lr" + K
+            tt("w%d_%d" % (k, t), kb["w%d_%d" % (k, t)], kb[w1], kb[row], w1 + " " + row, OP.mult)
+        tc("d5_" + K, "lam" + K, "cum", -2048.0, OP.mult, T.cum[:, 4:5], OP.add)
+        tc("d5_" + K, "d5_" + K, "", -2048.0, OP.add)
+        sc("dg%d" % (5 + k), kb["dg%d" % (5 + k)], kf["idf"], "idf d5_" + K, cf["d5_" + K])
     round_consts(0)
-    diag("m16", kb["m16"], -16.0)
-    for t in range(1, 6):
-        h = HS[t] if t < 5 else 1
-        if t < 5:
-            tc("fi%d" % h, "pc", "", 16 - h, OP.bitwise_and)
-        tc("dc%d" % t, "fi%d" % h, "", -1.0, OP.mult, 16.0 - h if t < 5 else 15.5, OP.add)
-        diag("dg%d" % t, kb["dg%d" % t], cf["dc%d" % t], "dc%d" % t)
-        diag("idh%d" % HS[t - 1], kb["idh%d" % HS[t - 1]], float(HS[t - 1]))
-    diag("i64b", kb["i64b"], 64.0)
 
     dkeys = ["dd%d" % c for c in range(NC)]
-    s_d = send(dkeys, lambda q: T.dd[:, :], T.dl[:, big(r)], "ad")
-    arrive("ad", others, "dl", s_d, 3500.0)
-    add("V", "srcu", lambda: [V.tensor_scalar(T.src[:, 128 * e:128 * e + 128], T.uns[:, e:256:2], -2048.0, None, OP.add) for e in (0, 1)],
-        ["uns"], ["srcA", "srcB"], dur=2 * vd(128), n=2)
+    send(dkeys, (1, 2, 3), eng_of, lambda b: T.dd[:, :], lambda b: T.dl[:, big(b)], "ad", "dl", 3000.0)
+    for b in near + off:
+        add("Y", "dbo", (lambda b: lambda: [Y.dma_start(T.sh0[rows(b), :], T.lsh[big(b), :])])(b), ["lsh%d" % b] + dkeys, ["sh%d" % b], dur=100, lat=3000, inc=16)
+    add("P", "pu", lambda: [P.matmul(T.pa0[rows(b), 128 * e:128 * e + 128], part(T.kh, H16M, "idd", 32 * b, 32 * b + 32),
+                                     (T.lx[:, 256 * b + e:256 * b + 256:2] if b else T.xo[:, e:256:2]), True, True) for b in range(4) for e in (0, 1)],
+        ["lx", "idd"] + xok, (), ["pa0"], dur=pe(16), n=8)
+    add("S", "su", lambda: [S.activation(T.src[:, 0:256], T.pa0[:, 0:256], AF.Copy)], (), ["srcA", "srcB"], ["pa0"], dur=sd(256))
+
+    places = [("pa0", 0, (0, 1)), ("pa1", 0, (2, 3)), ("pb1", 256, (4,)), ("pa3", 256, (5,)), ("pb2", 256, (6,)), ("pb3", 256, (7,))]
 
     def order(k):
-        pa2 = T.pa2
-        dq = [T.dd[:, :] if q == r or k else T.dl[:, big(q)] for q in range(4)]
-        dk = dkeys + ([] if k else ["dl"])
-        lks = ["lk%d" % s for s in range(8)] if k else ["lp0", "lp1", "ln0", "ln1"]
-
-        def lk(s):
-            return kb["lk%d" % s] if k else kb[("lp%d" if s < 4 else "ln%d") % (s % 2)]
+        pa2, K, po = T.pa2, str(k), 24 * k
+        dq = [T.dd[:, :] if b == 0 or k else T.dl[:, big(b)] for b in range(4)]
+        dk = ["du0", "du1"] if k else dkeys + ["dl"]
 
         def kcol():
-            o = [P.matmul(pa2[:, 0:8], T.negv[0:1, 0:128], ones8, True, False)]
+            o = [P.matmul(pa2[:, 0:8], T.num[0:1, 256:384], T.sg8[0:1, 8 * k:8 * k + 8], True, False)]
             if k:
                 return o + [P.matmul(pa2[:, 0:8], T.dd[:, :], T.r2[:, :], False, True)]
-            for q in range(4):
-                w = 0 if q < 2 else 2
-                o.append(P.matmul(pa2[:, 2 * q:2 * q + 2], dq[q], T.r1[:, w:w + 2], False, q == 3))
-            return o
-        places = [("pa0", list(range(0, 4))), ("pa1", list(range(SFROM, 8))), ("pa3", list(range(4, SFROM)))]
+            return o + [P.matmul(pa2[:, 2 * b:2 * b + 2], dq[b], T.r2[:, 2 * b:2 * b + 2], False, b == 3) for b in range(4)]
 
-        def kconst(bn, n):
-            add("P", "pk" + bn[2], lambda: [P.matmul(T[bn][:, 0:128 * n], onesrow, T.negv[0:1, 0:128 * n], True, False)], ["negv", "ones"], (), [bn],
-                dur=pe(2 * n))
+        def kconst(bn, o, ss):
+            a = 0 if low(k, ss[0] // 2) else 256
+            return P.matmul(T[bn][:, o:o + 128 * len(ss)], onesrow, T.num[0:1, a:a + 128 * len(ss)], True, False)
 
-        def krow(bn, ss):
-            add("P", "pkr" + bn[2], lambda: [P.matmul(T[bn][:, big(j)], lk(s), dq[s // 2], False, j == len(ss) - 1) for j, s in enumerate(ss)],
-                dk + lks, (), [bn], dur=pe(2 * len(ss)), n=len(ss))
+        def krow(i, bn, o, ss):
+            add("P", "pr%d" % i, lambda: [P.matmul(T[bn][:, o + 128 * j:o + 128 * j + 128], kb["lk%d" % s], dq[s // 2], False, j == len(ss) - 1)
+                                          for j, s in enumerate(ss)], dk + ["lk%d" % s for s in ss], (), [bn], dur=pe(2 * len(ss)), n=len(ss))
 
-        def compare(bn, j, s):
-            src, out = T[bn][:, big(j)], T.cc[:, :, 16 * s:16 * s + 16]
-            if bn == "pa1":
+        def compare(bn, o, s):
+            src, out = T[bn][:, o:o + 128], T.cc[:, :, 16 * s:16 * s + 16]
+            if s >= SFROM:
                 add("S", "cs", lambda: [S.activation(out, src, AF.Sign, bias=T.kc[:, s:s + 1], scale=-1.0)], ["kc"], ["cc%d" % s], [bn], dur=sd(128))
             else:
-                add("V", "cv", lambda: [V.tensor_scalar(out, src, T.kc[:, s:s + 1], None, OP.is_lt)], ["kc"], ["cc%d" % s], [bn], dur=vd(128))
-        for bn, ss in places:
-            kconst(bn, len(ss))
-        add("P", "pkc", kcol, dk + ["negv", "ones", "r2" if k else "r1"], (), ["pa2"], dur=pe(3), n=2 if k else 5)
+                add("V", "cv", lambda: [V.tensor_scalar(out, src, T.kc[:, s:s + 1], None, OP.is_lt if low(k, s // 2) else OP.is_gt)], ["kc"],
+                    ["cc%d" % s], [bn], dur=vd(128))
+        add("P", "pk", lambda: [kconst(*x) for x in places], ["neg", "pos", "ones"], (), [x[0] for x in places], dur=pe(16), n=len(places))
+        add("P", "pkc", kcol, dk + ["pos", "sg8" + K, "r2"], (), ["pa2"], dur=pe(2 if k else 5), n=2 if k else 5)
         add("V", "kc", lambda: [V.tensor_copy(T.kc[:, :], pa2[:, 0:8])], (), ["kc"], ["pa2"], dur=vd(8))
-        for bn, ss in places:
-            krow(bn, ss)
-        for bn, ss in places:
+        for i in (0, 3, 1, 4, 5, 2):
+            krow(i, *places[i])
+        for bn, o, ss in places:
             for j, s in enumerate(ss):
-                compare(bn, j, s)
-        qr = T.pb0[:, 0:128]
+                compare(bn, o + 128 * j, s)
+        qr = T.pb0[:, 256:384]
         if k:
             add("P", "pq", lambda: [P.matmul(qr, kb["sameb"], T.dd[:, :], True, True)], dk + ["sameb"], (), ["pb0"], dur=pe(2))
         else:
-            add("P", "pq", lambda: [P.matmul(qr, kb["ql%d" % q], dq[q], q == 0, q == 3) for q in range(4)], dk + ["ql%d" % q for q in range(4)], (),
-                ["pb0"], dur=pe(8), n=4)
-        sq = add("S", "sq_", lambda: [S.activation(T.src[:, 256:384], qr, AF.Identity, bias=-2048.0)], (), ["srcq"], ["pb0"], dur=sd(128))
+            add("P", "pq", lambda: [P.matmul(T.pb0[rows(b), 256:384], part(T.kb, B16M, "sameb", 32 * b, 32 * b + 32), dq[b], True, True) for b in range(4)],
+                dk + ["sameb"], (), ["pb0"], dur=pe(8), n=4)
+        add("S", "sq_", lambda: [S.activation(T.src[:, 256:384], qr, AF.Identity, bias=-2048.0)], (), ["srcq"], ["pb0"], dur=sd(128))
         if k:
-            add("S", "sq_", lambda: [S.activation(T.qo[:, :], qr, AF.Copy)], (), ["qo"], ["pb0"], dur=sd(128), extra=[sq])
+            add("S", "sq_", lambda: [S.activation(T.qo[:, 0:128], qr, AF.Copy)], (), ["qo"], ["pb0"], dur=sd(128))
         add("P", "pl", lambda: [P.matmul(pa2[:, 8 + j:9 + j], T.cc[:, j, :], ones1, True, True) for j in range(8)],
             ["cc%d" % s for s in range(8)] + ["ones"], (), ["pa2"], dur=pe(8), n=8)
 
-        def lists(sem, key, js, ab):
-            add("V", sem, lambda: [V.tensor_scalar(T.po[:, 8 * j:8 * j + 8], pa2[:, 8:16], cf[a], cf[b], OP.mult, OP.add) for j, (a, b) in zip(js, ab)],
-                [x for y in ab for x in y], [key], ["pa2"], dur=len(js) * vd(8), n=len(js))
-        lists("po", "po", (0, 1), [("scl2", "ad0"), ("scl2", "ad1")])
-        add("V", "scat", lambda: [V.tensor_copy(T.win[:, 0:256].indirect(T.po[:, 0:16]), T.src[:, 0:256])], ["po", "srcA", "srcB"], ["win"],
-            dur=50 + vd(256, 3.0))
+        def lists(sem, key, out, ab):
+            add("V", sem, lambda: [V.tensor_scalar(out(j), pa2[:, 8:16], cf[a], cf[b], OP.mult, OP.add) for j, (a, b) in enumerate(ab)],
+                [x for y in ab for x in y], [key], ["pa2"], dur=len(ab) * vd(8), n=len(ab))
+        both = [("s2_" + K, "ad0"), ("s2_" + K, "ad1")]
+        lists("po", "po" + K, lambda j: T.po[:, po + 8 * j:po + 8 * j + 8], both)
+        add("V", "scat", lambda: [V.tensor_copy(T.win[:, 0:256].indirect(T.po[:, po:po + 16]), T.src[:, 0:256])], ["po" + K, "srcA", "srcB"], ["win"],
+            dur=50 + vd(256, 3.5))
         for c in range(NC):
-            add("V", "nw%d" % c, (lambda w: lambda: [V.tensor_copy(T.wh[:, w], T.win[:, w])])(slice(64 * c, 64 * c + 64)), ["win"], ["wh%d" % c], dur=vd(64))
-        lists("poq", "poq", (2,), [("scl1", "ad2")])
-        add("V", "scq", lambda: [V.tensor_copy(T.win[:, 256:384].indirect(T.po[:, 16:24]), T.src[:, 256:384])], ["poq", "srcq"], ["winq"],
-            dur=50 + vd(128, 3.0))
-        add("V", "whq", lambda: [V.tensor_copy(T.wh[:, 256:384], T.win[:, 256:384])], ["winq"], ["whq"], dur=vd(128))
+            add("V", "mi%d" % c, (lambda w: lambda: [V.tensor_copy(T.wh[:, w], T.win[:, w])])(slice(64 * c, 64 * c + 64)), ["win"], ["wh%d" % c], dur=vd(64))
+        lists("poq", "poq" + K, lambda j: T.po[:, po + 16:po + 24], [("s1_" + K, "ad2")])
+        add("V", "scq", lambda: [V.tensor_copy(T.win[:, 256:384].indirect(T.po[:, po + 16:po + 24]), T.src[:, 256:384])], ["poq" + K, "srcq"], ["winq"],
+            dur=50 + vd(128, 3.5))
+        add("V", "scq", lambda: [V.tensor_copy(T.wh[:, 256:384], T.win[:, 256:384])], ["winq"], ["whq"], dur=vd(128))
+        if k:
+            lists("poq", "qp", lambda j: T.qo[:, 128 + 8 * j:136 + 8 * j], both)
 
-    def spap(c, t, st=1):
-        return T.sp[:, 320 * c + 64 * (t - 1):320 * c + 64 * t:st]
+    def dec(c, t, a=0, z=64):
+        o = 66 * (5 * c + t - 1)
+        return T.de[:, o + a:o + z]
 
-    def pre_g(c, t):
-        C, w, b = str(c), slice(64 * c, 64 * c + 64), T["pb%d" % c]
-        G = b[:, 64:128]
+    def half(col):
+        return P.matmul(col, T.cl[0:1, :], T.cr[0:1, 192:193], True, False)
 
-        def fn():
-            o = [P.matmul(G, kb["dg%d" % t], T.sg[:, w], True, False),
-                 P.matmul(b[:, 65:128:2], kb["m16"], T.sg[:, 64 * c + 1:64 * c + 64:2], False, False)]
-            for u in range(1, t):
-                o.append(P.matmul(G, kb["idh%d" % HS[u - 1]], spap(c, u), False, False))
-            if t == 5:
-                o.append(P.matmul(G, kb["i64b"], T.nt[:, w], False, False))
-            return o
-        n = t + 1 + (1 if t == 5 else 0)
-        add("P", "pg" + C, fn, ["sg" + C, "dg%d" % t, "m16"] + ["sp%d_%d" % (c, u) for u in range(1, t)] + ["idh%d" % HS[u - 1] for u in range(1, t)]
-            + (["i64b", "nt" + C] if t == 5 else []), (), ["pb" + C], dur=pe(n), n=n)
+    def pairs(col, c, data, w, last):
+        return [P.matmul(T["pa%d" % c][rows(s), col:col + 1], data, T.wsp[:, w + s:w + s + 1], False, last) for s in range(4)]
 
-    def first(k, c):
-        b, bk, o, W, C, K = T["pb%d" % c], ["pb%d" % c], 64 * c, T.wh, str(c), str(k)
-        add("P", "pD" + C, lambda: [P.matmul(b[:, 256:320:2], kh["pm" + K], W[:, o:o + 64:2], True, True),
-                                    P.matmul(b[:, 257:320:2], kh["idd"], W[:, o + 1:o + 64:2], True, True)],
-            ["wh" + C, "pm" + K, "idd"], (), bk, dur=pe(2), n=2)
-        add("V", "x" + C, lambda: [V.tensor_copy(T.x[:, o:o + 64], b[:, 256:320])], (), ["x" + C], bk, dur=vd(64))
+    def before(k, c):
+        a, bk, o, W, C, K = T["pa%d" % c], ["pa%d" % c], 64 * c, T.wh, str(c), str(k)
+        w = slice(o, o + 64)
+        add("P", "pw" + C, lambda: [half(a[:, 2:3])] + pairs(2, c, W[:, 256 + 32 * c:288 + 32 * c], 8 * k, True)
+            + [P.matmul(a[:, 192:256], T.cl[0:1, :], T.cr[0:1, 128:192], True, False), P.matmul(a[:, 192:256], kh["dm" + K], W[:, w], False, True),
+               P.matmul(a[:, 256:320], kh["dm" + K], W[:, w], True, True), P.matmul(a[:, 320:384], kh["idd"], W[:, w], True, True)],
+            ["wh" + C, "whq", "dm" + K, "cr2", "cr3", "wsp" + K, "idd"], (), bk, dur=pe(7.2), n=9)
+        add("V", "pt" + C, lambda: [V.tensor_scalar(T.pt[:, 132 * c:132 * c + 132], T.pat[:, :], a[:, 2:3], None, OP.mult),
+                                    V.tensor_scalar(T.tk[:, w], T["del"][:, :], a[:, 2:3], -1.0, OP.mult, OP.is_lt)],
+            ["pat", "del"], ["pt" + C, "tk" + C], bk, dur=2 * vd(66), n=2)
+        add("V", "ea" + C, lambda: [V.tensor_scalar(T.ea[:, w], a[:, 192:256], 2048.0, -4096.0, OP.is_ge, OP.mult)], (), ["ea" + C], bk, dur=vd(64))
+        add("V", "ea" + C, lambda: [V.tensor_tensor(T.ee[:, w], T.ea[:, w], a[:, 192:256], OP.add)], ["ea" + C], ["ee" + C], bk, dur=vd(64))
 
-    def rest_of(k, c):
-        b, bk, o, W, C, K = T["pb%d" % c], ["pb%d" % c], 64 * c, T.wh, str(c), str(k)
-        dm, idd, dqp, w, qw = kh["dm" + K], kh["idd"], b[:, 320:384], slice(64 * c, 64 * c + 64), slice(256 + 32 * c, 288 + 32 * c)
-        add("P", "pD" + C, lambda: [P.matmul(b[:, 128:192], dm, W[:, w], True, True), P.matmul(b[:, 192:256], idd, W[:, w], True, True),
-                                    P.matmul(b[:, 320:384:2], dm, W[:, qw], True, True), P.matmul(b[:, 321:384:2], dm, W[:, qw], True, True)],
-            ["wh" + C, "whq", "dm" + K, "idd"], (), bk, dur=pe(4), n=4)
-        add("S", "sg" + C, lambda: [S.activation(T.sg[:, w], dqp, AF.Sign, bias=-0.5, scale=cf["nl" + K])], ["nl" + K], ["sg" + C], bk, dur=sd(64))
-        add("V", "nt" + C, lambda: [V.tensor_scalar(T.nt[:, w], dqp, cf["th" + K], None, OP.is_le)], ["th" + K], ["nt" + C], bk, dur=vd(64))
+    acol = T["pb%d" % (NC - 1)][:, 64:65]
 
-    def trial(k, c, t, b1, b2):
-        b, bk, a, o, C, K = T["pb%d" % c], ["pb%d" % c], T["pa%d" % c], 64 * c, str(c), str(k)
-        w, w3, sp, h = slice(o, o + 64), slice(32 * c, 32 * c + 32), "sp%d_%d" % (c, t), "idh%d" % HS[t - 1]
-        measure(c, T.x, "x" + C, T.shs, slots, b1, b2, US)
+    def total(c, ts_, last):
+        add("P", "pA", lambda: [P.matmul(acol, kb["ah%d" % t], dec(c, t, 64, 65), False, last) for t in ts_],
+            ["de%d_%d" % (c, t) for t in ts_] + ["ah%d" % t for t in ts_], (), ["pb%d" % (NC - 1)], dur=pe(len(ts_)), n=len(ts_))
+
+    def trial(k, c, t, bb, bkeys):
+        a, b, o, C, K = T["pa%d" % c], T["pb%d" % c], 64 * c, str(c), str(k)
+        ak, bk, w, G = ["pa" + C], ["pb" + C], slice(o, o + 64), b[:, 0:64]
+        now[0] = CFG["N"][1 + 2 * k] + NC * (t - 1) + c
+        kx, kn = measure(c, "mask" if t > 1 else k, T.sh0, slots, bb, bkeys, CFG["US"], CFG["CUT"])
         if t == 1:
-            rest_of(k, c)
-        pre_g(c, t)
-        add("P", "pd" + C, lambda: [P.matmul(a[:, 128 + e:192:2], kb[n + K], ext(m, c), n == "sdp", n == "sdn")
-                                    for e in (0, 1) for n, m in (("sdp", T.mx), ("sdn", T.mn))],
-            ["mx" + C, "mn" + C, "sdp" + K, "sdn" + K], (), ["pa" + C], dur=pe(4), n=4)
-        add("V", "sp" + C, lambda: [V.tensor_scalar(spap(c, t), a[:, 128:192], 0.0, -0.5, OP.is_gt, OP.add)], (), [sp], ["pa" + C], dur=vd(64))
-        add("P", "pc" + C, lambda: [P.matmul(b[:, 64:128], kb[h], spap(c, t), False, True)], [sp, h], (), bk, dur=pe(1))
-        add("V", "mk" + C, lambda: [V.tensor_scalar(T.mk[:, w], b[:, 64:128], 0.0, None, OP.is_equal)], (), ["mk" + C], bk, dur=vd(64))
-        add("V", "md" + C, lambda: [V.tensor_tensor(T.md[:, w], T.mk[:, w], b[:, 128:192], OP.mult)], ["mk" + C], ["md" + C], bk, dur=vd(64))
-        nm, dst = ("x", T.x) if t < 5 else ("nw", T.nw)
-        add("V", nm + C, lambda: [V.tensor_tensor(dst[:, w], T.md[:, w], b[:, 192:256], OP.add)], ["md" + C],
-            [("x" if t < 5 else "new") + C], bk, dur=vd(64))
-        if t == 5 and k == 0:
-            add("P", "pD" + C, lambda: [P.matmul(b[:, 448:480], kb["idh%d" % HS[u - 1]], spap(c, u, 2), u == 1, u == 5) for u in range(1, 6)],
-                ["sp%d_%d" % (c, u) for u in range(1, 6)], (), bk, dur=pe(5), n=5)
-            add("V", "pf" + C, lambda: [V.tensor_tensor(T.pf[:, w3], T.sg[:, o:o + 64:2], b[:, 448:480], OP.mult)], ["sg" + C], ["pf" + C], bk, dur=vd(32))
+            before(k, c)
+        add("P", "pw" + C, lambda: [half(a[:, 0:1])], ["cr3"], (), ak, dur=pe(1))
+        dg = "dg%d" % (t + k if t == 5 else t)
+        known = [("w%d_%d" % (k, u), dec(c, u), "de%d_%d" % (c, u)) for u in range(1, t)] + ([("w%d_6" % k, T.tk[:, w], "tk" + C)] if t == 5 else [])
+        add("P", "pg" + C, lambda: [P.matmul(b[:, 0:65], kb[dg], T.one0[:, :], True, False)] + [P.matmul(G, kb[m], d, False, False) for m, d, _ in known],
+            [dg, "one0"] + [x[0] for x in known] + [x[2] for x in known], (), bk, dur=pe(1 + len(known)), n=1 + len(known))
+        counts = k == 0 and t == 5 and c == NC - 1
+        if counts:
+            for d in range(NC):
+                total(d, range(1, 6 if d < c else 5), False)
+        add("P", "pd" + C, lambda: pairs(0, c, ext(T.mx, c), 8 * k, False), kx + ["wsp" + K], (), ak, dur=pe(2.2), n=4)
+        add("P", "pe" + C, lambda: pairs(0, c, ext(T.mn, c), 8 * k + 4, True), kn + ["wsn" + K], (), ak, dur=pe(2.2), n=4)
+        p = 132 * c + (66 if t == 1 else 0)
+        add("V", "de" + C, lambda: [V.tensor_scalar(dec(c, t, 0, 65), T.pt[:, p:p + 65], a[:, 0:1], 0.0, OP.mult, OP.is_gt)], ["pt" + C],
+            ["de%d_%d" % (c, t)], ak, dur=vd(64))
+        add("P", "pc" + C, lambda: [P.matmul(G, kb["w%d_%d" % (k, t)], dec(c, t), False, not counts)], ["de%d_%d" % (c, t), "w%d_%d" % (k, t)], (), bk, dur=pe(1))
+        if counts:
+            total(c, (5,), True)
+            add("V", "nb", lambda: [V.tensor_scalar(T.nb[:, :], T.bf[:, :], acol, None, OP.add)], ["b4a"], ["nb"], bk, dur=vd(4))
+        if t < 5 or k == 0:
+            add("P", "pw" + C, lambda: sums(c, a, 64, T.wh, True, False), ["wh" + C], (), ak, dur=pe(2), n=2)
+            add("V", "mi" + C, lambda: [V.tensor_tensor(T.mi[:, w], G, T.ee[:, w], OP.min)], ["ee" + C], ["mi" + C], bk, dur=vd(64))
 
-    def trials(k, b1, b2):
-        for c in range(NC):
-            first(k, c)
+    def changed(c):
+        a, b, C, w = T["pa%d" % c], T["pb%d" % c], str(c), slice(64 * c, 64 * c + 64)
+        add("V", "md" + C, lambda: [V.tensor_scalar(T.mk[:, w], b[:, 0:64], 0.0, None, OP.is_gt)], (), ["mk" + C], ["pb" + C], dur=vd(64))
+        add("V", "md" + C, lambda: [V.tensor_tensor(T.md[:, w], T.mk[:, w], a[:, 256:320], OP.mult)], ["mk" + C], ["md" + C], ["pa" + C], dur=vd(64))
+        add("V", "md" + C, lambda: [V.tensor_tensor(T.nw[:, w], T.md[:, w], a[:, 320:384], OP.add)], ["md" + C], ["new" + C], ["pa" + C], dur=vd(64))
+
+    def trials(k, bb, bkeys):
         for t in range(1, 6):
             for c in range(NC):
-                trial(k, c, t, b1, b2)
+                if k == 0 and t == 5 and c == NC - 1:
+                    continue
+                trial(k, c, t, bb, bkeys)
     order(0)
-    trials(0, "b1", "b2")
-    ts("r2t", T.r2t[:, :], T.row8[:, :], "row8 ps lam1", cf["ps"], OP.is_equal, cf["lam1"], OP.mult, n=8)
-    ts("r2f", T.r2f[:, :], T.r2t[:, :], "r2t", 128.0, OP.mult, n=8)
-    ts("r2", T.r2[:, :], T.r2t[:, :], "r2t", 128.0, OP.mult, n=8)
-    for s in range(8):
-        ts("lk%d" % s, kb["lk%d" % s], kf["mrow"], "mrow r2f", 0.0, OP.mult, T.r2f[:, s:s + 1], OP.add)
-    ts("sameb", kb["sameb"], kf["sm"], "sm ps", cf["ps"], OP.is_equal)
+    trials(0, T.b4, ["b0", "b1", "b2", "b3"])
     round_consts(1)
-    nwk = ["new%d" % c for c in range(NC)] + ["po"]
-    add("S", "un1", lambda: [S.activation(T.src[:, 0:128], T.nw[:, :].indirect(T.po[:, 0:8]), AF.Copy)], nwk, ["srcA"], dur=sd(128, GR))
-    add("V", "un2", lambda: [V.tensor_copy(T.src[:, 128:256], T.nw[:, :].indirect(T.po[:, 8:16]))], nwk, ["srcB"], dur=50 + vd(128, GR))
-    add("V", "xo", lambda: [V.tensor_copy(T.xo[:, e:256:2], T.src[:, 128 * e:128 * e + 128]) for e in (0, 1)], ["srcA", "srcB"], xok, dur=2 * vd(128), n=2)
-    add("V", "red", lambda: [V.tensor_reduce(cf["asum"], T.pf[:, :], AxisListType.X, OP.add)], ["pf%d" % c for c in range(NC)], ["asum"], dur=vd(128))
-    add("V", "red", lambda: [V.tensor_scalar(cf["nb" + e], cf["asum"], cf["b" + e], 1984.0, OP.add, OP.add) for e in "12"], ["asum", "b1", "b2"],
-        ["nb1", "nb2"], dur=2 * vd(1), n=2)
-    measure_all(T.shs, slots, "nb1", "nb2")
+    for t in range(1, 6):
+        sc("ah%d" % t, kb["ah%d" % t], kb["w0_1"], "w0_1", HS[t - 1] / 4096.0)
+    ts("b4a", T.bf[:, :], T.b4[:, :], "b0 b1 b2 b3 dc", 3968.0, OP.add, n=4)
+    trial(0, NC - 1, 5, T.b4, ["b0", "b1", "b2", "b3"])
+    for c in range(NC):
+        now[0] = CFG["N"][2] + c
+        keys = measure(c, "mask", T.sh0, slots, T.nb, ["nb"], CFG["USM"], CFG["CUTM"])
+        changed(c)
+        spread(c, keys, T.ds, "ds")
+    nwk = ["new%d" % c for c in range(NC)]
+    add("S", "un1", lambda: [S.activation(T.src[:, 0:128], T.nw[:, 0:256].indirect(T.po[:, 0:8]), AF.Copy)], nwk + ["po0"], ["srcA"], dur=65 + 106 * GR)
+    add("V", "un2", lambda: [V.tensor_copy(T.src[:, 128:256], T.nw[:, 0:256].indirect(T.po[:, 8:16]))], nwk + ["po0"], ["srcB"], dur=50 + 106 * GR)
+    dsk = ["ds%d" % c for c in range(NC)] + ["poq0"]
+    add("S", "un1", lambda: [S.activation(T.dd[:, 0:64], T.ds[:, :].indirect(T.po[:, 16:20]), AF.Copy)], dsk, ["du0", "dd0", "dd1"], dur=65 + 53 * GR)
+    add("V", "un2", lambda: [V.tensor_copy(T.dd[:, 64:128], T.ds[:, :].indirect(T.po[:, 20:24]))], dsk, ["du1", "dd2", "dd3"], dur=50 + 53 * GR)
     order(1)
-    s_q = send(["qo"], lambda q: T.qo[:, :], T.lq[:, big(r)], "aq")
-    arrive("aq", others, "lq", s_q, 6000.0)
+    send(["qo", "qp"], (1, 2, 3), eng_of, lambda b: T.qo[:, :], lambda b: T.lq[:, 144 * b:144 * b + 144], "aq", "lq", 4000.0)
 
-    def yq():
-        o = []
-        for b in (0, 1):
-            p = 32 * r + 16 * b
-            for q in range(4):
-                s = T.qo[p:p + 1, :] if q == r else T.lq[p:p + 1, big(q)]
-                o.append(g.sync.dma_start(T.yq[2 * q + b:2 * q + b + 1, :], s))
-        return o
-    add("Y", "douq", yq, ["qo", "lq"], ["yq"], dur=800, lat=2000, n=8, inc=16)
-    trials(1, "nb1", "nb2")
+    def home(b, p, a, z):
+        return T.lq[p, 144 * b + a:144 * b + z] if b else T.qo[p, a:z]
+    add("Y", "douq", lambda: [Y.dma_start(T.yq[2 * (b ^ r) + j:2 * (b ^ r) + j + 1, :], home(b, slice(32 * b + 16 * j, 32 * b + 16 * j + 1), 0, 128))
+                              for b in range(4) for j in (0, 1)], ["qo", "lq"], ["yq"], dur=800, lat=2000, n=8, inc=16)
+    add("V", "ho", lambda: [V.tensor_scalar(T.ho[rows(b), :], home(b, rows(b), 128, 144), 256.0 * b, None, OP.add) for b in range(4)], ["qp", "lq"], ["ho"],
+        dur=4 * vd(16), n=4)
+    trials(1, T.nb, ["nb"])
+    for c in range(NC):
+        changed(c)
 
-    add("S", "un1", lambda: [S.activation(T.ou[:, 0:256:2], T.nw[:, :].indirect(T.po[:, 0:8]), AF.Identity, bias=2048.0)], nwk, ["ouA"], dur=sd(128, GR))
-    add("V", "un2", lambda: [V.tensor_scalar(T.ou[:, 1:256:2], T.nw[:, :].indirect(T.po[:, 8:16]), 2048.0, None, OP.add)], nwk, ["ouB"],
-        dur=50 + vd(128, GR))
-
-    def copies(eng, sem, cps, reads, key):
-        def fn():
-            return [V.tensor_copy(d, s) if eng == "V" else S.activation(d, s, AF.Copy) for d, s in cps]
-        add(eng, sem, fn, reads, [key], dur=(vd(64) if eng == "V" else sd(64)) * len(cps), n=len(cps))
-    blocks = [(T.sto[32 * a:32 * a + 32, 64 * q:64 * q + 64], T.ou[rows(q), 64 * a:64 * a + 64]) for q in others for a in range(4)]
-    copies("V", "x0", blocks[:7], ["ouA", "ouB"], "stoV")
-    copies("S", "sq0", blocks[7:], ["ouA", "ouB"], "stoS")
-    s_o = send(["stoV", "stoS"], lambda q: T.sto[:, 64 * q:64 * q + 64], T.lr[:, 64 * r:64 * r + 64], "al%d" % r)
-    add("Y", "dou", lambda: [g.sync.dma_start(T.yu[rows(r), :], T.ou[rows(r), :])], ["ouA", "ouB"], ["yu"], dur=100, lat=2000, inc=16)
-
-    def back(j, q):
-        arrive("al%d" % q, [q], "lr%d" % q, s_o, 3000.0 + 500.0 * j)
-        cps = [(T.yo[rows(q), 64 * a:64 * a + 64], T.lr[32 * a:32 * a + 32, 64 * q:64 * q + 64]) for a in range(4)]
-        m = 3 if j < 2 else 2
-        copies("V", "x1", cps[:m], ["lr%d" % q], "yoV%d" % q)
-        copies("S", "sq1", cps[m:], ["lr%d" % q], "yoS%d" % q)
-        add("Y", "dou", lambda: [g.sync.dma_start(T.yu[rows(q), :], T.yo[rows(q), :])], ["yoV%d" % q, "yoS%d" % q], ["yu%d" % q], dur=100, lat=2000, inc=16)
-    for j, q in enumerate(near + off):
-        back(j, q)
-    return emit(T, dict(V=V, S=S, P=P, G=g, Y=g.sync), tasks, count)
+    for j in (0, 1):
+        send(nwk[2 * j:2 * j + 2], (1, 2, 3), eng_of, (lambda j: lambda b: T.nw[:, big(j)])(j),
+             (lambda j: lambda b: T.nw[:, 256 * b + 128 * j:256 * b + 128 * j + 128])(j), "al", "ln%d" % j, 3000.0)
+    hk = nwk + ["ln1", "ho"]
+    add("S", "un1", lambda: [S.activation(T.ou[:, 0:256:2], T.nw[:, :].indirect(T.ho[:, 0:8]), AF.Identity, bias=2048.0)], hk, ["ouA"], dur=65 + 106 * GR)
+    add("V", "un2", lambda: [V.tensor_scalar(T.ou[:, 1:256:2], T.nw[:, :].indirect(T.ho[:, 8:16]), 2048.0, None, OP.add)], hk, ["ouB"], dur=50 + 106 * GR)
+    for j, E in ((0, Y), (1, S)):
+        mine = runs[j::2]
+        if mine:
+            add("YS"[j], "dou", (lambda E, mine: lambda: [E.dma_start(T.yu[b, :], T.ou[a, :]) for a, b in mine])(E, mine), ["ouA", "ouB"], ["yu%d" % j],
+                dur=100 * len(mine), lat=2000, n=len(mine), inc=16)
+    return emit(T, dict(V=V, S=S, P=P, G=g, Y=Y), tasks, count)
 
 
 def place(tasks, pred, succ, key, back):
-    n = len(tasks)
+    n, wake = len(tasks), CFG["WAKE"]
     need, st, busy = [len(p) for p in pred], [0.0] * n, {}
     pool = set(i for i in range(n) if need[i] == 0)
     while pool:
@@ -495,7 +568,7 @@ def place(tasks, pred, succ, key, back):
         t = tasks[i]
         s, d = 0.0, t["dur"]
         for p, hard in pred[i]:
-            s = max(s, st[p] + tasks[p]["dur"] + ((t if back else tasks[p])["lat"] + WAKE if hard else 0.0))
+            s = max(s, st[p] + tasks[p]["dur"] + ((t if back else tasks[p])["lat"] + wake if hard else 0.0))
         if t["eng"] != "R":
             iv = busy.setdefault(t["eng"], [])
             j = len(iv)
@@ -513,33 +586,33 @@ def place(tasks, pred, succ, key, back):
     return st
 
 
-def bias(t):
-    x = t["sem"]
-    y = x.rstrip("0123456789")
-    return SB.get(y, 0.0) + (LB * (3 - int(x[len(y):])) if y != x and len(y) <= 2 and y in LANE else 0.0)
-
-
 def emit(T, E, tasks, count):
-    n = len(tasks)
+    n, wake = len(tasks), CFG["WAKE"]
     pred, succ, before = [[] for _ in range(n)], [[] for _ in range(n)], {}
     for i, t in enumerate(tasks):
-        if t["sem"] in before and tasks[before[t["sem"]]]["eng"] == t["eng"]:
-            t["soft"].add(before[t["sem"]])
+        p = before.get(t["sem"])
+        if p is not None and t["eng"] != "R":
+            if t["sem"] not in FREE:
+                t["deps"].add(p)
+            elif tasks[p]["eng"] == t["eng"]:
+                t["soft"].add(p)
         before[t["sem"]] = i
         for hard, ds in ((1, t["deps"]), (0, t["soft"] - t["deps"])):
             for d in ds:
                 pred[i].append((d, hard))
                 succ[d].append((i, hard))
-    rest = [0.0] * n
+    key = [0.0] * n
     for i in range(n - 1, -1, -1):
-        rest[i] = tasks[i]["dur"] + tasks[i]["lat"] + max([rest[j] + WAKE for j, h in succ[i] if h] or [0.0])
-    st = place(tasks, pred, succ, [-x - bias(t) for x, t in zip(rest, tasks)], False)
+        t = tasks[i]
+        late = min([key[j] - (wake + t["lat"] if h else 0.0) for j, h in succ[i]] or [CFG["N"][4] * CFG["Q"]]) - t["dur"]
+        key[i] = late if t["plan"] is None else t["plan"]
+    st = place(tasks, pred, succ, key, False)
     best = (1e18, None)
-    for k in range(ITERS + 1):
+    for k in range(CFG["ITERS"] + 1):
         end = max(s + t["dur"] + t["lat"] for s, t in zip(st, tasks))
         if end < best[0]:
             best = (end, st)
-        if k < ITERS:
+        if k < CFG["ITERS"]:
             sb = place(tasks, succ, pred, [-(s + t["dur"]) for s, t in zip(st, tasks)], True)
             st = place(tasks, pred, succ, [-(s + t["dur"]) for s, t in zip(sb, tasks)], False)
     st, seq = best[1], {}
@@ -565,7 +638,7 @@ def emit(T, E, tasks, count):
                                 ck[s] = max(ck.get(s, 0), v)
                     for ins in t["fn"]():
                         ins.then_inc(T.sem[t["sem"]], t["inc"])
-                after[i] = dict(ck)
+                after[i] = dict(ck) if e != "R" else {}
                 after[i][t["sem"]] = max(ck.get(t["sem"], 0), t["val"])
                 pos[e] += 1
                 left -= 1

@@ -6,37 +6,39 @@ BIG = 786432.0
 SHIFT = 53 * 4096.0
 HS = (16, 8, 4, 2, 1)
 MS = (2, 1)
-SFROM = 5
-CFG = dict(US=31, USM=28, CUT=0, CUTM=0, YE="V", GR=1.56, VF=12.0, SFX=65.0, PEC=0.6, WAKE=130.0, ITERS=0, Q=1440.0, N=(0, 12, 33, 44, 70),
-           PHI=dict(y=-3280.0, sq=-2500.0, t=-1740.0, sf=-3140.0, of=-2360.0, ga=-800.0, gb=-700.0, gv=300.0, mx=-1700.0, mn=700.0, mx_=900.0, mn_=1100.0,
-                    de=300.0, mi=1780.0))
+SFROM = 6
+CFG = dict(US=28, A0=18, A1=32, A2=28, A3=32, B0=26, B1=32, B2=32, B3=29, C0=28, C1=31, C2=30, C3=31, D0=22, D1=26, D2=28, D3=32, CUT=20, MK="V", DC=3,
+           HOME=((0, 2), (2, 3), (3, 4)), VB=1, VD=0, VW=2, YE="V", GR=1.56, VF=12.0, SFX=65.0, PEC=0.71, WAKE=150.0, ITERS=1, Q=1440.0, N=(0, 12, 33, 44, 70),
+           FIX=((17, 32), (49, 64)), EARLY=11, LATD=4000.0,
+           PHI=dict(px=-0.2, pv=-0.08, y=0.02, py=0.08, pz=0.11, sq=0.33, t=0.57, sf=0.75, of=1.47, gv=1.68, ga=1.76, gb=1.96, mx=2.05, mn=2.15,
+                    mx_=2.25, mn_=2.39, pg=2.37, pw=2.43, pd=2.55, pe=2.57, de=2.92, pc=3.42, mi=3.49, pw2=3.52))
 
 F32M = ["mrow", "sm", "im", "idf", "le", "same", "tmp"]
 B16M = (["ineg", "idb", "sameb", "ones", "spr0", "spr1", "lr0", "lr1"] + ["br%d" % t for t in range(2, 6)] + ["dg%d" % t for t in range(1, 7)]
         + ["lk%d" % s for s in range(8)] + ["w%d_%d" % (k, t) for k in (0, 1) for t in range(1, 7)] + ["ah%d" % t for t in range(1, 6)])
 H16M = ["tri", "onesb", "i64h", "idd"] + [n + k for n in ("pm", "dm", "tp", "op") for k in "01"]
-COLF = ["pcf", "ps", "pi", "k5", "u5", "fc", "ad0", "ad1", "ad2", "sa", "sb"] + [n + k for n in ("mu", "lam", "px", "psx", "spc", "s2_", "s1_", "d5_") for k in "01"]
+COLF = ["pcf", "ps", "pi", "k5", "u5", "fc", "ad0", "ad1", "ad2", "ad3", "s32", "sa"] + [n + k for n in ("mu", "lam", "px", "psx", "spc", "s2_", "s1_", "d5_") for k in "01"]
 COLI = ["pc", "psi", "ii", "odd", "bit0", "bit1", "k5i", "u5i", "sai", "sbi"]
 SCRATCH = {"cc": ("sbuf", [128, 8, 128], "bfloat16"), "st": ("dram", [512, 1024], "bfloat16"), "lsh": ("dram", [512, 1024], "bfloat16")}
 for _d, _l in (("float32", (("kf", 128 * len(F32M)), ("cf", len(COLF)), ("row8", 8), ("ind", 8), ("sq", 256), ("md", 256), ("ee", 256), ("ea", 256),
                             ("b4", 4), ("nb", 4), ("bf", 4), ("nf", 5), ("cum", 5), ("dc", 5), ("one5", 5), ("urow", 64),
-                            ("nw", 1024), ("kc", 8), ("src", 384), ("win", 384), ("ou", 256), ("qo", 144), ("lq", 576))),
+                            ("nw", 1024), ("kc", 2), ("src", 384), ("win", 384), ("ou", 256), ("qo", 144), ("lq", 576))),
                ("bfloat16", (("kb", 128 * len(B16M)), ("r2", 8), ("num", 512), ("sg8", 16), ("cl", 128), ("cr", 400), ("mmx", 1024), ("mmn", 1024),
                              ("sh0", 4096), ("y", 256), ("ga", 4096), ("mx", 4096), ("mn", 4096), ("mk", 256), ("wsp", 16),
                              ("pat", 132), ("one0", 65), ("del", 64), ("pt", 528), ("tk", 256), ("de", 20 * 66), ("dd", 128), ("ds", 128), ("dl", 512))),
                ("float16", (("kh", 128 * len(H16M)), ("xo", 256), ("lx", 1024), ("mi", 256), ("wh", 384))),
                ("int32", (("ci", len(COLI)), ("bi", 4), ("un0", 256), ("t3", 256), ("sf", 256))),
-               ("uint16", (("of", 256), ("po", 48), ("ho", 16)))):
+               ("uint16", (("of", 256), ("po", 56), ("ho", 16)))):
     for _n, _w in _l:
         SCRATCH[_n] = ("sbuf", [128, _w], _d)
 for _i in range(4):
     SCRATCH["pa%d" % _i] = ("psum", [128, 512], "float32")
     SCRATCH["pb%d" % _i] = ("psum", [128, 512], "float32")
-LANE = "pw px pv py pz y sq t sf of ga gv mx mn pd pe de pg pc mi pt ea md dd".split()
-ONE = ("vk0 vk1 vk2 vk3 sk0 sk1 gk pu su xo pkc kc pk pr0 pr1 pr2 pr3 pr4 pr5 cv cs pq sq_ pl po poq scat scq pA nb un1 un2 ho "
-       "dun dst0 dst1 dst2 dsh dbo douq dou ax ash0 ash1 ash2 ad aq al loc").split()
+LANE = "pw px pv py y sq t sf of ga gb gv mx mn mx_ mn_ pd de pg pc mi pt md".split()
+ONE = ("vk0 vk1 vk2 vk3 sk0 sk1 gk xo kc pk pr0 pr1 pr2 pr3 pc_0 pc_1 pc_2 pc_3 cv0 cv1 cv2 cv3 pq sq_ pl po poq scat scq pA nb un1 un2 ho "
+       "dun dst0 dst1 dst2 dsh dbo douq dou ax ash ashn ashf adn adf aq al loc lod").split()
 SEMAPHORES = [s + str(c) for s in LANE for c in range(NC)] + ONE
-FREE = ("cv", "cs", "loc", "dbo", "dou", "pk")
+FREE = ("loc", "dbo", "dou", "pl", "pd0", "pd1", "pd2", "pd3")
 
 
 def vd(n, rate=1.0):
@@ -60,7 +62,7 @@ def rank_program(g, core, T, topo):
     GR = CFG["GR"]
     tasks, lastw, readers, bank, count, turn, now = [], {}, {}, {}, {}, {}, [0]
 
-    def add(eng, sem, fn, reads=(), writes=(), banks=(), dur=60.0, lat=0.0, n=1, inc=1, extra=()):
+    def add(eng, sem, fn, reads=(), writes=(), banks=(), dur=60.0, lat=0.0, n=1, inc=1, extra=(), kind=None):
         i = len(tasks)
         deps, soft = set(extra), set()
         for k in list(reads) + list(writes):
@@ -83,9 +85,10 @@ def rank_program(g, core, T, topo):
             lastw[k] = i
             readers[k] = []
         count[sem] = count.get(sem, 0) + n * inc
-        kind = sem.rstrip("0123456789")
-        plan = now[0] * CFG["Q"] + CFG["PHI"][kind] if kind in CFG["PHI"] and "win" not in reads else None
-        tasks.append(dict(eng=eng, sem=sem, val=count[sem], inc=inc, fn=fn, deps=deps, soft=soft - deps, dur=dur, lat=lat, plan=plan))
+        kind = kind or sem.rstrip("0123456789")
+        plan = (now[0] + CFG["PHI"][kind]) * CFG["Q"] if kind in CFG["PHI"] else None
+        tasks.append(dict(eng=eng, sem=sem, val=count[sem], inc=inc, fn=fn, deps=deps, soft=soft - deps, dur=dur, lat=lat, plan=plan,
+                          fixed=plan is not None and any(a <= now[0] + CFG["PHI"][kind] < z for a, z in CFG["FIX"])))
         return i
 
     def mats(buf, names):
@@ -119,18 +122,24 @@ def rank_program(g, core, T, topo):
     eng_of = {b: offe[share * j:share * j + share] for j, b in enumerate(off)}
     eng_of[near[0]] = neare
 
-    def send(reads, blocks, engines, src_of, dst_of, sem, key, lat):
+    def send(reads, blocks, engines, src_of, dst_of, sem, key, lat, apart=False, after=None):
+        tag = {b: ("n" if b in near else "f") if apart else "" for b in blocks}
+
         def fn():
             tr = []
             for b in blocks:
                 rid, pid = topo.addr(cores[b ^ r], core)
                 tr.append(RemoteDMATransfer(dst_ids=[DstId(rid=rid, pnc=pid)], dma_engine_mask=sum(1 << e for e in engines[b]),
-                                            remote_sem=T.sem[sem], src=src_of(b), dst=dst_of(b)))
-            g.remote_dma_fused(tr, local_sem=T.sem["loc"])
+                                            remote_sem=T.sem[sem + tag[b]], src=src_of(b), dst=dst_of(b)))
+            g.remote_dma_fused(tr, local_sem=T.sem["lod" if sem == "ad" else "loc"])
             return []
-        n = sum(len(engines[b]) for b in blocks)
-        i = add("G", "loc", fn, reads, (), dur=800, lat=1000, n=n)
-        return add("R", sem, None, (), [key], dur=0.0, lat=lat, n=n, extra=[i])
+        i = add("G", "lod" if sem == "ad" else "loc", fn, reads, (), dur=800, lat=1000, n=sum(len(engines[b]) for b in blocks))
+        if after is not None:
+            tasks[i]["soft"].add(after)
+        for x in sorted(set(tag.values())):
+            add("R", sem + x, None, (), [key + x], dur=0.0, lat=lat - (1000.0 if x == "n" else 0.0), n=sum(len(engines[b]) for b in blocks if tag[b] == x),
+                extra=[i])
+        return i
 
     span = 128 if r == 0 else 32 * (r & -r)
     runs = [(slice(p, p + span), slice(p ^ (32 * r), (p ^ (32 * r)) + span)) for p in range(0, 128, span)]
@@ -141,13 +150,14 @@ def rank_program(g, core, T, topo):
     stage(0, off[0], [])
     i = add("Y", "dsh", lambda: [Y.dma_start(T.sh0[a, :], T.shelf[b, :]) for a, b in runs], (), ["sh0"], dur=100 * len(runs), lat=7000, n=len(runs), inc=16)
     tasks[i]["soft"].add(i - 1)
-    stage(1, off[1], ["st%d" % off[0]])
+    stage(1, off[1], ["sh0"])
     stage(2, near[0], ["sh0"])
 
     def const(eng, fn, reads, key, dur):
         m = {"V": 4, "S": 2, "G": 1}[eng]
         turn[eng] = turn.get(eng, 0) + 1
-        add(eng, "gk" if eng == "G" else "%sk%d" % (eng.lower(), turn[eng] % m), lambda: [fn()], reads, [key], dur=dur)
+        i = add(eng, "gk" if eng == "G" else "%sk%d" % (eng.lower(), turn[eng] % m), lambda: [fn()], reads, [key], dur=dur)
+        tasks[i]["spare"] = now[0] > 0
 
     def iota(key, out, pattern, base, cm, n, flag=True):
         kw = dict(allow_small_or_imprecise_dtypes=True) if flag else {}
@@ -199,8 +209,7 @@ def rank_program(g, core, T, topo):
         ms(name, buf[:, 0:1024:32], v, 32)
 
     send(xok, (1, 2, 3), eng_of, lambda b: T.xo[:, :], lambda b: T.lx[:, 256 * b:256 * b + 256], "ax", "lx", 3000.0)
-    for j, b in enumerate(off + near):
-        send(["st%d" % b], (b,), {b: offe if b in off else neare}, lambda b: T.st[big(b), :], lambda b: T.lsh[big(b), :], "ash%d" % j, "lsh%d" % b, 5000.0)
+    send(["st%d" % off[0]], off[:1], {off[0]: offe}, lambda b: T.st[big(b), :], lambda b: T.lsh[big(b), :], "ash", "lsh", 5000.0)
     slots = ["sh0", "sh1", "sh2", "sh3"]
 
     def sums(c, bank_, at, xb, start, stop):
@@ -208,7 +217,13 @@ def rank_program(g, core, T, topo):
         return [P.matmul(bank_[:, at:at + 64], kh["tri"], xb[:, o:o + 64], start, False),
                 P.matmul(bank_[:, at + 1:at + 64:2], kh["onesb"], xb[:, o:o + 64:2], False, stop)]
 
-    def measure(c, kind, shelf, skeys, bb, bkeys, us, cut):
+    def cast(eng, sem, out, in_, n, reads, writes, kind=None):
+        if eng == "G":
+            add("G", sem, lambda: [g.affine_select(out, in_, [[0, n]], OP.is_ge, 0.0, 0, 0)], reads, writes, dur=170 + 1.66 * n, kind=kind)
+        else:
+            add("V", sem, lambda: [V.tensor_copy(out, in_)], reads, writes, dur=vd(n), kind=kind)
+
+    def measure(c, kind, shelf, skeys, bb, bkeys, us, cut, ofe, flip=False):
         a, b, C, o, v = T["pa%d" % c], T["pb%d" % c], str(c), 64 * c, 1024 * c
         ak, bk, w, j = ["pa" + C], ["pb" + C], slice(o, o + 64), 2 if kind == "mask" else 0
         XY, X1, X0 = a[:, 64:128], a[:, 128:192], b[:, 128:192]
@@ -240,12 +255,12 @@ def rank_program(g, core, T, topo):
         else:
             add("S", "y" + C, lambda: [S.activation(T.y[:, w], XY, AF.Identity, bias=bb[:, j:j + 1])], bkeys, ["y" + C], ak, dur=sd(64))
         add("P", "py" + C, lambda: [P.matmul(X0, kb["ineg"], T.y[:, w], False, True)], ["y" + C, "ineg"], (), bk, dur=pe(1))
-        add("P", "pz" + C, f1, keys + ["cl", "cr0", "i64h"], (), ak, dur=pe(n[2]), n=n[2])
+        add("P", "pw" + C, f1, keys + ["cl", "cr0", "i64h"], (), ak, dur=pe(n[2]), n=n[2], kind="pz")
         add("S", "sq" + C, lambda: [S.activation(T.sq[:, w], X0, AF.Square, bias=bb[:, j + 1:j + 2])], bkeys, ["sq" + C], bk, dur=sd(64))
         add("V", "t" + C, lambda: [V.tensor_tensor(T.t3[:, w], T.sq[:, w], X1, OP.add)], ["sq" + C], ["t3" + C], ak, dur=vd(64))
         add("V", "sf" + C, lambda: [V.tensor_scalar(T.sf[:, w], T.t3[:, w], 6, 4095, OP.arith_shift_right, OP.bitwise_and)], ["t3" + C], ["sf" + C],
             dur=vd(64))
-        add("V", "of" + C, lambda: [V.tensor_copy(T.of[:, w], T.sf[:, w])], ["sf" + C], ["of" + C], dur=vd(64))
+        cast(ofe, "of" + C, T.of[:, w], T.sf[:, w], 64, ["sf" + C], ["of" + C])
 
         def gather(eng, sem, a, z):
             out, src = T.ga[:, v + 32 * a:v + 32 * z], shelf[:, :].indirect(T.of[:, o + 2 * a:o + 2 * z])
@@ -254,9 +269,10 @@ def rank_program(g, core, T, topo):
 
         def scans(tag, a, z, keys):
             s = slice(v + 32 * a, v + 32 * z)
-            for nm, buf, mask, op in (("mx", T.mx, T.mmx, OP.max), ("mn", T.mn, T.mmn, OP.min)):
+            both = [(T.mx, T.mmx, OP.max), (T.mn, T.mmn, OP.min)]
+            for nm, (buf, mask, op) in zip(("mx", "mn"), both[::-1] if flip else both):
                 add("V", nm + tag + C, (lambda buf, mask, op: lambda: [V.tensor_tensor_scan(buf[:, s], mask[:, 0:32 * (z - a)], T.ga[:, s], 0.0, OP.add, op)])(buf, mask, op),
-                    keys + ["m" + nm], [nm + tag + C], dur=vd(32 * (z - a), 0.5))
+                    keys + ["mmx", "mmn"], [nm + tag + C], dur=vd(32 * (z - a), 0.5))
         gv = ["gv" + C] if us < CU else []
         vu = CU - us
         if vu:
@@ -274,12 +290,12 @@ def rank_program(g, core, T, topo):
     def ext(buf, c):
         return buf[:, 1024 * c + 31:1024 * c + 1024:32]
 
-    def spread(c, keys, out, key):
-        add("V", "dd%d" % c, lambda: [V.tensor_tensor(out[:, 32 * c:32 * c + 32], ext(T.mx, c), ext(T.mn, c), OP.subtract)],
-            keys[0] + keys[1], [key + str(c)], dur=vd(64))
+    def spread(c, keys):
+        add("V", "md%d" % c, lambda: [V.tensor_tensor(T.dd[:, 32 * c:32 * c + 32], ext(T.mx, c), ext(T.mn, c), OP.subtract)],
+            keys[0] + keys[1], ["dd" + str(c)], dur=vd(64))
     for c in range(NC):
         now[0] = c
-        spread(c, measure(c, "own", T.sh0, ["sh0"], T.b4, ["b0", "b1"], CFG["USM"], CFG["CUTM"]), T.dd, "dd")
+        spread(c, measure(c, "own", T.sh0, ["sh0"], T.b4, ["b0", "b1"], CFG["A%d" % c], CFG["CUT"] if c == NC - 1 else 0, "V"))
 
     iota("row8", T.row8[:, :], [[1, 8]], 0, 0, 8)
     iota("neg", T.num[0:1, 0:256], [[0, 2], [-1, 128]], 0, 0, 256)
@@ -369,79 +385,90 @@ def rank_program(g, core, T, topo):
         tc("d5_" + K, "d5_" + K, "", -2048.0, OP.add)
         sc("dg%d" % (5 + k), kb["dg%d" % (5 + k)], kf["idf"], "idf d5_" + K, cf["d5_" + K])
     round_consts(0)
+    tc("s32", "s1_0", "", 32.0, OP.mult)
+    tc("ad3", "ad2", "", 32.0, OP.mult, 31.0, OP.add)
 
     dkeys = ["dd%d" % c for c in range(NC)]
-    send(dkeys, (1, 2, 3), eng_of, lambda b: T.dd[:, :], lambda b: T.dl[:, big(b)], "ad", "dl", 3000.0)
-    for b in near + off:
-        add("Y", "dbo", (lambda b: lambda: [Y.dma_start(T.sh0[rows(b), :], T.lsh[big(b), :])])(b), ["lsh%d" % b] + dkeys, ["sh%d" % b], dur=100, lat=3000, inc=16)
-    add("P", "pu", lambda: [P.matmul(T.pa0[rows(b), 128 * e:128 * e + 128], part(T.kh, H16M, "idd", 32 * b, 32 * b + 32),
+    i = send(dkeys, (1, 2, 3), eng_of, lambda b: T.dd[:, :], lambda b: T.dl[:, big(b)], "ad", "dl", CFG["LATD"], True)
+    left = add("R", "lod", None, (), ["left"], dur=0.0, n=0, extra=[i])
+    send(["st%d" % off[1], "st%d" % near[0]], off[1:] + near, {off[1]: offe, near[0]: neare}, lambda b: T.st[big(b), :], lambda b: T.lsh[big(b), :],
+         "ash", "lsh", 5000.0, True, i)
+    for b, key in ((off[0], "lsh"), (near[0], "lshn"), (off[1], "lshf")):
+        add("Y", "dbo", (lambda b: lambda: [Y.dma_start(T.sh0[rows(b), :], T.lsh[big(b), :])])(b), [key, "left"], ["sh%d" % b], dur=100, lat=2500, inc=16)
+    add("P", "pq", lambda: [P.matmul(T.pa0[rows(b), 128 * e:128 * e + 128], part(T.kh, H16M, "idd", 32 * b, 32 * b + 32),
                                      (T.lx[:, 256 * b + e:256 * b + 256:2] if b else T.xo[:, e:256:2]), True, True) for b in range(4) for e in (0, 1)],
         ["lx", "idd"] + xok, (), ["pa0"], dur=pe(16), n=8)
-    add("S", "su", lambda: [S.activation(T.src[:, 0:256], T.pa0[:, 0:256], AF.Copy)], (), ["srcA", "srcB"], ["pa0"], dur=sd(256))
+    add("S", "sq_", lambda: [S.activation(T.src[:, 0:256], T.pa0[:, 0:256], AF.Copy)], (), ["srcA", "srcB"], ["pa0"], dur=sd(256))
 
-    places = [("pa0", 0, (0, 1)), ("pa1", 0, (2, 3)), ("pb1", 256, (4,)), ("pa3", 256, (5,)), ("pb2", 256, (6,)), ("pb3", 256, (7,))]
+    keyrow = ["pa0", "pa1", "pb1", "pb2"]
+    keycol = ["pa2", "pb3", "pa2", "pb0"]
 
     def order(k):
-        pa2, K, po = T.pa2, str(k), 24 * k
+        K, po, cnt = str(k), 24 * k, T.pa3[:, 448:456]
         dq = [T.dd[:, :] if b == 0 or k else T.dl[:, big(b)] for b in range(4)]
-        dk = ["du0", "du1"] if k else dkeys + ["dl"]
+        dk = [["du"] if k else (["dln" if b in near else "dlf"] if b else dkeys) for b in range(4)]
+        add("P", "pk", lambda: [P.matmul(T[keyrow[b]][:, 256:512], onesrow, T.num[0:1, (0 if low(k, b) else 256):(256 if low(k, b) else 512)], True, False)
+                                for b in range(4)], ["neg", "pos", "ones"], (), keyrow, dur=pe(16), n=4)
 
-        def kcol():
-            o = [P.matmul(pa2[:, 0:8], T.num[0:1, 256:384], T.sg8[0:1, 8 * k:8 * k + 8], True, False)]
-            if k:
-                return o + [P.matmul(pa2[:, 0:8], T.dd[:, :], T.r2[:, :], False, True)]
-            return o + [P.matmul(pa2[:, 2 * b:2 * b + 2], dq[b], T.r2[:, 2 * b:2 * b + 2], False, b == 3) for b in range(4)]
+        def keys(b):
+            B, row, col = str(b), T[keyrow[b]], T[keycol[b]][:, 384 + 2 * b:386 + 2 * b]
+            add("P", "pc_" + B, lambda: [P.matmul(col, T.num[0:1, 256:384], T.sg8[0:1, 8 * k + 2 * b:8 * k + 2 * b + 2], True, False),
+                                         P.matmul(col, dq[b], T.r2[:, 2 * b:2 * b + 2], False, True)],
+                dk[b] + ["pos", "sg8" + K, "r2"], (), [keycol[b]], dur=pe(2), n=2)
+            if b == 3:
+                add("S", "kc", lambda: [S.activation(T.kc[:, :], col, AF.Copy)], (), ["kc"], [keycol[b]], dur=sd(2))
+            add("P", "pr" + B, lambda: [P.matmul(row[:, 256 + 128 * j:384 + 128 * j], kb["lk%d" % (2 * b + j)], dq[b], False, j == 1) for j in (0, 1)],
+                dk[b] + ["lk%d" % (2 * b), "lk%d" % (2 * b + 1)], (), [keyrow[b]], dur=pe(4), n=2)
 
-        def kconst(bn, o, ss):
-            a = 0 if low(k, ss[0] // 2) else 256
-            return P.matmul(T[bn][:, o:o + 128 * len(ss)], onesrow, T.num[0:1, a:a + 128 * len(ss)], True, False)
-
-        def krow(i, bn, o, ss):
-            add("P", "pr%d" % i, lambda: [P.matmul(T[bn][:, o + 128 * j:o + 128 * j + 128], kb["lk%d" % s], dq[s // 2], False, j == len(ss) - 1)
-                                          for j, s in enumerate(ss)], dk + ["lk%d" % s for s in ss], (), [bn], dur=pe(2 * len(ss)), n=len(ss))
-
-        def compare(bn, o, s):
-            src, out = T[bn][:, o:o + 128], T.cc[:, :, 16 * s:16 * s + 16]
-            if s >= SFROM:
-                add("S", "cs", lambda: [S.activation(out, src, AF.Sign, bias=T.kc[:, s:s + 1], scale=-1.0)], ["kc"], ["cc%d" % s], [bn], dur=sd(128))
+        def compare(b):
+            B, row, col = str(b), T[keyrow[b]], T[keycol[b]]
+            io_ = [(T.cc[:, :, 32 * b + 16 * j:32 * b + 16 * j + 16], row[:, 256 + 128 * j:384 + 128 * j]) for j in (0, 1)]
+            if b == 3:
+                add("S", "cv" + B, lambda: [S.activation(out, src, AF.Sign, bias=T.kc[:, j:j + 1], scale=-1.0) for j, (out, src) in enumerate(io_)],
+                    ["kc"], ["cc" + B], [keyrow[b]], dur=2 * sd(128), n=2)
             else:
-                add("V", "cv", lambda: [V.tensor_scalar(out, src, T.kc[:, s:s + 1], None, OP.is_lt if low(k, s // 2) else OP.is_gt)], ["kc"],
-                    ["cc%d" % s], [bn], dur=vd(128))
-        add("P", "pk", lambda: [kconst(*x) for x in places], ["neg", "pos", "ones"], (), [x[0] for x in places], dur=pe(16), n=len(places))
-        add("P", "pkc", kcol, dk + ["pos", "sg8" + K, "r2"], (), ["pa2"], dur=pe(2 if k else 5), n=2 if k else 5)
-        add("V", "kc", lambda: [V.tensor_copy(T.kc[:, :], pa2[:, 0:8])], (), ["kc"], ["pa2"], dur=vd(8))
-        for i in (0, 3, 1, 4, 5, 2):
-            krow(i, *places[i])
-        for bn, o, ss in places:
-            for j, s in enumerate(ss):
-                compare(bn, o + 128 * j, s)
+                add("V", "cv" + B, lambda: [V.tensor_scalar(out, src, col[:, 384 + 2 * b + j:385 + 2 * b + j], None, OP.is_lt if low(k, b) else OP.is_gt)
+                                            for j, (out, src) in enumerate(io_)], (), ["cc" + B], [keyrow[b], keycol[b]], dur=2 * vd(128), n=2)
+
+        def counted(b):
+            add("P", "pl", lambda: [P.matmul(T.pa3[rows(b), 448 + j:449 + j], T.cc[:, j, 32 * b:32 * b + 32], ones1, True, True) for j in range(8)],
+                ["cc%d" % b, "ones"], (), ["pa3"], dur=pe(4.6), n=8)
+        turns = (0, 3, 1, 2) if k else (0, 1, 3, 2)
+        for b in turns[:3]:
+            keys(b)
+        compare(0)
+        keys(2)
+        for b in (1, 3, 2):
+            compare(b)
+        for b in (0, 1, 3, 2):
+            counted(b)
         qr = T.pb0[:, 256:384]
         if k:
-            add("P", "pq", lambda: [P.matmul(qr, kb["sameb"], T.dd[:, :], True, True)], dk + ["sameb"], (), ["pb0"], dur=pe(2))
+            add("P", "pq", lambda: [P.matmul(qr, kb["sameb"], T.dd[:, :], True, True)], ["du", "sameb"], (), ["pb0"], dur=pe(2))
         else:
             add("P", "pq", lambda: [P.matmul(T.pb0[rows(b), 256:384], part(T.kb, B16M, "sameb", 32 * b, 32 * b + 32), dq[b], True, True) for b in range(4)],
-                dk + ["sameb"], (), ["pb0"], dur=pe(8), n=4)
+                dkeys + ["dln", "dlf", "sameb"], (), ["pb0"], dur=pe(8), n=4)
         add("S", "sq_", lambda: [S.activation(T.src[:, 256:384], qr, AF.Identity, bias=-2048.0)], (), ["srcq"], ["pb0"], dur=sd(128))
         if k:
             add("S", "sq_", lambda: [S.activation(T.qo[:, 0:128], qr, AF.Copy)], (), ["qo"], ["pb0"], dur=sd(128))
-        add("P", "pl", lambda: [P.matmul(pa2[:, 8 + j:9 + j], T.cc[:, j, :], ones1, True, True) for j in range(8)],
-            ["cc%d" % s for s in range(8)] + ["ones"], (), ["pa2"], dur=pe(8), n=8)
 
         def lists(sem, key, out, ab):
-            add("V", sem, lambda: [V.tensor_scalar(out(j), pa2[:, 8:16], cf[a], cf[b], OP.mult, OP.add) for j, (a, b) in enumerate(ab)],
-                [x for y in ab for x in y], [key], ["pa2"], dur=len(ab) * vd(8), n=len(ab))
+            add("V", sem, lambda: [V.tensor_scalar(out(j), cnt, cf[a], cf[b], OP.mult, OP.add) for j, (a, b) in enumerate(ab)],
+                [x for y in ab for x in y], [key], ["pa3"], dur=len(ab) * vd(8), n=len(ab))
         both = [("s2_" + K, "ad0"), ("s2_" + K, "ad1")]
         lists("po", "po" + K, lambda j: T.po[:, po + 8 * j:po + 8 * j + 8], both)
         add("V", "scat", lambda: [V.tensor_copy(T.win[:, 0:256].indirect(T.po[:, po:po + 16]), T.src[:, 0:256])], ["po" + K, "srcA", "srcB"], ["win"],
             dur=50 + vd(256, 3.5))
         for c in range(NC):
-            add("V", "mi%d" % c, (lambda w: lambda: [V.tensor_copy(T.wh[:, w], T.win[:, w])])(slice(64 * c, 64 * c + 64)), ["win"], ["wh%d" % c], dur=vd(64))
+            cast("V" if c < CFG["VW"] else "G", "mi%d" % c, T.wh[:, 64 * c:64 * c + 64], T.win[:, 64 * c:64 * c + 64], 64, ["win"], ["wh%d" % c], "-")
         lists("poq", "poq" + K, lambda j: T.po[:, po + 16:po + 24], [("s1_" + K, "ad2")])
         add("V", "scq", lambda: [V.tensor_copy(T.win[:, 256:384].indirect(T.po[:, po + 16:po + 24]), T.src[:, 256:384])], ["poq" + K, "srcq"], ["winq"],
             dur=50 + vd(128, 3.5))
-        add("V", "scq", lambda: [V.tensor_copy(T.wh[:, 256:384], T.win[:, 256:384])], ["winq"], ["whq"], dur=vd(128))
+        cast("G", "scq", T.wh[:, 256:384], T.win[:, 256:384], 128, ["winq"], ["whq"])
         if k:
             lists("poq", "qp", lambda j: T.qo[:, 128 + 8 * j:136 + 8 * j], both)
+        else:
+            lists("poq", "pend", lambda j: T.po[:, 48:56], [("s32", "ad3")])
 
     def dec(c, t, a=0, z=64):
         o = 66 * (5 * c + t - 1)
@@ -459,12 +486,12 @@ def rank_program(g, core, T, topo):
         add("P", "pw" + C, lambda: [half(a[:, 2:3])] + pairs(2, c, W[:, 256 + 32 * c:288 + 32 * c], 8 * k, True)
             + [P.matmul(a[:, 192:256], T.cl[0:1, :], T.cr[0:1, 128:192], True, False), P.matmul(a[:, 192:256], kh["dm" + K], W[:, w], False, True),
                P.matmul(a[:, 256:320], kh["dm" + K], W[:, w], True, True), P.matmul(a[:, 320:384], kh["idd"], W[:, w], True, True)],
-            ["wh" + C, "whq", "dm" + K, "cr2", "cr3", "wsp" + K, "idd"], (), bk, dur=pe(7.2), n=9)
+            ["wh" + C, "whq", "dm" + K, "cr2", "cr3", "wsp" + K, "idd"], (), bk, dur=pe(7.2), n=9, kind="-")
         add("V", "pt" + C, lambda: [V.tensor_scalar(T.pt[:, 132 * c:132 * c + 132], T.pat[:, :], a[:, 2:3], None, OP.mult),
                                     V.tensor_scalar(T.tk[:, w], T["del"][:, :], a[:, 2:3], -1.0, OP.mult, OP.is_lt)],
             ["pat", "del"], ["pt" + C, "tk" + C], bk, dur=2 * vd(66), n=2)
-        add("V", "ea" + C, lambda: [V.tensor_scalar(T.ea[:, w], a[:, 192:256], 2048.0, -4096.0, OP.is_ge, OP.mult)], (), ["ea" + C], bk, dur=vd(64))
-        add("V", "ea" + C, lambda: [V.tensor_tensor(T.ee[:, w], T.ea[:, w], a[:, 192:256], OP.add)], ["ea" + C], ["ee" + C], bk, dur=vd(64))
+        add("V", "md" + C, lambda: [V.tensor_scalar(T.ea[:, w], a[:, 192:256], 2048.0, -4096.0, OP.is_ge, OP.mult)], (), ["ea" + C], bk, dur=vd(64))
+        add("V", "md" + C, lambda: [V.tensor_tensor(T.ee[:, w], T.ea[:, w], a[:, 192:256], OP.add)], ["ea" + C], ["ee" + C], bk, dur=vd(64))
 
     acol = T["pb%d" % (NC - 1)][:, 64:65]
 
@@ -476,7 +503,8 @@ def rank_program(g, core, T, topo):
         a, b, o, C, K = T["pa%d" % c], T["pb%d" % c], 64 * c, str(c), str(k)
         ak, bk, w, G = ["pa" + C], ["pb" + C], slice(o, o + 64), b[:, 0:64]
         now[0] = CFG["N"][1 + 2 * k] + NC * (t - 1) + c
-        kx, kn = measure(c, "mask" if t > 1 else k, T.sh0, slots, bb, bkeys, CFG["US"], CFG["CUT"])
+        kx, kn = measure(c, "mask" if t > 1 else k, T.sh0, slots, bb, bkeys, CFG[{1: "B%d" % c, 5: "C%d" % c}.get(t, "US")],
+                         CFG["CUT"], "V" if t == 1 and c < CFG["VB"] else "G")
         if t == 1:
             before(k, c)
         add("P", "pw" + C, lambda: [half(a[:, 0:1])], ["cr3"], (), ak, dur=pe(1))
@@ -489,7 +517,7 @@ def rank_program(g, core, T, topo):
             for d in range(NC):
                 total(d, range(1, 6 if d < c else 5), False)
         add("P", "pd" + C, lambda: pairs(0, c, ext(T.mx, c), 8 * k, False), kx + ["wsp" + K], (), ak, dur=pe(2.2), n=4)
-        add("P", "pe" + C, lambda: pairs(0, c, ext(T.mn, c), 8 * k + 4, True), kn + ["wsn" + K], (), ak, dur=pe(2.2), n=4)
+        add("P", "pd" + C, lambda: pairs(0, c, ext(T.mn, c), 8 * k + 4, True), kn + ["wsn" + K], (), ak, dur=pe(2.2), n=4, kind="pe")
         p = 132 * c + (66 if t == 1 else 0)
         add("V", "de" + C, lambda: [V.tensor_scalar(dec(c, t, 0, 65), T.pt[:, p:p + 65], a[:, 0:1], 0.0, OP.mult, OP.is_gt)], ["pt" + C],
             ["de%d_%d" % (c, t)], ak, dur=vd(64))
@@ -498,12 +526,18 @@ def rank_program(g, core, T, topo):
             total(c, (5,), True)
             add("V", "nb", lambda: [V.tensor_scalar(T.nb[:, :], T.bf[:, :], acol, None, OP.add)], ["b4a"], ["nb"], bk, dur=vd(4))
         if t < 5 or k == 0:
-            add("P", "pw" + C, lambda: sums(c, a, 64, T.wh, True, False), ["wh" + C], (), ak, dur=pe(2), n=2)
+            add("P", "pw" + C, lambda: sums(c, a, 64, T.wh, True, False), ["wh" + C], (), ak, dur=pe(2), n=2, kind="pw2")
             add("V", "mi" + C, lambda: [V.tensor_tensor(T.mi[:, w], G, T.ee[:, w], OP.min)], ["ee" + C], ["mi" + C], bk, dur=vd(64))
 
+    def taken(c, eng):
+        b, C, w = T["pb%d" % c], str(c), slice(64 * c, 64 * c + 64)
+        if eng == "V":
+            add("V", "md" + C, lambda: [V.tensor_scalar(T.mk[:, w], b[:, 0:64], 0.0, None, OP.is_gt)], (), ["mk" + C], ["pb" + C], dur=vd(64))
+        else:
+            add("S", "md" + C, lambda: [S.activation(T.mk[:, w], b[:, 0:64], AF.Relu, scale=1.0 / 2048)], (), ["mk" + C], ["pb" + C], dur=sd(64))
+
     def changed(c):
-        a, b, C, w = T["pa%d" % c], T["pb%d" % c], str(c), slice(64 * c, 64 * c + 64)
-        add("V", "md" + C, lambda: [V.tensor_scalar(T.mk[:, w], b[:, 0:64], 0.0, None, OP.is_gt)], (), ["mk" + C], ["pb" + C], dur=vd(64))
+        a, C, w = T["pa%d" % c], str(c), slice(64 * c, 64 * c + 64)
         add("V", "md" + C, lambda: [V.tensor_tensor(T.md[:, w], T.mk[:, w], a[:, 256:320], OP.mult)], ["mk" + C], ["md" + C], ["pa" + C], dur=vd(64))
         add("V", "md" + C, lambda: [V.tensor_tensor(T.nw[:, w], T.md[:, w], a[:, 320:384], OP.add)], ["md" + C], ["new" + C], ["pa" + C], dur=vd(64))
 
@@ -520,17 +554,20 @@ def rank_program(g, core, T, topo):
         sc("ah%d" % t, kb["ah%d" % t], kb["w0_1"], "w0_1", HS[t - 1] / 4096.0)
     ts("b4a", T.bf[:, :], T.b4[:, :], "b0 b1 b2 b3 dc", 3968.0, OP.add, n=4)
     trial(0, NC - 1, 5, T.b4, ["b0", "b1", "b2", "b3"])
+    kx, kn = [], []
     for c in range(NC):
         now[0] = CFG["N"][2] + c
-        keys = measure(c, "mask", T.sh0, slots, T.nb, ["nb"], CFG["USM"], CFG["CUTM"])
+        taken(c, CFG["MK"])
+        keys = measure(c, "mask", T.sh0, slots, T.nb, ["nb"], CFG["D%d" % c], CFG["CUT"] if c >= CFG["DC"] else 0,
+                       "V" if c < CFG["VD"] else "G", True)
+        kx, kn = kx + keys[0], kn + keys[1]
         changed(c)
-        spread(c, keys, T.ds, "ds")
     nwk = ["new%d" % c for c in range(NC)]
     add("S", "un1", lambda: [S.activation(T.src[:, 0:128], T.nw[:, 0:256].indirect(T.po[:, 0:8]), AF.Copy)], nwk + ["po0"], ["srcA"], dur=65 + 106 * GR)
     add("V", "un2", lambda: [V.tensor_copy(T.src[:, 128:256], T.nw[:, 0:256].indirect(T.po[:, 8:16]))], nwk + ["po0"], ["srcB"], dur=50 + 106 * GR)
-    dsk = ["ds%d" % c for c in range(NC)] + ["poq0"]
-    add("S", "un1", lambda: [S.activation(T.dd[:, 0:64], T.ds[:, :].indirect(T.po[:, 16:20]), AF.Copy)], dsk, ["du0", "dd0", "dd1"], dur=65 + 53 * GR)
-    add("V", "un2", lambda: [V.tensor_copy(T.dd[:, 64:128], T.ds[:, :].indirect(T.po[:, 20:24]))], dsk, ["du1", "dd2", "dd3"], dur=50 + 53 * GR)
+    add("S", "un1", lambda: [S.activation(T.ds[:, :], T.mn[:, :].indirect(T.po[:, 48:56]), AF.Identity, scale=-1.0)], kx + ["pend"], ["ds"], dur=65 + 106 * GR)
+    add("V", "un2", lambda: [V.tensor_tensor(T.dd[:, :], T.mx[:, :].indirect(T.po[:, 48:56]), T.ds[:, :], OP.add)], kn + ["pend", "ds"], ["du"] + dkeys,
+        dur=50 + 106 * GR)
     order(1)
     send(["qo", "qp"], (1, 2, 3), eng_of, lambda b: T.qo[:, :], lambda b: T.lq[:, 144 * b:144 * b + 144], "aq", "lq", 4000.0)
 
@@ -542,12 +579,13 @@ def rank_program(g, core, T, topo):
         dur=4 * vd(16), n=4)
     trials(1, T.nb, ["nb"])
     for c in range(NC):
+        taken(c, "V" if c == NC - 1 else CFG["MK"])
         changed(c)
 
-    for j in (0, 1):
-        send(nwk[2 * j:2 * j + 2], (1, 2, 3), eng_of, (lambda j: lambda b: T.nw[:, big(j)])(j),
-             (lambda j: lambda b: T.nw[:, 256 * b + 128 * j:256 * b + 128 * j + 128])(j), "al", "ln%d" % j, 3000.0)
-    hk = nwk + ["ln1", "ho"]
+    for a, z in CFG["HOME"]:
+        send(nwk[a:z], (1, 2, 3), eng_of, (lambda a, z: lambda b: T.nw[:, 64 * a:64 * z])(a, z),
+             (lambda a, z: lambda b: T.nw[:, 256 * b + 64 * a:256 * b + 64 * z])(a, z), "al", "ln", 3000.0)
+    hk = nwk + ["ln", "ho"]
     add("S", "un1", lambda: [S.activation(T.ou[:, 0:256:2], T.nw[:, :].indirect(T.ho[:, 0:8]), AF.Identity, bias=2048.0)], hk, ["ouA"], dur=65 + 106 * GR)
     add("V", "un2", lambda: [V.tensor_scalar(T.ou[:, 1:256:2], T.nw[:, :].indirect(T.ho[:, 8:16]), 2048.0, None, OP.add)], hk, ["ouB"], dur=50 + 106 * GR)
     for j, E in ((0, Y), (1, S)):
@@ -589,6 +627,10 @@ def place(tasks, pred, succ, key, back):
 def emit(T, E, tasks, count):
     n, wake = len(tasks), CFG["WAKE"]
     pred, succ, before = [[] for _ in range(n)], [[] for _ in range(n)], {}
+    for i in sorted((i for i in range(n) if tasks[i]["fixed"]), key=lambda i: tasks[i]["plan"]):
+        if tasks[i]["eng"] in before:
+            tasks[i]["soft"].add(before[tasks[i]["eng"]])
+        before[tasks[i]["eng"]] = i
     for i, t in enumerate(tasks):
         p = before.get(t["sem"])
         if p is not None and t["eng"] != "R":
@@ -604,8 +646,12 @@ def emit(T, E, tasks, count):
     key = [0.0] * n
     for i in range(n - 1, -1, -1):
         t = tasks[i]
-        late = min([key[j] - (wake + t["lat"] if h else 0.0) for j, h in succ[i]] or [CFG["N"][4] * CFG["Q"]]) - t["dur"]
+        late = min([key[j] - (wake + t["lat"] if h else 0.0) for j, h in succ[i] if j > i and not tasks[j].get("spare")] or [CFG["N"][4] * CFG["Q"]]) - t["dur"]
         key[i] = late if t["plan"] is None else t["plan"]
+        if t.get("spare"):
+            key[i] = CFG["EARLY"] * CFG["Q"] + i
+        if t["eng"] == "G" and t["sem"] != "gk":
+            key[i] = min(key[i], key[i] - 3 * CFG["Q"])
     st = place(tasks, pred, succ, key, False)
     best = (1e18, None)
     for k in range(CFG["ITERS"] + 1):

@@ -7,26 +7,25 @@ SHIFT = 53 * 4096.0
 HS = (16, 8, 4, 2, 1)
 MS = (2, 1)
 SFROM = 6
-CFG = dict(US=28, A0=18, A1=32, A2=28, A3=32, B0=26, B1=32, B2=32, B3=29, C0=28, C1=31, C2=30, C3=31, D0=22, D1=26, D2=28, D3=32, CUT=20, MK="V", DC=3,
-           HOME=((0, 2), (2, 3), (3, 4)), VB=1, VD=0, VW=2, YE="V", GR=1.56, VF=12.0, SFX=65.0, PEC=0.71, WAKE=150.0, ITERS=1, Q=1440.0, N=(0, 12, 33, 44, 70),
-           FIX=((17, 32), (49, 64)), EARLY=11, LATD=4000.0,
-           PHI=dict(px=-0.2, pv=-0.08, y=0.02, py=0.08, pz=0.11, sq=0.33, t=0.57, sf=0.75, of=1.47, gv=1.68, ga=1.76, gb=1.96, mx=2.05, mn=2.15,
-                    mx_=2.25, mn_=2.39, pg=2.37, pw=2.43, pd=2.55, pe=2.57, de=2.92, pc=3.42, mi=3.49, pw2=3.52))
+CFG = dict(US=28, A0=18, A1=29, A2=24, A3=29, B0=26, B1=28, B2=32, B3=32, C0=29, C1=28, C2=27, C3=30, D0=22, D1=24, D2=28, D3=29, CUT=16, MK="V", DC=3,
+           HOME=((0, 2), (2, 4)), VB=2, VD=0, VW=1, GR=1.56, VF=12.0, SFX=65.0, PEC=0.71, WAKE=170.0, ITERS=1, Q=1440.0, N=(0, 12, 33, 44, 70),
+           FIX=((16, 32), (48, 64)), EARLY=11, LATD=3000.0, LATS=5000.0, KAP=0, FIRST=1, RI=800.0, VQ="V",
+           PHI=dict(px=-0.29, y=0.07, pv=0.14, py=0.22, pz=0.31, sq=0.65, t=0.67, sf=0.95, of=1.01, pg=1.61, gb=1.7, ga=1.72, gv=1.98, mx_=2.08, mn_=2.15,
+                    mx=2.21, pw=2.64, pd=2.83, mn=2.87, pe=2.94, de=3.12, pc=3.36, pw2=3.44, mi=3.56))
 
-F32M = ["mrow", "sm", "im", "idf", "le", "same", "tmp"]
-B16M = (["ineg", "idb", "sameb", "ones", "spr0", "spr1", "lr0", "lr1"] + ["br%d" % t for t in range(2, 6)] + ["dg%d" % t for t in range(1, 7)]
-        + ["lk%d" % s for s in range(8)] + ["w%d_%d" % (k, t) for k in (0, 1) for t in range(1, 7)] + ["ah%d" % t for t in range(1, 6)])
-H16M = ["tri", "onesb", "i64h", "idd"] + [n + k for n in ("pm", "dm", "tp", "op") for k in "01"]
-COLF = ["pcf", "ps", "pi", "k5", "u5", "fc", "ad0", "ad1", "ad2", "ad3", "s32", "sa"] + [n + k for n in ("mu", "lam", "px", "psx", "spc", "s2_", "s1_", "d5_") for k in "01"]
+B16M = (["mrow", "mrow2", "sm", "im", "le", "same", "tri", "ntri", "idd", "ineg", "i64h", "ones"] + ["dg%d" % t for t in range(1, 7)]
+        + ["lk%d" % s for s in range(8)] + ["w%d_%d" % (k, t) for k in (0, 1) for t in range(1, 7)] + ["ah%d" % t for t in range(1, 6)]
+        + [n + k for n in ("pm", "dm", "tp", "op", "rb", "x") for k in "01"])
+COLF = ["pcf", "ps", "pi", "kv", "u5", "fc", "ad0", "ad1", "ad2", "ad3", "s32", "sa"] + [n + k for n in ("mu", "lam", "px", "psx", "spc", "s2_", "s1_", "d5_") for k in "01"]
 COLI = ["pc", "psi", "ii", "odd", "bit0", "bit1", "k5i", "u5i", "sai", "sbi"]
 SCRATCH = {"cc": ("sbuf", [128, 8, 128], "bfloat16"), "st": ("dram", [512, 1024], "bfloat16"), "lsh": ("dram", [512, 1024], "bfloat16")}
-for _d, _l in (("float32", (("kf", 128 * len(F32M)), ("cf", len(COLF)), ("row8", 8), ("ind", 8), ("sq", 256), ("md", 256), ("ee", 256), ("ea", 256),
+for _d, _l in (("float32", (("wc", 4), ("cf", len(COLF)), ("row8", 8), ("ind", 8), ("sq", 256), ("md", 256), ("ee", 256), ("ea", 256),
                             ("b4", 4), ("nb", 4), ("bf", 4), ("nf", 5), ("cum", 5), ("dc", 5), ("one5", 5), ("urow", 64),
                             ("nw", 1024), ("kc", 2), ("src", 384), ("win", 384), ("ou", 256), ("qo", 144), ("lq", 576))),
-               ("bfloat16", (("kb", 128 * len(B16M)), ("r2", 8), ("num", 512), ("sg8", 16), ("cl", 128), ("cr", 400), ("mmx", 1024), ("mmn", 1024),
+               ("bfloat16", (("kb", 128 * len(B16M)), ("r2", 8), ("neg", 256), ("xw", 768), ("sg8", 16), ("cl", 128), ("cr", 400), ("mmx", 1024), ("mmn", 1024),
                              ("sh0", 4096), ("y", 256), ("ga", 4096), ("mx", 4096), ("mn", 4096), ("mk", 256), ("wsp", 16),
                              ("pat", 132), ("one0", 65), ("del", 64), ("pt", 528), ("tk", 256), ("de", 20 * 66), ("dd", 128), ("ds", 128), ("dl", 512))),
-               ("float16", (("kh", 128 * len(H16M)), ("xo", 256), ("lx", 1024), ("mi", 256), ("wh", 384))),
+               ("float16", (("xo", 256), ("xs", 192), ("lx", 192), ("mi", 256), ("wh", 384))),
                ("int32", (("ci", len(COLI)), ("bi", 4), ("un0", 256), ("t3", 256), ("sf", 256))),
                ("uint16", (("of", 256), ("po", 56), ("ho", 16)))):
     for _n, _w in _l:
@@ -38,7 +37,7 @@ LANE = "pw px pv py y sq t sf of ga gb gv mx mn mx_ mn_ pd de pg pc mi pt md".sp
 ONE = ("vk0 vk1 vk2 vk3 sk0 sk1 gk xo kc pk pr0 pr1 pr2 pr3 pc_0 pc_1 pc_2 pc_3 cv0 cv1 cv2 cv3 pq sq_ pl po poq scat scq pA nb un1 un2 ho "
        "dun dst0 dst1 dst2 dsh dbo douq dou ax ash ashn ashf adn adf aq al loc lod").split()
 SEMAPHORES = [s + str(c) for s in LANE for c in range(NC)] + ONE
-FREE = ("loc", "dbo", "dou", "pl", "pd0", "pd1", "pd2", "pd3")
+FREE = ("loc", "dbo", "dou", "dun", "pl", "pd0", "pd1", "pd2", "pd3")
 
 
 def vd(n, rate=1.0):
@@ -93,7 +92,7 @@ def rank_program(g, core, T, topo):
 
     def mats(buf, names):
         return {n: buf[:, 128 * i:128 * i + 128] for i, n in enumerate(names)}
-    kf, kb, kh = mats(T.kf, F32M), mats(T.kb, B16M), mats(T.kh, H16M)
+    kb = mats(T.kb, B16M)
     cf = {n: T.cf[:, i:i + 1] for i, n in enumerate(COLF)}
     ci = {n: T.ci[:, i:i + 1] for i, n in enumerate(COLI)}
     ob = B16M.index("ones") * 128
@@ -133,7 +132,7 @@ def rank_program(g, core, T, topo):
                                             remote_sem=T.sem[sem + tag[b]], src=src_of(b), dst=dst_of(b)))
             g.remote_dma_fused(tr, local_sem=T.sem["lod" if sem == "ad" else "loc"])
             return []
-        i = add("G", "lod" if sem == "ad" else "loc", fn, reads, (), dur=800, lat=1000, n=sum(len(engines[b]) for b in blocks))
+        i = add("G", "lod" if sem == "ad" else "loc", fn, reads, (), dur=CFG["RI"], lat=1000, n=sum(len(engines[b]) for b in blocks))
         if after is not None:
             tasks[i]["soft"].add(after)
         for x in sorted(set(tag.values())):
@@ -143,15 +142,20 @@ def rank_program(g, core, T, topo):
 
     span = 128 if r == 0 else 32 * (r & -r)
     runs = [(slice(p, p + span), slice(p ^ (32 * r), (p ^ (32 * r)) + span)) for p in range(0, 128, span)]
-    add("S", "dun", lambda: [S.dma_start(T.un0[a, :], T.units[b, :]) for a, b in runs], (), ["un0"], dur=100 * len(runs), lat=2000, n=len(runs), inc=16)
+    def both(sem, out, in_, reads, key, lat):
+        for E, e, mine in ((S, "S", runs[0::2]), (Y, "Y", runs[1::2])):
+            if mine:
+                add(e, sem, (lambda E, mine: lambda: [E.dma_start(out(a, b), in_(a, b)) for a, b in mine])(E, mine), reads, [key + e],
+                    dur=100 * len(mine), lat=lat, n=len(mine), inc=16)
+        return [key + e for e in "SY"[:len(runs)]]
+    unk = both("dun", lambda a, b: T.un0[a, :], lambda a, b: T.units[b, :], (), "un0", 2000)
 
-    def stage(j, b, reads):
-        add("Y", "dst%d" % j, lambda: [Y.dma_start(T.st[big(b), :], T.shelf[rows(b ^ r), :])], reads, ["st%d" % b], dur=100, lat=2500, inc=16)
-    stage(0, off[0], [])
-    i = add("Y", "dsh", lambda: [Y.dma_start(T.sh0[a, :], T.shelf[b, :]) for a, b in runs], (), ["sh0"], dur=100 * len(runs), lat=7000, n=len(runs), inc=16)
-    tasks[i]["soft"].add(i - 1)
-    stage(1, off[1], ["sh0"])
-    stage(2, near[0], ["sh0"])
+    add("Y", "dsh", lambda: [Y.dma_start(T.sh0[a, :], T.shelf[b, :]) for a, b in runs], (), ["sh0"], dur=100 * len(runs), lat=6000, n=len(runs), inc=16)
+    tasks[-1]["soft"].add(len(tasks) - 2)
+    for j, b in enumerate(off + near):
+        add("Y", "dst%d" % j, (lambda b: lambda: [Y.dma_start(T.st[big(b), :], T.shelf[rows(b ^ r), :])])(b), ["sh0"] if j >= CFG["FIRST"] else [],
+            ["st%d" % b], dur=100, lat=2500 if j >= CFG["FIRST"] else 7500, inc=16)
+        tasks[-1]["soft"].add(len(tasks) - 2)
 
     def const(eng, fn, reads, key, dur):
         m = {"V": 4, "S": 2, "G": 1}[eng]
@@ -179,14 +183,14 @@ def rank_program(g, core, T, topo):
     def sc(key, out, in0, rk, scale):
         const("S", lambda: S.activation(out, in0, AF.Identity, scale=scale), rk.split(), key, sd(128))
 
-    def diag(name, out, v):
-        ts(name, out, kf["mrow"], "mrow pcf", cf["pcf"], OP.is_equal, v, OP.mult)
+    def hit(name, row, col, v, op=OP.is_equal):
+        ts(name, kb[name], kb[row], row + " " + col, cf[col], op, v, OP.mult, n=64)
     iota("pc", ci["pc"], [[0, 1]], 0, 1, 1, False)
-    iota("mrow", kf["mrow"], [[1, 128]], 0, 0, 128)
-    iota("sm", kf["sm"], [[1, 8], [0, 16]], 0, 0, 128)
-    iota("im", kf["im"], [[0, 8], [1, 16]], 0, 0, 128)
+    iota("sm", kb["sm"], [[1, 8], [0, 16]], 0, 0, 128)
+    iota("im", kb["im"], [[0, 8], [1, 16]], 0, 0, 128)
+    iota("mrow", part(T.kb, B16M, "mrow", 0, 256), [[0, 2], [1, 128]], 0, 0, 256)
     ms("cl", T.cl[:, :], -512.0, 128)
-    for j, v in enumerate((256.0, 512.0, -4.0, 2.0 ** -10)):
+    for j, v in ((0, 256.0), (2, -4.0), (3, 2.0 ** -10)):
         ms("cr%d" % j, T.cr[:, 64 * j:64 * j + 64], v, 64)
     tc("pcf", "pc", "", 1.0, OP.mult)
     tc("psi", "pc", "", 4, OP.arith_shift_right)
@@ -196,26 +200,32 @@ def rank_program(g, core, T, topo):
     tc("pi", "ii", "", 1.0, OP.mult)
     ts("b0", T.b4[:, 0:1], ci["odd"], "odd", -2048.0, OP.mult, BIG + 0.5, OP.add, n=1)
     ts("b1", T.b4[:, 1:2], ci["odd"], "odd", -2048.0, OP.mult, BIG + 2048.0, OP.add, n=1)
-    ts("same", kf["same"], kf["sm"], "sm ps", cf["ps"], OP.is_equal)
-    ts("le", kf["le"], kf["im"], "im pi", cf["pi"], OP.is_ge)
-    tt("tri", kh["tri"], kf["same"], kf["le"], "same le", OP.mult)
-    ts("onesb", kh["onesb"], kf["sm"], "sm ps", cf["ps"], OP.is_equal)
+    hit("same", "sm", "ps", 1.0)
+    hit("le", "im", "pi", 1.0, OP.is_ge)
+    tt("tri", kb["tri"], kb["same"], kb["le"], "same le", OP.mult)
     xok = ["xo%d" % c for c in range(NC)]
-    add("V", "xo", lambda: [V.tensor_scalar(T.xo[:, :], T.un0[:, :], -2048.0, None, OP.add)], ["un0"], xok, dur=vd(256))
-    diag("ineg", kb["ineg"], -1.0)
-    diag("i64h", kh["i64h"], 64.0)
+    add("V", "xo", lambda: [V.tensor_scalar(T.xo[:, :], T.un0[:, :], -2048.0, None, OP.add)], unk, xok, dur=vd(256))
+    hit("idd", "mrow", "pcf", 1.0)
+    hit("ineg", "mrow", "pcf", -1.0)
+    hit("i64h", "mrow", "pcf", 64.0)
     for name, buf, v in (("mmx", T.mmx, -512.0), ("mmn", T.mmn, 512.0)):
         ms(name, buf[:, :], 0.0, 1024)
         ms(name, buf[:, 0:1024:32], v, 32)
 
-    send(xok, (1, 2, 3), eng_of, lambda b: T.xo[:, :], lambda b: T.lx[:, 256 * b:256 * b + 256], "ax", "lx", 3000.0)
+    def block(name, b):
+        return part(T.kb, B16M, name, 32 * b, 32 * b + 32)
+
+    add("P", "pq", lambda: [P.matmul(T.pb3[rows(a), 192 + 64 * b:256 + 64 * b], block("idd", b), T.xo[:, 64 * a:64 * a + 64], True, True)
+                            for b in (1, 2, 3) for a in range(4)], xok + ["idd"], (), ["pb3"], dur=pe(12), n=12)
+    add("V", "xo", lambda: [V.tensor_copy(T.xs[:, :], T.pb3[:, 256:448])], (), ["xs"], ["pb3"], dur=vd(192))
+    send(["xs"], (1, 2, 3), eng_of, lambda b: T.xs[:, 64 * b - 64:64 * b], lambda b: T.lx[:, 64 * b - 64:64 * b], "ax", "lx", 3000.0)
     send(["st%d" % off[0]], off[:1], {off[0]: offe}, lambda b: T.st[big(b), :], lambda b: T.lsh[big(b), :], "ash", "lsh", 5000.0)
     slots = ["sh0", "sh1", "sh2", "sh3"]
 
     def sums(c, bank_, at, xb, start, stop):
         o = 64 * c
-        return [P.matmul(bank_[:, at:at + 64], kh["tri"], xb[:, o:o + 64], start, False),
-                P.matmul(bank_[:, at + 1:at + 64:2], kh["onesb"], xb[:, o:o + 64:2], False, stop)]
+        return [P.matmul(bank_[:, at:at + 64], kb["tri"], xb[:, o:o + 64], start, False),
+                P.matmul(bank_[:, at + 1:at + 64:2], kb["same"], xb[:, o:o + 64:2], False, stop)]
 
     def cast(eng, sem, out, in_, n, reads, writes, kind=None):
         if eng == "G":
@@ -232,28 +242,34 @@ def rank_program(g, core, T, topo):
             keys, n = ["mi" + C, "wh" + C], (2, 4, 2)
             fy = lambda: sums(c, a, 64, T.mi, False, True)
             f0 = lambda: sums(c, b, 128, T.wh, True, False) + sums(c, b, 128, T.mi, False, False)
-            f1 = lambda: [P.matmul(X1, kh["i64h"], T.wh[:, w], True, False), P.matmul(X1, kh["i64h"], T.mi[:, w], False, True)]
+            f1 = lambda: [P.matmul(X1, kb["i64h"], T.wh[:, w], True, False), P.matmul(X1, kb["i64h"], T.mi[:, w], False, True)]
         elif kind == "own":
-            keys, n = ["xo" + C, "tri", "onesb"], (2, 2, 2)
+            keys, n = ["xo" + C, "tri", "same"], (2, 2, 2)
             fy = lambda: sums(c, a, 64, T.xo, True, True)
             f0 = lambda: sums(c, b, 128, T.xo, True, False)
-            f1 = lambda: [shift(), P.matmul(X1, kh["i64h"], T.xo[:, w], False, True)]
+            f1 = lambda: [shift(), P.matmul(X1, kb["i64h"], T.xo[:, w], False, True)]
         else:
             K, lo, up = str(kind), T.wh[:, o:o + 64:2], T.wh[:, o + 1:o + 64:2]
-            keys, n = ["wh" + C, "tp" + K, "op" + K, "pm" + K], (3, 3, 3)
+            keys, n = ["wh" + C, "tp" + K, "op" + K, "pm" + K, "ntri"], (3, 4, 3)
 
             def mixed(bank_, at, stop):
-                return [P.matmul(bank_[:, at:at + 64], kh["tri"], T.wh[:, w], True, False), P.matmul(bank_[:, at:at + 64:2], kh["tp" + K], lo, False, False),
-                        P.matmul(bank_[:, at + 1:at + 64:2], kh["op" + K], lo, False, stop)]
-            fy = lambda: mixed(a, 64, True)
+                return [P.matmul(bank_[:, at:at + 64], kb["tri"], T.wh[:, w], True, False), P.matmul(bank_[:, at:at + 64:2], kb["tp" + K], lo, False, False),
+                        P.matmul(bank_[:, at:at + 64:2], kb["ntri"], lo, False, False), P.matmul(bank_[:, at + 1:at + 64:2], kb["op" + K], lo, False, stop)]
+            fy = lambda: [P.matmul(a[:, 64:128:2], kb["tp" + K], lo, True, True), P.matmul(a[:, 65:128:2], kb["tri"], up, True, False),
+                          P.matmul(a[:, 65:128:2], kb["op" + K], lo, False, True)]
             f0 = lambda: mixed(b, 128, False)
-            f1 = lambda: [shift(), P.matmul(a[:, 128:192:2], kh["pm" + K], lo, False, False), P.matmul(a[:, 129:192:2], kh["i64h"], up, False, True)]
+            f1 = lambda: [shift(), P.matmul(a[:, 128:192:2], kb["pm" + K], lo, False, False), P.matmul(a[:, 129:192:2], kb["i64h"], up, False, True)]
+        was = now[0]
+        if kind != "mask" or flip:
+            now[0] = was - c * CFG["KAP"]
         add("P", "px" + C, fy, keys, (), ak, dur=pe(n[0]), n=n[0])
         add("P", "pv" + C, f0, keys, (), bk, dur=pe(n[1]), n=n[1])
-        if CFG["YE"] == "V":
-            add("V", "y" + C, lambda: [V.tensor_scalar(T.y[:, w], XY, bb[:, j:j + 1], None, OP.add)], bkeys, ["y" + C], ak, dur=vd(64))
+        if flip and c == 0:
+            add("V", "y" + C, lambda: [V.tensor_scalar(T.y[:, w], XY, acol, T.bf[:, j:j + 1], OP.add, OP.add)], ["b4a"], ["y" + C], ak + ["pb%d" % (NC - 1)],
+                dur=vd(64))
+            after_sum()
         else:
-            add("S", "y" + C, lambda: [S.activation(T.y[:, w], XY, AF.Identity, bias=bb[:, j:j + 1])], bkeys, ["y" + C], ak, dur=sd(64))
+            add("V", "y" + C, lambda: [V.tensor_scalar(T.y[:, w], XY, bb[:, j:j + 1], None, OP.add)], bkeys, ["y" + C], ak, dur=vd(64))
         add("P", "py" + C, lambda: [P.matmul(X0, kb["ineg"], T.y[:, w], False, True)], ["y" + C, "ineg"], (), bk, dur=pe(1))
         add("P", "pw" + C, f1, keys + ["cl", "cr0", "i64h"], (), ak, dur=pe(n[2]), n=n[2], kind="pz")
         add("S", "sq" + C, lambda: [S.activation(T.sq[:, w], X0, AF.Square, bias=bb[:, j + 1:j + 2])], bkeys, ["sq" + C], bk, dur=sd(64))
@@ -261,6 +277,7 @@ def rank_program(g, core, T, topo):
         add("V", "sf" + C, lambda: [V.tensor_scalar(T.sf[:, w], T.t3[:, w], 6, 4095, OP.arith_shift_right, OP.bitwise_and)], ["t3" + C], ["sf" + C],
             dur=vd(64))
         cast(ofe, "of" + C, T.of[:, w], T.sf[:, w], 64, ["sf" + C], ["of" + C])
+        now[0] = was
 
         def gather(eng, sem, a, z):
             out, src = T.ga[:, v + 32 * a:v + 32 * z], shelf[:, :].indirect(T.of[:, o + 2 * a:o + 2 * z])
@@ -298,8 +315,8 @@ def rank_program(g, core, T, topo):
         spread(c, measure(c, "own", T.sh0, ["sh0"], T.b4, ["b0", "b1"], CFG["A%d" % c], CFG["CUT"] if c == NC - 1 else 0, "V"))
 
     iota("row8", T.row8[:, :], [[1, 8]], 0, 0, 8)
-    iota("neg", T.num[0:1, 0:256], [[0, 2], [-1, 128]], 0, 0, 256)
-    iota("pos", T.num[0:1, 256:512], [[0, 2], [1, 128]], 0, 0, 256)
+    mo = 128 * B16M.index("mrow")
+    const("S", lambda: S.activation(T.neg[0:1, :], T.kb[0:1, mo:mo + 256], AF.Identity, scale=-1.0), ["mrow"], "neg", sd(256))
     sgn = [-1 if low(k, 0) else 1 for k in (0, 1)]
     iota("sg80", T.sg8[0:1, 0:8], [[-2 * sgn[0], 2], [0, 4]], sgn[0], 0, 8)
     ms("ones", kb["ones"], 1.0, 128)
@@ -309,23 +326,20 @@ def rank_program(g, core, T, topo):
     ts("r2", T.r2[:, :], T.row8[:, :], "row8 ps", cf["ps"], OP.is_equal, 128.0, OP.mult, n=8)
     for s in range(8):
         sc("lk%d" % s, kb["lk%d" % s], kb["ones"], "ones ind", T.ind[:, s:s + 1])
-    sc("sameb", kb["sameb"], kf["same"], "same", 1.0)
+    sc("ntri", kb["ntri"], kb["tri"], "tri", -1.0)
     tc("fc", "ps", "", float(SFROM), OP.is_ge)
     tc("ad0", "fc", "", 127.0, OP.mult)
     tc("ad1", "fc", "", 127.0, OP.mult, 1.0, OP.add)
     tc("ad2", "fc", "", 63.5, OP.mult)
-    ms("win", T.win[:, 0:256], 0.0, 512)
-    ms("winq", T.win[:, 256:384], 0.0, 256)
-    diag("idf", kf["idf"], 1.0)
-    diag("idd", kh["idd"], 1.0)
     tc("k5i", "pc", "", 5, OP.arith_shift_right)
-    tc("k5", "k5i", "", 1.0, OP.mult)
+    tc("sai", "psi", "", 1, OP.bitwise_and)
+    tc("sa", "sai", "", 1.0, OP.mult)
+    tc("kv", "k5i", "sa", cf["sa"], OP.subtract, 0.5, OP.mult)
     tc("u5i", "pc", "", 31, OP.bitwise_and)
     tc("u5", "u5i", "", 1.0, OP.mult)
     iota("urow", T.urow[:, :], [[1, 32], [0, 2]], 0, 0, 64)
-    for t in range(2, 6):
-        h = HS[t - 1]
-        iota("br%d" % t, kb["br%d" % t], [[0, 64 // h], [2, 2]] + ([[0, h]] if h > 1 else []), -1, 0, 128)
+    iota("win", T.win[:, 0:256], [[0, 256]], 0, 0, 256)
+    iota("winq", T.win[:, 256:384], [[0, 128]], 0, 0, 128)
     ts("del", T["del"][:, :], T.urow[:, :], "urow u5", cf["u5"], OP.is_equal, n=64)
     ms("pat", T.pat[:, :], -1.0, 132)
     ts("pat", T.pat[:, 0:64], T["del"][:, :], "del", -1.0, OP.mult, n=32)
@@ -343,7 +357,8 @@ def rank_program(g, core, T, topo):
     ts("bf", T.bf[:, :], T.bi[:, :], bik, -4096.0, OP.mult, n=4)
     tt("dc", T.dc[:, 0:4], T.cum[:, 0:4], T.bf[:, :], "cum bf", OP.add, n=8)
     for t in range(1, 5):
-        sc("dg%d" % t, kb["dg%d" % t], kf["idf"], "idf dc", T.dc[:, t - 1:t])
+        sc("dg%d" % t, kb["dg%d" % t], kb["idd"], "idd dc", T.dc[:, t - 1:t])
+    ts("wc", T.wc[:, :], T.bi[:, :], bik, -8192.0, OP.mult, 4096.0, OP.add, n=4)
 
     def round_consts(k):
         K, m = str(k), MS[k]
@@ -355,35 +370,35 @@ def rank_program(g, core, T, topo):
         tc("s2_" + K, "lam" + K, "fc", -2.0, OP.add, cf["fc"], OP.mult)
         tc("s1_" + K, "s2_" + K, "", 2.0, OP.add, 0.5, OP.mult)
         tc("s2_" + K, "s2_" + K, "", 2.0, OP.add)
-        ts("pm" + K, kh["pm" + K], kf["mrow"], "mrow px" + K, cf["px" + K], OP.is_equal, 64.0, OP.mult)
-        ts("op" + K, kh["op" + K], kf["sm"], "sm psx" + K, cf["psx" + K], OP.is_equal)
-        tt("tmp", kf["tmp"], kh["op" + K], kf["same"], "same op" + K, OP.subtract)
-        tt("tp" + K, kh["tp" + K], kf["tmp"], kf["le"], "le tmp", OP.mult)
-        ts("tmp", kf["tmp"], kf["mrow"], "mrow px" + K, cf["px" + K], OP.is_equal)
-        tt("dm" + K, kh["dm" + K], kf["tmp"], kf["idf"], "idf tmp", OP.subtract)
+        hit("pm" + K, "mrow", "px" + K, 64.0)
+        hit("dm" + K, "mrow", "px" + K, 1.0)
+        hit("op" + K, "sm", "psx" + K, 1.0)
+        tt("tp" + K, kb["tp" + K], kb["op" + K], kb["le"], "le op" + K, OP.mult)
         if k == 0:
-            tc("sai", "psi", "", 3, OP.bitwise_and)
-            tc("spc0", "sai", "", 1.0, OP.mult)
-            iota("spr0", kb["spr0"], [[0, 2], [1, 4], [0, 16]], 0, 0, 128)
-            iota("lr0", kb["lr0"], [[-2 * sgn[0], 2], [0, 64]], sgn[0], 0, 128)
+            tc("sbi", "psi", "", 3, OP.bitwise_and)
+            tc("spc0", "sbi", "", 1.0, OP.mult)
+            iota("rb0", kb["rb0"], [[0, 2], [1, 2], [0, 32]], 0, 0, 128)
         else:
-            tc("sai", "psi", "", 1, OP.bitwise_and)
-            tc("sa", "sai", "", 1.0, OP.mult)
             tc("spc1", "bit0", "sa", 2.0, OP.mult, cf["sa"], OP.add)
-            for a in (0, 1):
-                iota("spr1", part(T.kb, B16M, "spr1", 64 * a, 64 * a + 64), [[0, 2], [1, 2], [0, 16]], 2 * a, 0, 64)
-            iota("lr1", kb["lr1"], [[0, 2], [-2 * sgn[1], 2], [0, 32]], sgn[1], 0, 128)
+            iota("rb1", kb["rb1"], [[1, 2], [0, 64]], 0, 0, 128)
             iota("sg81", T.sg8[0:1, 8:16], [[0, 2], [-2 * sgn[1], 2], [0, 2]], sgn[1], 0, 8)
         ts("wsp" + K, T.wsp[:, 8 * k:8 * k + 4], T.row8[:, 0:4], "row8 spc%s lam%s" % (K, K), cf["spc" + K], OP.is_equal, cf["lam" + K], OP.mult, n=4)
         ts("wsn" + K, T.wsp[:, 8 * k + 4:8 * k + 8], T.wsp[:, 8 * k:8 * k + 4], "wsp" + K, -1.0, OP.mult, n=4)
-        w1 = "w%d_1" % k
-        ts(w1, kb[w1], kb["spr" + K], "k5 spr" + K, cf["k5"], OP.is_equal, -4096.0, OP.mult, n=64)
-        for t in range(2, 7):
-            row = "br%d" % t if t < 6 else "lr" + K
-            tt("w%d_%d" % (k, t), kb["w%d_%d" % (k, t)], kb[w1], kb[row], w1 + " " + row, OP.mult)
+        x = "x" + K
+        hit(x, "rb" + K, "kv", 1.0)
+        sc("xw1", T.xw[:, 0:128], kb[x], x, -4096.0)
+        for t in range(2, 6):
+            sc("xw%d" % t, T.xw[:, 128 * t - 128:128 * t], kb[x], x + " wc", T.wc[:, t - 2:t - 1])
+        for b in range(4):
+            sc("xw6%d" % b, T.xw[:, 640 + 32 * b:672 + 32 * b], block(x, b), x, 4096.0 if low(k, b) else -4096.0)
+        for t, keys in ((1, "xw1 xw2 xw3"), (4, "xw4 xw5 xw60 xw61 xw62 xw63")):
+            const("V", (lambda t: lambda: V.transpose(part(T.kb, B16M, "w%d_%d" % (k, t), 0, 384), T.xw[:, 128 * t - 128:128 * t + 256]))(t), keys.split(),
+                  "w%d_%d" % (k, t), vd(192))
+            for u in (t + 1, t + 2):
+                lastw["w%d_%d" % (k, u)] = len(tasks) - 1
         tc("d5_" + K, "lam" + K, "cum", -2048.0, OP.mult, T.cum[:, 4:5], OP.add)
         tc("d5_" + K, "d5_" + K, "", -2048.0, OP.add)
-        sc("dg%d" % (5 + k), kb["dg%d" % (5 + k)], kf["idf"], "idf d5_" + K, cf["d5_" + K])
+        sc("dg%d" % (5 + k), kb["dg%d" % (5 + k)], kb["idd"], "idd d5_" + K, cf["d5_" + K])
     round_consts(0)
     tc("s32", "s1_0", "", 32.0, OP.mult)
     tc("ad3", "ad2", "", 32.0, OP.mult, 31.0, OP.add)
@@ -392,32 +407,38 @@ def rank_program(g, core, T, topo):
     i = send(dkeys, (1, 2, 3), eng_of, lambda b: T.dd[:, :], lambda b: T.dl[:, big(b)], "ad", "dl", CFG["LATD"], True)
     left = add("R", "lod", None, (), ["left"], dur=0.0, n=0, extra=[i])
     send(["st%d" % off[1], "st%d" % near[0]], off[1:] + near, {off[1]: offe, near[0]: neare}, lambda b: T.st[big(b), :], lambda b: T.lsh[big(b), :],
-         "ash", "lsh", 5000.0, True, i)
+         "ash", "lsh", CFG["LATS"], True, i)
     for b, key in ((off[0], "lsh"), (near[0], "lshn"), (off[1], "lshf")):
         add("Y", "dbo", (lambda b: lambda: [Y.dma_start(T.sh0[rows(b), :], T.lsh[big(b), :])])(b), [key, "left"], ["sh%d" % b], dur=100, lat=2500, inc=16)
-    add("P", "pq", lambda: [P.matmul(T.pa0[rows(b), 128 * e:128 * e + 128], part(T.kh, H16M, "idd", 32 * b, 32 * b + 32),
-                                     (T.lx[:, 256 * b + e:256 * b + 256:2] if b else T.xo[:, e:256:2]), True, True) for b in range(4) for e in (0, 1)],
-        ["lx", "idd"] + xok, (), ["pa0"], dur=pe(16), n=8)
+    add("P", "pq", lambda: [P.matmul(T.pa0[rows(0), 128 * e:128 * e + 128], block("idd", 0), T.xo[:, e:256:2], True, True) for e in (0, 1)]
+        + [P.matmul(T.pa0[rows(b), 128 * e + 32 * a:128 * e + 32 * a + 32], block("idd", a), T.lx[:, 64 * b - 64 + e:64 * b:2], True, True)
+           for b in (1, 2, 3) for a in range(4) for e in (0, 1)], ["lx", "idd"] + xok, (), ["pa0"], dur=pe(18), n=26)
     add("S", "sq_", lambda: [S.activation(T.src[:, 0:256], T.pa0[:, 0:256], AF.Copy)], (), ["srcA", "srcB"], ["pa0"], dur=sd(256))
 
     keyrow = ["pa0", "pa1", "pb1", "pb2"]
-    keycol = ["pa2", "pb3", "pa2", "pb0"]
 
     def order(k):
-        K, po, cnt = str(k), 24 * k, T.pa3[:, 448:456]
+        K, po, cb = str(k), 24 * k, "pa3" if k else "pa2"
+        cnt = T[cb][:, 448:456]
         dq = [T.dd[:, :] if b == 0 or k else T.dl[:, big(b)] for b in range(4)]
         dk = [["du"] if k else (["dln" if b in near else "dlf"] if b else dkeys) for b in range(4)]
-        add("P", "pk", lambda: [P.matmul(T[keyrow[b]][:, 256:512], onesrow, T.num[0:1, (0 if low(k, b) else 256):(256 if low(k, b) else 512)], True, False)
-                                for b in range(4)], ["neg", "pos", "ones"], (), keyrow, dur=pe(16), n=4)
+        keycol = ["pa2", "pa2", "pa2", "pb0"] if k else ["pa2", "pb3", "pa3", "pb0"]
+        spans = ((0, 3), (3, 4)) if k else ((0, 1), (1, 2), (2, 3), (3, 4))
+        add("P", "pk", lambda: [P.matmul(T[keyrow[b]][:, 256:512], onesrow, T.neg[0:1, :] if low(k, b) else T.kb[0:1, mo:mo + 256], True, False)
+                                for b in range(4)]
+            + [P.matmul(T[keycol[a]][:, 384 + 2 * a:384 + 2 * z], T.kb[0:1, mo:mo + 128], T.sg8[0:1, 8 * k + 2 * a:8 * k + 2 * z], True, False) for a, z in spans],
+            ["neg", "ones", "sg8" + K], (), keyrow + [keycol[a] for a, _ in spans], dur=pe(16 + len(spans)), n=4 + len(spans))
+
+        def column(a, z):
+            col = T[keycol[a]][:, 384 + 2 * a:384 + 2 * z]
+            add("P", "pc_%d" % a, lambda: [P.matmul(col, dq[a], T.r2[:, 2 * a:2 * z], False, True)], dk[a] + ["r2"], (), [keycol[a]], dur=pe(1))
+            if a == 3:
+                add("S", "kc", lambda: [S.activation(T.kc[:, :], col, AF.Copy)], (), ["kc"], [keycol[a]], dur=sd(2))
+            return len(tasks) - (2 if a == 3 else 1)
 
         def keys(b):
-            B, row, col = str(b), T[keyrow[b]], T[keycol[b]][:, 384 + 2 * b:386 + 2 * b]
-            add("P", "pc_" + B, lambda: [P.matmul(col, T.num[0:1, 256:384], T.sg8[0:1, 8 * k + 2 * b:8 * k + 2 * b + 2], True, False),
-                                         P.matmul(col, dq[b], T.r2[:, 2 * b:2 * b + 2], False, True)],
-                dk[b] + ["pos", "sg8" + K, "r2"], (), [keycol[b]], dur=pe(2), n=2)
-            if b == 3:
-                add("S", "kc", lambda: [S.activation(T.kc[:, :], col, AF.Copy)], (), ["kc"], [keycol[b]], dur=sd(2))
-            add("P", "pr" + B, lambda: [P.matmul(row[:, 256 + 128 * j:384 + 128 * j], kb["lk%d" % (2 * b + j)], dq[b], False, j == 1) for j in (0, 1)],
+            B, row = str(b), T[keyrow[b]]
+            return add("P", "pr" + B, lambda: [P.matmul(row[:, 256 + 128 * j:384 + 128 * j], kb["lk%d" % (2 * b + j)], dq[b], False, j == 1) for j in (0, 1)],
                 dk[b] + ["lk%d" % (2 * b), "lk%d" % (2 * b + 1)], (), [keyrow[b]], dur=pe(4), n=2)
 
         def compare(b):
@@ -430,31 +451,29 @@ def rank_program(g, core, T, topo):
                 add("V", "cv" + B, lambda: [V.tensor_scalar(out, src, col[:, 384 + 2 * b + j:385 + 2 * b + j], None, OP.is_lt if low(k, b) else OP.is_gt)
                                             for j, (out, src) in enumerate(io_)], (), ["cc" + B], [keyrow[b], keycol[b]], dur=2 * vd(128), n=2)
 
-        def counted(b):
-            add("P", "pl", lambda: [P.matmul(T.pa3[rows(b), 448 + j:449 + j], T.cc[:, j, 32 * b:32 * b + 32], ones1, True, True) for j in range(8)],
-                ["cc%d" % b, "ones"], (), ["pa3"], dur=pe(4.6), n=8)
-        turns = (0, 3, 1, 2) if k else (0, 1, 3, 2)
-        for b in turns[:3]:
-            keys(b)
-        compare(0)
-        keys(2)
-        for b in (1, 3, 2):
-            compare(b)
+        if k:
+            turn_ = [column(3, 4), column(0, 3), keys(0), keys(3), keys(1), keys(2)]
+        else:
+            turn_ = [column(0, 1), keys(0), column(1, 2), keys(1), column(3, 4), column(2, 3), keys(2), keys(3)]
+        for a, z in zip(turn_, turn_[1:]):
+            tasks[z]["soft"].add(a)
         for b in (0, 1, 3, 2):
-            counted(b)
+            compare(b)
+        add("P", "pl", lambda: [P.matmul(T[cb][:, 448 + j:449 + j], T.cc[:, j, :], ones1, True, True) for j in range(8)],
+            ["cc0", "cc1", "cc2", "cc3", "ones"], (), [cb], dur=pe(8), n=8)
         qr = T.pb0[:, 256:384]
         if k:
-            add("P", "pq", lambda: [P.matmul(qr, kb["sameb"], T.dd[:, :], True, True)], ["du", "sameb"], (), ["pb0"], dur=pe(2))
+            add("P", "pq", lambda: [P.matmul(qr, kb["same"], T.dd[:, :], True, True)], ["du"], (), ["pb0"], dur=pe(2))
         else:
-            add("P", "pq", lambda: [P.matmul(T.pb0[rows(b), 256:384], part(T.kb, B16M, "sameb", 32 * b, 32 * b + 32), dq[b], True, True) for b in range(4)],
-                dkeys + ["dln", "dlf", "sameb"], (), ["pb0"], dur=pe(8), n=4)
+            add("P", "pq", lambda: [P.matmul(T.pb0[rows(b), 256:384], block("same", b), dq[b], True, True) for b in range(4)],
+                dkeys + ["dln", "dlf"], (), ["pb0"], dur=pe(8), n=4)
         add("S", "sq_", lambda: [S.activation(T.src[:, 256:384], qr, AF.Identity, bias=-2048.0)], (), ["srcq"], ["pb0"], dur=sd(128))
         if k:
             add("S", "sq_", lambda: [S.activation(T.qo[:, 0:128], qr, AF.Copy)], (), ["qo"], ["pb0"], dur=sd(128))
 
         def lists(sem, key, out, ab):
             add("V", sem, lambda: [V.tensor_scalar(out(j), cnt, cf[a], cf[b], OP.mult, OP.add) for j, (a, b) in enumerate(ab)],
-                [x for y in ab for x in y], [key], ["pa3"], dur=len(ab) * vd(8), n=len(ab))
+                [x for y in ab for x in y], [key], [cb], dur=len(ab) * vd(8), n=len(ab))
         both = [("s2_" + K, "ad0"), ("s2_" + K, "ad1")]
         lists("po", "po" + K, lambda j: T.po[:, po + 8 * j:po + 8 * j + 8], both)
         add("V", "scat", lambda: [V.tensor_copy(T.win[:, 0:256].indirect(T.po[:, po:po + 16]), T.src[:, 0:256])], ["po" + K, "srcA", "srcB"], ["win"],
@@ -464,7 +483,7 @@ def rank_program(g, core, T, topo):
         lists("poq", "poq" + K, lambda j: T.po[:, po + 16:po + 24], [("s1_" + K, "ad2")])
         add("V", "scq", lambda: [V.tensor_copy(T.win[:, 256:384].indirect(T.po[:, po + 16:po + 24]), T.src[:, 256:384])], ["poq" + K, "srcq"], ["winq"],
             dur=50 + vd(128, 3.5))
-        cast("G", "scq", T.wh[:, 256:384], T.win[:, 256:384], 128, ["winq"], ["whq"])
+        cast(CFG["VQ"], "scq", T.wh[:, 256:384], T.win[:, 256:384], 128, ["winq"], ["whq"])
         if k:
             lists("poq", "qp", lambda j: T.qo[:, 128 + 8 * j:136 + 8 * j], both)
         else:
@@ -484,9 +503,10 @@ def rank_program(g, core, T, topo):
         a, bk, o, W, C, K = T["pa%d" % c], ["pa%d" % c], 64 * c, T.wh, str(c), str(k)
         w = slice(o, o + 64)
         add("P", "pw" + C, lambda: [half(a[:, 2:3])] + pairs(2, c, W[:, 256 + 32 * c:288 + 32 * c], 8 * k, True)
-            + [P.matmul(a[:, 192:256], T.cl[0:1, :], T.cr[0:1, 128:192], True, False), P.matmul(a[:, 192:256], kh["dm" + K], W[:, w], False, True),
-               P.matmul(a[:, 256:320], kh["dm" + K], W[:, w], True, True), P.matmul(a[:, 320:384], kh["idd"], W[:, w], True, True)],
-            ["wh" + C, "whq", "dm" + K, "cr2", "cr3", "wsp" + K, "idd"], (), bk, dur=pe(7.2), n=9, kind="-")
+            + [P.matmul(a[:, 192:256], T.cl[0:1, :], T.cr[0:1, 128:192], True, False), P.matmul(a[:, 192:256], kb["dm" + K], W[:, w], False, False),
+               P.matmul(a[:, 192:256], kb["ineg"], W[:, w], False, True), P.matmul(a[:, 256:320], kb["dm" + K], W[:, w], True, False),
+               P.matmul(a[:, 256:320], kb["ineg"], W[:, w], False, True), P.matmul(a[:, 320:384], kb["idd"], W[:, w], True, True)],
+            ["wh" + C, "whq", "dm" + K, "cr2", "cr3", "wsp" + K, "idd"], (), bk, dur=pe(9.2), n=11, kind="-")
         add("V", "pt" + C, lambda: [V.tensor_scalar(T.pt[:, 132 * c:132 * c + 132], T.pat[:, :], a[:, 2:3], None, OP.mult),
                                     V.tensor_scalar(T.tk[:, w], T["del"][:, :], a[:, 2:3], -1.0, OP.mult, OP.is_lt)],
             ["pat", "del"], ["pt" + C, "tk" + C], bk, dur=2 * vd(66), n=2)
@@ -524,10 +544,18 @@ def rank_program(g, core, T, topo):
         add("P", "pc" + C, lambda: [P.matmul(G, kb["w%d_%d" % (k, t)], dec(c, t), False, not counts)], ["de%d_%d" % (c, t), "w%d_%d" % (k, t)], (), bk, dur=pe(1))
         if counts:
             total(c, (5,), True)
-            add("V", "nb", lambda: [V.tensor_scalar(T.nb[:, :], T.bf[:, :], acol, None, OP.add)], ["b4a"], ["nb"], bk, dur=vd(4))
         if t < 5 or k == 0:
             add("P", "pw" + C, lambda: sums(c, a, 64, T.wh, True, False), ["wh" + C], (), ak, dur=pe(2), n=2, kind="pw2")
-            add("V", "mi" + C, lambda: [V.tensor_tensor(T.mi[:, w], G, T.ee[:, w], OP.min)], ["ee" + C], ["mi" + C], bk, dur=vd(64))
+            if not counts:
+                masked(c)
+
+    def masked(c):
+        C, w = str(c), slice(64 * c, 64 * c + 64)
+        add("V", "mi" + C, lambda: [V.tensor_tensor(T.mi[:, w], T["pb" + C][:, 0:64], T.ee[:, w], OP.min)], ["ee" + C], ["mi" + C], ["pb" + C], dur=vd(64))
+
+    def after_sum():
+        add("V", "nb", lambda: [V.tensor_scalar(T.nb[:, :], T.bf[:, :], acol, None, OP.add)], ["b4a"], ["nb"], ["pb%d" % (NC - 1)], dur=vd(4))
+        masked(NC - 1)
 
     def taken(c, eng):
         b, C, w = T["pb%d" % c], str(c), slice(64 * c, 64 * c + 64)
@@ -588,11 +616,7 @@ def rank_program(g, core, T, topo):
     hk = nwk + ["ln", "ho"]
     add("S", "un1", lambda: [S.activation(T.ou[:, 0:256:2], T.nw[:, :].indirect(T.ho[:, 0:8]), AF.Identity, bias=2048.0)], hk, ["ouA"], dur=65 + 106 * GR)
     add("V", "un2", lambda: [V.tensor_scalar(T.ou[:, 1:256:2], T.nw[:, :].indirect(T.ho[:, 8:16]), 2048.0, None, OP.add)], hk, ["ouB"], dur=50 + 106 * GR)
-    for j, E in ((0, Y), (1, S)):
-        mine = runs[j::2]
-        if mine:
-            add("YS"[j], "dou", (lambda E, mine: lambda: [E.dma_start(T.yu[b, :], T.ou[a, :]) for a, b in mine])(E, mine), ["ouA", "ouB"], ["yu%d" % j],
-                dur=100 * len(mine), lat=2000, n=len(mine), inc=16)
+    both("dou", lambda a, b: T.yu[b, :], lambda a, b: T.ou[a, :], ["ouA", "ouB"], "yu", 2000)
     return emit(T, dict(V=V, S=S, P=P, G=g, Y=Y), tasks, count)
 
 
@@ -676,7 +700,7 @@ def emit(T, E, tasks, count):
                     break
                 ck = clocks.get(e, {})
                 if e != "R":
-                    for d in sorted(t["deps"], key=lambda d: -st[d]):
+                    for d in sorted(t["deps"], key=lambda d: (-st[d], -d) if tasks[d]["sem"] not in FREE else (-1e12 - d, 0)):
                         sem, val = tasks[d]["sem"], tasks[d]["val"]
                         if ck.get(sem, 0) < val:
                             E[e].wait_ge(T.sem[sem], int(val))

@@ -7,16 +7,16 @@ SHIFT = 53 * 4096.0
 HS = (16, 8, 4, 2, 1)
 MS = (2, 1)
 SFROM = 6
-CFG = dict(US=28, A0=18, A1=29, A2=24, A3=29, B0=26, B1=28, B2=32, B3=32, C0=29, C1=28, C2=27, C3=30, D0=22, D1=24, D2=28, D3=29, CUT=16, MK="V", DC=3,
-           HOME=((0, 2), (2, 4)), VB=2, VD=0, VW=1, GR=1.56, VF=12.0, SFX=65.0, PEC=0.71, WAKE=170.0, ITERS=1, Q=1440.0, N=(0, 12, 33, 44, 70),
-           FIX=((16, 32), (48, 64)), EARLY=11, LATD=3000.0, LATS=5000.0, KAP=0, FIRST=1, RI=800.0, VQ="V",
+CFG = dict(US=28, A0=18, A1=27, A2=26, A3=28, B0=18, B1=32, B2=30, B3=32, C0=29, C1=29, C2=28, C3=30, D0=22, D1=24, D2=30, D3=28, CUT=16, MK="V", DC=3,
+           HOME=((0, 2), (2, 4)), VB=1, VD=2, VW=1, GR=1.56, VF=12.0, SFX=65.0, PEC=0.65, WAKE=200.0, ITERS=2, Q=1440.0, N=(0, 12, 33, 44, 70),
+           FIX=((16, 32), (48, 64)), EARLY=7, LATD=4000.0, LATS=5000.0, KAP=0, FIRST=1, APART=0, AHEAD=4000.0, RI=900.0, RF=2500.0, VQ="G",
            PHI=dict(px=-0.29, y=0.07, pv=0.14, py=0.22, pz=0.31, sq=0.65, t=0.67, sf=0.95, of=1.01, pg=1.61, gb=1.7, ga=1.72, gv=1.98, mx_=2.08, mn_=2.15,
                     mx=2.21, pw=2.64, pd=2.83, mn=2.87, pe=2.94, de=3.12, pc=3.36, pw2=3.44, mi=3.56))
 
 B16M = (["mrow", "mrow2", "sm", "im", "le", "same", "tri", "ntri", "idd", "ineg", "i64h", "ones"] + ["dg%d" % t for t in range(1, 7)]
         + ["lk%d" % s for s in range(8)] + ["w%d_%d" % (k, t) for k in (0, 1) for t in range(1, 7)] + ["ah%d" % t for t in range(1, 6)]
         + [n + k for n in ("pm", "dm", "tp", "op", "rb", "x") for k in "01"])
-COLF = ["pcf", "ps", "pi", "kv", "u5", "fc", "ad0", "ad1", "ad2", "ad3", "s32", "sa"] + [n + k for n in ("mu", "lam", "px", "psx", "spc", "s2_", "s1_", "d5_") for k in "01"]
+COLF = ["pcf", "ps", "pi", "kv", "u5", "fc", "ad0", "ad1", "ad2", "ad3", "ad4", "ad5", "s32", "sa"] + [n + k for n in ("mu", "lam", "px", "psx", "spc", "s2_", "s1_", "d5_") for k in "01"]
 COLI = ["pc", "psi", "ii", "odd", "bit0", "bit1", "k5i", "u5i", "sai", "sbi"]
 SCRATCH = {"cc": ("sbuf", [128, 8, 128], "bfloat16"), "st": ("dram", [512, 1024], "bfloat16"), "lsh": ("dram", [512, 1024], "bfloat16")}
 for _d, _l in (("float32", (("wc", 4), ("cf", len(COLF)), ("row8", 8), ("ind", 8), ("sq", 256), ("md", 256), ("ee", 256), ("ea", 256),
@@ -33,11 +33,12 @@ for _d, _l in (("float32", (("wc", 4), ("cf", len(COLF)), ("row8", 8), ("ind", 8
 for _i in range(4):
     SCRATCH["pa%d" % _i] = ("psum", [128, 512], "float32")
     SCRATCH["pb%d" % _i] = ("psum", [128, 512], "float32")
-LANE = "pw px pv py y sq t sf of ga gb gv mx mn mx_ mn_ pd de pg pc mi pt md".split()
-ONE = ("vk0 vk1 vk2 vk3 sk0 sk1 gk xo kc pk pr0 pr1 pr2 pr3 pc_0 pc_1 pc_2 pc_3 cv0 cv1 cv2 cv3 pq sq_ pl po poq scat scq pA nb un1 un2 ho "
+LANE = "pw px py y sq t sf of ga gb gv mx mn pd de pc mi pt md".split()
+TURNS = {"V": 6, "S": 3, "G": 3}
+ONE = ("vk0 vk1 vk2 vk3 vk4 vk5 sk0 sk1 sk2 gk0 gk1 gk2 xo kc pk pr0 pr1 pr2 pr3 pc_0 pc_1 pc_2 pc_3 cv0 cv1 cv2 cv3 pq sq_ pl po poq scat scq pA nb un1 un2 ho "
        "dun dst0 dst1 dst2 dsh dbo douq dou ax ash ashn ashf adn adf aq al loc lod").split()
 SEMAPHORES = [s + str(c) for s in LANE for c in range(NC)] + ONE
-FREE = ("loc", "dbo", "dou", "dun", "pl", "pd0", "pd1", "pd2", "pd3")
+FREE = ["loc", "dbo", "dou", "dun"] + [s + str(c) for s in ("px", "py", "pd", "pc", "mx", "mn") for c in range(NC)]
 
 
 def vd(n, rate=1.0):
@@ -126,13 +127,13 @@ def rank_program(g, core, T, topo):
 
         def fn():
             tr = []
-            for b in blocks:
+            for b in sorted(blocks, key=lambda b: b in near):
                 rid, pid = topo.addr(cores[b ^ r], core)
                 tr.append(RemoteDMATransfer(dst_ids=[DstId(rid=rid, pnc=pid)], dma_engine_mask=sum(1 << e for e in engines[b]),
                                             remote_sem=T.sem[sem + tag[b]], src=src_of(b), dst=dst_of(b)))
             g.remote_dma_fused(tr, local_sem=T.sem["lod" if sem == "ad" else "loc"])
             return []
-        i = add("G", "lod" if sem == "ad" else "loc", fn, reads, (), dur=CFG["RI"], lat=1000, n=sum(len(engines[b]) for b in blocks))
+        i = add("G", "lod" if sem == "ad" else "loc", fn, reads, (), dur=CFG["RI"] + (CFG["RF"] if sem == "ax" else 0.0), lat=1000, n=sum(len(engines[b]) for b in blocks))
         if after is not None:
             tasks[i]["soft"].add(after)
         for x in sorted(set(tag.values())):
@@ -158,9 +159,7 @@ def rank_program(g, core, T, topo):
         tasks[-1]["soft"].add(len(tasks) - 2)
 
     def const(eng, fn, reads, key, dur):
-        m = {"V": 4, "S": 2, "G": 1}[eng]
-        turn[eng] = turn.get(eng, 0) + 1
-        i = add(eng, "gk" if eng == "G" else "%sk%d" % (eng.lower(), turn[eng] % m), lambda: [fn()], reads, [key], dur=dur)
+        i = add(eng, eng, lambda: [fn()], reads, [key], dur=dur)
         tasks[i]["spare"] = now[0] > 0
 
     def iota(key, out, pattern, base, cm, n, flag=True):
@@ -263,7 +262,7 @@ def rank_program(g, core, T, topo):
         if kind != "mask" or flip:
             now[0] = was - c * CFG["KAP"]
         add("P", "px" + C, fy, keys, (), ak, dur=pe(n[0]), n=n[0])
-        add("P", "pv" + C, f0, keys, (), bk, dur=pe(n[1]), n=n[1])
+        add("P", "py" + C, f0, keys, (), bk, dur=pe(n[1]), n=n[1], kind="pv")
         if flip and c == 0:
             add("V", "y" + C, lambda: [V.tensor_scalar(T.y[:, w], XY, acol, T.bf[:, j:j + 1], OP.add, OP.add)], ["b4a"], ["y" + C], ak + ["pb%d" % (NC - 1)],
                 dur=vd(64))
@@ -288,17 +287,17 @@ def rank_program(g, core, T, topo):
             s = slice(v + 32 * a, v + 32 * z)
             both = [(T.mx, T.mmx, OP.max), (T.mn, T.mmn, OP.min)]
             for nm, (buf, mask, op) in zip(("mx", "mn"), both[::-1] if flip else both):
-                add("V", nm + tag + C, (lambda buf, mask, op: lambda: [V.tensor_tensor_scan(buf[:, s], mask[:, 0:32 * (z - a)], T.ga[:, s], 0.0, OP.add, op)])(buf, mask, op),
-                    keys + ["mmx", "mmn"], [nm + tag + C], dur=vd(32 * (z - a), 0.5))
+                add("V", nm + C, (lambda buf, mask, op: lambda: [V.tensor_tensor_scan(buf[:, s], mask[:, 0:32 * (z - a)], T.ga[:, s], 0.0, OP.add, op)])(buf, mask, op),
+                    keys + ["mmx", "mmn"], [nm + tag + C], dur=vd(32 * (z - a), 0.5), kind=nm + tag)
         gv = ["gv" + C] if us < CU else []
         vu = CU - us
         if vu:
             gather("V", "gv", 0, vu)
         if cut:
-            gather("S", "ga", vu, cut)
             gather("S", "gb", cut, CU)
-            scans("", 0, cut, gv + ["ga" + C])
+            gather("S", "ga", vu, cut)
             scans("_", cut, CU, ["gb" + C])
+            scans("", 0, cut, gv + ["ga" + C])
             return ["mx" + C, "mx_" + C], ["mn" + C, "mn_" + C]
         gather("S", "ga", vu, CU)
         scans("", 0, CU, gv + ["ga" + C])
@@ -485,7 +484,7 @@ def rank_program(g, core, T, topo):
             dur=50 + vd(128, 3.5))
         cast(CFG["VQ"], "scq", T.wh[:, 256:384], T.win[:, 256:384], 128, ["winq"], ["whq"])
         if k:
-            lists("poq", "qp", lambda j: T.qo[:, 128 + 8 * j:136 + 8 * j], both)
+            lists("poq", "qp", lambda j: T.qo[:, 128 + 8 * j:136 + 8 * j], [("s2_1", "ad4"), ("s2_1", "ad5")])
         else:
             lists("poq", "pend", lambda j: T.po[:, 48:56], [("s32", "ad3")])
 
@@ -527,11 +526,11 @@ def rank_program(g, core, T, topo):
                          CFG["CUT"], "V" if t == 1 and c < CFG["VB"] else "G")
         if t == 1:
             before(k, c)
-        add("P", "pw" + C, lambda: [half(a[:, 0:1])], ["cr3"], (), ak, dur=pe(1))
+        add("P", "pd" + C, lambda: [half(a[:, 0:1])], ["cr3"], (), ak, dur=pe(1), kind="pw")
         dg = "dg%d" % (t + k if t == 5 else t)
         known = [("w%d_%d" % (k, u), dec(c, u), "de%d_%d" % (c, u)) for u in range(1, t)] + ([("w%d_6" % k, T.tk[:, w], "tk" + C)] if t == 5 else [])
-        add("P", "pg" + C, lambda: [P.matmul(b[:, 0:65], kb[dg], T.one0[:, :], True, False)] + [P.matmul(G, kb[m], d, False, False) for m, d, _ in known],
-            [dg, "one0"] + [x[0] for x in known] + [x[2] for x in known], (), bk, dur=pe(1 + len(known)), n=1 + len(known))
+        add("P", "pc" + C, lambda: [P.matmul(b[:, 0:65], kb[dg], T.one0[:, :], True, False)] + [P.matmul(G, kb[m], d, False, False) for m, d, _ in known],
+            [dg, "one0"] + [x[0] for x in known] + [x[2] for x in known], (), bk, dur=pe(1 + len(known)), n=1 + len(known), kind="pg")
         counts = k == 0 and t == 5 and c == NC - 1
         if counts:
             for d in range(NC):
@@ -545,7 +544,7 @@ def rank_program(g, core, T, topo):
         if counts:
             total(c, (5,), True)
         if t < 5 or k == 0:
-            add("P", "pw" + C, lambda: sums(c, a, 64, T.wh, True, False), ["wh" + C], (), ak, dur=pe(2), n=2, kind="pw2")
+            add("P", "px" + C, lambda: sums(c, a, 64, T.wh, True, False), ["wh" + C], (), ak, dur=pe(2), n=2, kind="pw2")
             if not counts:
                 masked(c)
 
@@ -578,6 +577,8 @@ def rank_program(g, core, T, topo):
     order(0)
     trials(0, T.b4, ["b0", "b1", "b2", "b3"])
     round_consts(1)
+    tc("ad4", "k5i", "ad0", 256.0, OP.mult, cf["ad0"], OP.add)
+    tc("ad5", "k5i", "ad1", 256.0, OP.mult, cf["ad1"], OP.add)
     for t in range(1, 6):
         sc("ah%d" % t, kb["ah%d" % t], kb["w0_1"], "w0_1", HS[t - 1] / 4096.0)
     ts("b4a", T.bf[:, :], T.b4[:, :], "b0 b1 b2 b3 dc", 3968.0, OP.add, n=4)
@@ -603,17 +604,19 @@ def rank_program(g, core, T, topo):
         return T.lq[p, 144 * b + a:144 * b + z] if b else T.qo[p, a:z]
     add("Y", "douq", lambda: [Y.dma_start(T.yq[2 * (b ^ r) + j:2 * (b ^ r) + j + 1, :], home(b, slice(32 * b + 16 * j, 32 * b + 16 * j + 1), 0, 128))
                               for b in range(4) for j in (0, 1)], ["qo", "lq"], ["yq"], dur=800, lat=2000, n=8, inc=16)
-    add("V", "ho", lambda: [V.tensor_scalar(T.ho[rows(b), :], home(b, rows(b), 128, 144), 256.0 * b, None, OP.add) for b in range(4)], ["qp", "lq"], ["ho"],
-        dur=4 * vd(16), n=4)
+    for b in range(4):
+        cast("V", "ho", T.ho[rows(b), :], home(b, rows(b), 128, 144), 16, ["qp", "lq"], ["ho%d" % b])
     trials(1, T.nb, ["nb"])
     for c in range(NC):
         taken(c, "V" if c == NC - 1 else CFG["MK"])
         changed(c)
 
+    i = None
     for a, z in CFG["HOME"]:
-        send(nwk[a:z], (1, 2, 3), eng_of, (lambda a, z: lambda b: T.nw[:, 64 * a:64 * z])(a, z),
-             (lambda a, z: lambda b: T.nw[:, 256 * b + 64 * a:256 * b + 64 * z])(a, z), "al", "ln", 3000.0)
-    hk = nwk + ["ln", "ho"]
+        for bs in ((off, near) if z == NC and CFG["APART"] else ((1, 2, 3),)):
+            i = send(nwk[a:z], bs, eng_of, (lambda a, z: lambda b: T.nw[:, 64 * a:64 * z])(a, z),
+                     (lambda a, z: lambda b: T.nw[:, 256 * b + 64 * a:256 * b + 64 * z])(a, z), "al", "ln", 3000.0, False, i)
+    hk = nwk + ["ln", "ho0", "ho1", "ho2", "ho3"]
     add("S", "un1", lambda: [S.activation(T.ou[:, 0:256:2], T.nw[:, :].indirect(T.ho[:, 0:8]), AF.Identity, bias=2048.0)], hk, ["ouA"], dur=65 + 106 * GR)
     add("V", "un2", lambda: [V.tensor_scalar(T.ou[:, 1:256:2], T.nw[:, :].indirect(T.ho[:, 8:16]), 2048.0, None, OP.add)], hk, ["ouB"], dur=50 + 106 * GR)
     both("dou", lambda a, b: T.yu[b, :], lambda a, b: T.ou[a, :], ["ouA", "ouB"], "yu", 2000)
@@ -657,7 +660,7 @@ def emit(T, E, tasks, count):
         before[tasks[i]["eng"]] = i
     for i, t in enumerate(tasks):
         p = before.get(t["sem"])
-        if p is not None and t["eng"] != "R":
+        if p is not None and t["eng"] != "R" and "spare" not in t:
             if t["sem"] not in FREE:
                 t["deps"].add(p)
             elif tasks[p]["eng"] == t["eng"]:
@@ -670,12 +673,12 @@ def emit(T, E, tasks, count):
     key = [0.0] * n
     for i in range(n - 1, -1, -1):
         t = tasks[i]
-        late = min([key[j] - (wake + t["lat"] if h else 0.0) for j, h in succ[i] if j > i and not tasks[j].get("spare")] or [CFG["N"][4] * CFG["Q"]]) - t["dur"]
+        late = min([key[j] - (wake + t["lat"] if h else 0.0) for j, h in succ[i] if j > i] or [CFG["N"][4] * CFG["Q"]]) - t["dur"]
         key[i] = late if t["plan"] is None else t["plan"]
         if t.get("spare"):
-            key[i] = CFG["EARLY"] * CFG["Q"] + i
-        if t["eng"] == "G" and t["sem"] != "gk":
-            key[i] = min(key[i], key[i] - 3 * CFG["Q"])
+            key[i] = max(key[i] - CFG["AHEAD"], CFG["EARLY"] * CFG["Q"] + 1e-3 * key[i])
+        if t["eng"] == "G" and "spare" not in t:
+            key[i] -= 3 * CFG["Q"]
     st = place(tasks, pred, succ, key, False)
     best = (1e18, None)
     for k in range(CFG["ITERS"] + 1):
@@ -688,6 +691,14 @@ def emit(T, E, tasks, count):
     st, seq = best[1], {}
     for i in sorted(range(n), key=lambda i: (st[i], i)):
         seq.setdefault(tasks[i]["eng"], []).append(i)
+    for e, m in TURNS.items():
+        mine = [i for i in seq[e] if "spare" in tasks[i]]
+        count.pop(e, None)
+        for j, i in enumerate(mine):
+            tasks[i]["sem"], tasks[i]["val"] = "%sk%d" % (e.lower(), j % m), j // m + 1
+            count[tasks[i]["sem"]] = j // m + 1
+            if j >= m:
+                tasks[i]["deps"].add(mine[j - m])
     clocks, after = {e: {} for e in E}, [None] * n
     pos, left = {e: 0 for e in seq}, n
     while left:

from concourse.bass import DstId, RemoteDMATransfer
from concourse.mybir import dt, AluOpType as OP, AxisListType, ActivationFunctionType as AF

NC, CU = 4, 32
BIG = 786432.0
SHIFT = 53 * 4096.0
HS = (16, 8, 4, 2, 1)
MS = (2, 1)
SFROM = 6
CFG = dict(US=28, A0=18, A1=27, A2=26, A3=28, B0=18, B1=32, B2=30, B3=32, C0=29, C1=29, C2=28, C3=30, D0=22, D1=24, D2=30, D3=28, CUT=16, MK="V", DC=3,
           HOME=((0, 2), (2, 4)), VB=1, VD=2, VW=1, GR=1.56, VF=12.0, SFX=65.0, PEC=0.65, WAKE=200.0, ITERS=2, Q=1440.0, N=(0, 12, 33, 44, 70),
           FIX=((16, 32), (48, 64)), EARLY=7, LATD=4000.0, LATS=5000.0, KAP=0, FIRST=1, APART=0, AHEAD=4000.0, RI=900.0, RF=2500.0, VQ="G",
           PHI=dict(px=-0.29, y=0.07, pv=0.14, py=0.22, pz=0.31, sq=0.65, t=0.67, sf=0.95, of=1.01, pg=1.61, gb=1.7, ga=1.72, gv=1.98, mx_=2.08, mn_=2.15,
                    mx=2.21, pw=2.64, pd=2.83, mn=2.87, pe=2.94, de=3.12, pc=3.36, pw2=3.44, mi=3.56))

B16M = (["mrow", "mrow2", "sm", "im", "le", "same", "tri", "ntri", "idd", "ineg", "i64h", "ones"] + ["dg%d" % t for t in range(1, 7)]
        + ["lk%d" % s for s in range(8)] + ["w%d_%d" % (k, t) for k in (0, 1) for t in range(1, 7)] + ["ah%d" % t for t in range(1, 6)]
        + [n + k for n in ("pm", "dm", "tp", "op", "rb", "x") for k in "01"])
COLF = ["pcf", "ps", "pi", "kv", "u5", "fc", "ad0", "ad1", "ad2", "ad3", "ad4", "ad5", "s32", "sa"] + [n + k for n in ("mu", "lam", "px", "psx", "spc", "s2_", "s1_", "d5_") for k in "01"]
COLI = ["pc", "psi", "ii", "odd", "bit0", "bit1", "k5i", "u5i", "sai", "sbi"]
SCRATCH = {"cc": ("sbuf", [128, 8, 128], "bfloat16"), "st": ("dram", [512, 1024], "bfloat16"), "lsh": ("dram", [512, 1024], "bfloat16")}
for _d, _l in (("float32", (("wc", 4), ("cf", len(COLF)), ("row8", 8), ("ind", 8), ("sq", 256), ("md", 256), ("ee", 256), ("ea", 256),
                            ("b4", 4), ("nb", 4), ("bf", 4), ("nf", 5), ("cum", 5), ("dc", 5), ("one5", 5), ("urow", 64),
                            ("nw", 1024), ("kc", 2), ("src", 384), ("win", 384), ("ou", 256), ("qo", 144), ("lq", 576))),
               ("bfloat16", (("kb", 128 * len(B16M)), ("r2", 8), ("neg", 256), ("xw", 768), ("sg8", 16), ("cl", 128), ("cr", 400), ("mmx", 1024), ("mmn", 1024),
                             ("sh0", 4096), ("y", 256), ("ga", 4096), ("mx", 4096), ("mn", 4096), ("mk", 256), ("wsp", 16),
                             ("pat", 132), ("one0", 65), ("del", 64), ("pt", 528), ("tk", 256), ("de", 20 * 66), ("dd", 128), ("ds", 128), ("dl", 512))),
               ("float16", (("xo", 256), ("xs", 192), ("lx", 192), ("mi", 256), ("wh", 384))),
               ("int32", (("ci", len(COLI)), ("bi", 4), ("un0", 256), ("t3", 256), ("sf", 256))),
               ("uint16", (("of", 256), ("po", 56), ("ho", 16)))):
    for _n, _w in _l:
        SCRATCH[_n] = ("sbuf", [128, _w], _d)
for _i in range(4):
    SCRATCH["pa%d" % _i] = ("psum", [128, 512], "float32")
    SCRATCH["pb%d" % _i] = ("psum", [128, 512], "float32")
LANE = "pw px py y sq t sf of ga gb gv mx mn pd de pc mi pt md".split()
TURNS = {"V": 6, "S": 3, "G": 3}
ONE = ("vk0 vk1 vk2 vk3 vk4 vk5 sk0 sk1 sk2 gk0 gk1 gk2 xo kc pk pr0 pr1 pr2 pr3 pc_0 pc_1 pc_2 pc_3 cv0 cv1 cv2 cv3 pq sq_ pl po poq scat scq pA nb un1 un2 ho "
       "dun dst0 dst1 dst2 dsh dbo douq dou ax ash ashn ashf adn adf aq al loc lod").split()
SEMAPHORES = [s + str(c) for s in LANE for c in range(NC)] + ONE
FREE = ["loc", "dbo", "dou", "dun"] + [s + str(c) for s in ("px", "py", "pd", "pc", "mx", "mn") for c in range(NC)]


def vd(n, rate=1.0):
    return max(64.0, n * rate) * 0.83 + CFG["VF"]


def sd(n, rate=1.0):
    return max(64.0, n * rate) * 0.83 + CFG["SFX"]


def pe(n):
    return n * (64 * CFG["PEC"] + 8.0)


def rank_program(g, core, T, topo):
    r = T.rank_of(core)
    if r is None:
        return
    cores = list(T.cores)
    V, S, P, Y = g.vector, g.scalar, g.tensor, g.sync
    GR = CFG["GR"]
    tasks, lastw, readers, bank, count, turn, now = [], {}, {}, {}, {}, {}, [0]

    def add(eng, sem, fn, reads=(), writes=(), banks=(), dur=60.0, lat=0.0, n=1, inc=1, extra=(), kind=None):
        i = len(tasks)
        deps, soft = set(extra), set()
        for k in list(reads) + list(writes):
            if k in lastw:
                deps.add(lastw[k])
            else:
                assert k in writes, k
        for k in writes:
            deps.update(readers.get(k, ()))
        for b in banks:
            st = bank.setdefault(b, {})
            for e in [e for e in st if e != eng]:
                deps.update(st.pop(e))
            if eng in st:
                soft.add(st[eng][-1])
            st.setdefault(eng, []).append(i)
        for k in reads:
            readers.setdefault(k, []).append(i)
        for k in writes:
            lastw[k] = i
            readers[k] = []
        count[sem] = count.get(sem, 0) + n * inc
        kind = kind or sem.rstrip("0123456789")
        plan = (now[0] + CFG["PHI"][kind]) * CFG["Q"] if kind in CFG["PHI"] else None
        tasks.append(dict(eng=eng, sem=sem, val=count[sem], inc=inc, fn=fn, deps=deps, soft=soft - deps, dur=dur, lat=lat, plan=plan,
                          fixed=plan is not None and any(a <= now[0] + CFG["PHI"][kind] < z for a, z in CFG["FIX"])))
        return i

    def mats(buf, names):
        return {n: buf[:, 128 * i:128 * i + 128] for i, n in enumerate(names)}
    kb = mats(T.kb, B16M)
    cf = {n: T.cf[:, i:i + 1] for i, n in enumerate(COLF)}
    ci = {n: T.ci[:, i:i + 1] for i, n in enumerate(COLI)}
    ob = B16M.index("ones") * 128
    ones1, onesrow, ones64 = T.kb[:, ob:ob + 1], T.kb[0:1, ob:ob + 128], T.kb[:, ob:ob + 64]

    def part(buf, names, n, a, b):
        o = 128 * names.index(n)
        return buf[:, o + a:o + b]

    def rows(q):
        return slice(32 * q, 32 * q + 32)

    def big(q):
        return slice(128 * q, 128 * q + 128)

    def low(k, b):
        return ((b ^ r) & MS[k]) == 0

    def far(p, q):
        return (topo.host(cores[p]), topo.chip(cores[p])) != (topo.host(cores[q]), topo.chip(cores[q]))
    off = [b for b in (1, 2, 3) if far(r, b ^ r)]
    near = [b for b in (1, 2, 3) if b not in off]
    offe = topo.engines(core, cores[off[0] ^ r])
    neare = [e for e in topo.engines(core, cores[near[0] ^ r]) if e not in offe]
    share = len(offe) // len(off)
    eng_of = {b: offe[share * j:share * j + share] for j, b in enumerate(off)}
    eng_of[near[0]] = neare

    def send(reads, blocks, engines, src_of, dst_of, sem, key, lat, apart=False, after=None):
        tag = {b: ("n" if b in near else "f") if apart else "" for b in blocks}

        def fn():
            tr = []
            for b in sorted(blocks, key=lambda b: b in near):
                rid, pid = topo.addr(cores[b ^ r], core)
                tr.append(RemoteDMATransfer(dst_ids=[DstId(rid=rid, pnc=pid)], dma_engine_mask=sum(1 << e for e in engines[b]),
                                            remote_sem=T.sem[sem + tag[b]], src=src_of(b), dst=dst_of(b)))
            g.remote_dma_fused(tr, local_sem=T.sem["lod" if sem == "ad" else "loc"])
            return []
        i = add("G", "lod" if sem == "ad" else "loc", fn, reads, (), dur=CFG["RI"] + (CFG["RF"] if sem == "ax" else 0.0), lat=1000, n=sum(len(engines[b]) for b in blocks))
        if after is not None:
            tasks[i]["soft"].add(after)
        for x in sorted(set(tag.values())):
            add("R", sem + x, None, (), [key + x], dur=0.0, lat=lat - (1000.0 if x == "n" else 0.0), n=sum(len(engines[b]) for b in blocks if tag[b] == x),
                extra=[i])
        return i

    span = 128 if r == 0 else 32 * (r & -r)
    runs = [(slice(p, p + span), slice(p ^ (32 * r), (p ^ (32 * r)) + span)) for p in range(0, 128, span)]
    def both(sem, out, in_, reads, key, lat):
        for E, e, mine in ((S, "S", runs[0::2]), (Y, "Y", runs[1::2])):
            if mine:
                add(e, sem, (lambda E, mine: lambda: [E.dma_start(out(a, b), in_(a, b)) for a, b in mine])(E, mine), reads, [key + e],
                    dur=100 * len(mine), lat=lat, n=len(mine), inc=16)
        return [key + e for e in "SY"[:len(runs)]]
    unk = both("dun", lambda a, b: T.un0[a, :], lambda a, b: T.units[b, :], (), "un0", 2000)

    add("Y", "dsh", lambda: [Y.dma_start(T.sh0[a, :], T.shelf[b, :]) for a, b in runs], (), ["sh0"], dur=100 * len(runs), lat=6000, n=len(runs), inc=16)
    tasks[-1]["soft"].add(len(tasks) - 2)
    for j, b in enumerate(off + near):
        add("Y", "dst%d" % j, (lambda b: lambda: [Y.dma_start(T.st[big(b), :], T.shelf[rows(b ^ r), :])])(b), ["sh0"] if j >= CFG["FIRST"] else [],
            ["st%d" % b], dur=100, lat=2500 if j >= CFG["FIRST"] else 7500, inc=16)
        tasks[-1]["soft"].add(len(tasks) - 2)

    def const(eng, fn, reads, key, dur):
        i = add(eng, eng, lambda: [fn()], reads, [key], dur=dur)
        tasks[i]["spare"] = now[0] > 0

    def iota(key, out, pattern, base, cm, n, flag=True):
        kw = dict(allow_small_or_imprecise_dtypes=True) if flag else {}
        const("G", lambda: g.iota(out, pattern, base, cm, **kw), [], key, 130 + 1.66 * n)

    def ts(key, out, in0, rk, s1, op0, s2=None, op1=None, n=128):
        a = (out, in0, s1, None, op0) if op1 is None else (out, in0, s1, s2, op0, op1)
        const("V", lambda: V.tensor_scalar(*a), rk.split(), key, vd(n))

    def tc(name, in0, rk, *a):
        ts(name, cf[name] if name in cf else ci[name], (cf[in0] if in0 in cf else ci[in0]), in0 + " " + rk, *a, n=1)

    def tt(key, out, a, b, rk, op, n=256):
        const("V", lambda: V.tensor_tensor(out, a, b, op), rk.split(), key, vd(n))

    def ms(key, ap, v, n):
        const("V", lambda: V.memset(ap, v), [], key, vd(n, 0.5))

    def sc(key, out, in0, rk, scale):
        const("S", lambda: S.activation(out, in0, AF.Identity, scale=scale), rk.split(), key, sd(128))

    def hit(name, row, col, v, op=OP.is_equal):
        ts(name, kb[name], kb[row], row + " " + col, cf[col], op, v, OP.mult, n=64)
    iota("pc", ci["pc"], [[0, 1]], 0, 1, 1, False)
    iota("sm", kb["sm"], [[1, 8], [0, 16]], 0, 0, 128)
    iota("im", kb["im"], [[0, 8], [1, 16]], 0, 0, 128)
    iota("mrow", part(T.kb, B16M, "mrow", 0, 256), [[0, 2], [1, 128]], 0, 0, 256)
    ms("cl", T.cl[:, :], -512.0, 128)
    for j, v in ((0, 256.0), (2, -4.0), (3, 2.0 ** -10)):
        ms("cr%d" % j, T.cr[:, 64 * j:64 * j + 64], v, 64)
    tc("pcf", "pc", "", 1.0, OP.mult)
    tc("psi", "pc", "", 4, OP.arith_shift_right)
    tc("ii", "pc", "", 15, OP.bitwise_and)
    tc("odd", "pc", "", 1, OP.bitwise_and)
    tc("ps", "psi", "", 1.0, OP.mult)
    tc("pi", "ii", "", 1.0, OP.mult)
    ts("b0", T.b4[:, 0:1], ci["odd"], "odd", -2048.0, OP.mult, BIG + 0.5, OP.add, n=1)
    ts("b1", T.b4[:, 1:2], ci["odd"], "odd", -2048.0, OP.mult, BIG + 2048.0, OP.add, n=1)
    hit("same", "sm", "ps", 1.0)
    hit("le", "im", "pi", 1.0, OP.is_ge)
    tt("tri", kb["tri"], kb["same"], kb["le"], "same le", OP.mult)
    xok = ["xo%d" % c for c in range(NC)]
    add("V", "xo", lambda: [V.tensor_scalar(T.xo[:, :], T.un0[:, :], -2048.0, None, OP.add)], unk, xok, dur=vd(256))
    hit("idd", "mrow", "pcf", 1.0)
    hit("ineg", "mrow", "pcf", -1.0)
    hit("i64h", "mrow", "pcf", 64.0)
    for name, buf, v in (("mmx", T.mmx, -512.0), ("mmn", T.mmn, 512.0)):
        ms(name, buf[:, :], 0.0, 1024)
        ms(name, buf[:, 0:1024:32], v, 32)

    def block(name, b):
        return part(T.kb, B16M, name, 32 * b, 32 * b + 32)

    add("P", "pq", lambda: [P.matmul(T.pb3[rows(a), 192 + 64 * b:256 + 64 * b], block("idd", b), T.xo[:, 64 * a:64 * a + 64], True, True)
                            for b in (1, 2, 3) for a in range(4)], xok + ["idd"], (), ["pb3"], dur=pe(12), n=12)
    add("V", "xo", lambda: [V.tensor_copy(T.xs[:, :], T.pb3[:, 256:448])], (), ["xs"], ["pb3"], dur=vd(192))
    send(["xs"], (1, 2, 3), eng_of, lambda b: T.xs[:, 64 * b - 64:64 * b], lambda b: T.lx[:, 64 * b - 64:64 * b], "ax", "lx", 3000.0)
    send(["st%d" % off[0]], off[:1], {off[0]: offe}, lambda b: T.st[big(b), :], lambda b: T.lsh[big(b), :], "ash", "lsh", 5000.0)
    slots = ["sh0", "sh1", "sh2", "sh3"]

    def sums(c, bank_, at, xb, start, stop):
        o = 64 * c
        return [P.matmul(bank_[:, at:at + 64], kb["tri"], xb[:, o:o + 64], start, False),
                P.matmul(bank_[:, at + 1:at + 64:2], kb["same"], xb[:, o:o + 64:2], False, stop)]

    def cast(eng, sem, out, in_, n, reads, writes, kind=None):
        if eng == "G":
            add("G", sem, lambda: [g.affine_select(out, in_, [[0, n]], OP.is_ge, 0.0, 0, 0)], reads, writes, dur=170 + 1.66 * n, kind=kind)
        else:
            add("V", sem, lambda: [V.tensor_copy(out, in_)], reads, writes, dur=vd(n), kind=kind)

    def measure(c, kind, shelf, skeys, bb, bkeys, us, cut, ofe, flip=False):
        a, b, C, o, v = T["pa%d" % c], T["pb%d" % c], str(c), 64 * c, 1024 * c
        ak, bk, w, j = ["pa" + C], ["pb" + C], slice(o, o + 64), 2 if kind == "mask" else 0
        XY, X1, X0 = a[:, 64:128], a[:, 128:192], b[:, 128:192]
        shift = lambda: P.matmul(X1, T.cl[0:1, :], T.cr[0:1, 0:64], True, False)
        if kind == "mask":
            keys, n = ["mi" + C, "wh" + C], (2, 4, 2)
            fy = lambda: sums(c, a, 64, T.mi, False, True)
            f0 = lambda: sums(c, b, 128, T.wh, True, False) + sums(c, b, 128, T.mi, False, False)
            f1 = lambda: [P.matmul(X1, kb["i64h"], T.wh[:, w], True, False), P.matmul(X1, kb["i64h"], T.mi[:, w], False, True)]
        elif kind == "own":
            keys, n = ["xo" + C, "tri", "same"], (2, 2, 2)
            fy = lambda: sums(c, a, 64, T.xo, True, True)
            f0 = lambda: sums(c, b, 128, T.xo, True, False)
            f1 = lambda: [shift(), P.matmul(X1, kb["i64h"], T.xo[:, w], False, True)]
        else:
            K, lo, up = str(kind), T.wh[:, o:o + 64:2], T.wh[:, o + 1:o + 64:2]
            keys, n = ["wh" + C, "tp" + K, "op" + K, "pm" + K, "ntri"], (3, 4, 3)

            def mixed(bank_, at, stop):
                return [P.matmul(bank_[:, at:at + 64], kb["tri"], T.wh[:, w], True, False), P.matmul(bank_[:, at:at + 64:2], kb["tp" + K], lo, False, False),
                        P.matmul(bank_[:, at:at + 64:2], kb["ntri"], lo, False, False), P.matmul(bank_[:, at + 1:at + 64:2], kb["op" + K], lo, False, stop)]
            fy = lambda: [P.matmul(a[:, 64:128:2], kb["tp" + K], lo, True, True), P.matmul(a[:, 65:128:2], kb["tri"], up, True, False),
                          P.matmul(a[:, 65:128:2], kb["op" + K], lo, False, True)]
            f0 = lambda: mixed(b, 128, False)
            f1 = lambda: [shift(), P.matmul(a[:, 128:192:2], kb["pm" + K], lo, False, False), P.matmul(a[:, 129:192:2], kb["i64h"], up, False, True)]
        was = now[0]
        if kind != "mask" or flip:
            now[0] = was - c * CFG["KAP"]
        add("P", "px" + C, fy, keys, (), ak, dur=pe(n[0]), n=n[0])
        add("P", "py" + C, f0, keys, (), bk, dur=pe(n[1]), n=n[1], kind="pv")
        if flip and c == 0:
            add("V", "y" + C, lambda: [V.tensor_scalar(T.y[:, w], XY, acol, T.bf[:, j:j + 1], OP.add, OP.add)], ["b4a"], ["y" + C], ak + ["pb%d" % (NC - 1)],
                dur=vd(64))
            after_sum()
        else:
            add("V", "y" + C, lambda: [V.tensor_scalar(T.y[:, w], XY, bb[:, j:j + 1], None, OP.add)], bkeys, ["y" + C], ak, dur=vd(64))
        add("P", "py" + C, lambda: [P.matmul(X0, kb["ineg"], T.y[:, w], False, True)], ["y" + C, "ineg"], (), bk, dur=pe(1))
        add("P", "pw" + C, f1, keys + ["cl", "cr0", "i64h"], (), ak, dur=pe(n[2]), n=n[2], kind="pz")
        add("S", "sq" + C, lambda: [S.activation(T.sq[:, w], X0, AF.Square, bias=bb[:, j + 1:j + 2])], bkeys, ["sq" + C], bk, dur=sd(64))
        add("V", "t" + C, lambda: [V.tensor_tensor(T.t3[:, w], T.sq[:, w], X1, OP.add)], ["sq" + C], ["t3" + C], ak, dur=vd(64))
        add("V", "sf" + C, lambda: [V.tensor_scalar(T.sf[:, w], T.t3[:, w], 6, 4095, OP.arith_shift_right, OP.bitwise_and)], ["t3" + C], ["sf" + C],
            dur=vd(64))
        cast(ofe, "of" + C, T.of[:, w], T.sf[:, w], 64, ["sf" + C], ["of" + C])
        now[0] = was

        def gather(eng, sem, a, z):
            out, src = T.ga[:, v + 32 * a:v + 32 * z], shelf[:, :].indirect(T.of[:, o + 2 * a:o + 2 * z])
            add(eng, sem + C, lambda: [S.activation(out, src, AF.Copy) if eng == "S" else V.tensor_copy(out, src)], ["of" + C] + skeys, [sem + C],
                dur=(65 if eng == "S" else 50) + 32 * (z - a) * GR * 0.83)

        def scans(tag, a, z, keys):
            s = slice(v + 32 * a, v + 32 * z)
            both = [(T.mx, T.mmx, OP.max), (T.mn, T.mmn, OP.min)]
            for nm, (buf, mask, op) in zip(("mx", "mn"), both[::-1] if flip else both):
                add("V", nm + C, (lambda buf, mask, op: lambda: [V.tensor_tensor_scan(buf[:, s], mask[:, 0:32 * (z - a)], T.ga[:, s], 0.0, OP.add, op)])(buf, mask, op),
                    keys + ["mmx", "mmn"], [nm + tag + C], dur=vd(32 * (z - a), 0.5), kind=nm + tag)
        gv = ["gv" + C] if us < CU else []
        vu = CU - us
        if vu:
            gather("V", "gv", 0, vu)
        if cut:
            gather("S", "gb", cut, CU)
            gather("S", "ga", vu, cut)
            scans("_", cut, CU, ["gb" + C])
            scans("", 0, cut, gv + ["ga" + C])
            return ["mx" + C, "mx_" + C], ["mn" + C, "mn_" + C]
        gather("S", "ga", vu, CU)
        scans("", 0, CU, gv + ["ga" + C])
        return ["mx" + C], ["mn" + C]

    def ext(buf, c):
        return buf[:, 1024 * c + 31:1024 * c + 1024:32]

    def spread(c, keys):
        add("V", "md%d" % c, lambda: [V.tensor_tensor(T.dd[:, 32 * c:32 * c + 32], ext(T.mx, c), ext(T.mn, c), OP.subtract)],
            keys[0] + keys[1], ["dd" + str(c)], dur=vd(64))
    for c in range(NC):
        now[0] = c
        spread(c, measure(c, "own", T.sh0, ["sh0"], T.b4, ["b0", "b1"], CFG["A%d" % c], CFG["CUT"] if c == NC - 1 else 0, "V"))

    iota("row8", T.row8[:, :], [[1, 8]], 0, 0, 8)
    mo = 128 * B16M.index("mrow")
    const("S", lambda: S.activation(T.neg[0:1, :], T.kb[0:1, mo:mo + 256], AF.Identity, scale=-1.0), ["mrow"], "neg", sd(256))
    sgn = [-1 if low(k, 0) else 1 for k in (0, 1)]
    iota("sg80", T.sg8[0:1, 0:8], [[-2 * sgn[0], 2], [0, 4]], sgn[0], 0, 8)
    ms("ones", kb["ones"], 1.0, 128)
    ms("one0", T.one0[:, :], 1.0, 65)
    ms("one0", T.one0[:, 64:65], 0.0, 1)
    ts("ind", T.ind[:, :], T.row8[:, :], "row8 ps", cf["ps"], OP.is_equal, 128.0, OP.mult, n=8)
    ts("r2", T.r2[:, :], T.row8[:, :], "row8 ps", cf["ps"], OP.is_equal, 128.0, OP.mult, n=8)
    for s in range(8):
        sc("lk%d" % s, kb["lk%d" % s], kb["ones"], "ones ind", T.ind[:, s:s + 1])
    sc("ntri", kb["ntri"], kb["tri"], "tri", -1.0)
    tc("fc", "ps", "", float(SFROM), OP.is_ge)
    tc("ad0", "fc", "", 127.0, OP.mult)
    tc("ad1", "fc", "", 127.0, OP.mult, 1.0, OP.add)
    tc("ad2", "fc", "", 63.5, OP.mult)
    tc("k5i", "pc", "", 5, OP.arith_shift_right)
    tc("sai", "psi", "", 1, OP.bitwise_and)
    tc("sa", "sai", "", 1.0, OP.mult)
    tc("kv", "k5i", "sa", cf["sa"], OP.subtract, 0.5, OP.mult)
    tc("u5i", "pc", "", 31, OP.bitwise_and)
    tc("u5", "u5i", "", 1.0, OP.mult)
    iota("urow", T.urow[:, :], [[1, 32], [0, 2]], 0, 0, 64)
    iota("win", T.win[:, 0:256], [[0, 256]], 0, 0, 256)
    iota("winq", T.win[:, 256:384], [[0, 128]], 0, 0, 128)
    ts("del", T["del"][:, :], T.urow[:, :], "urow u5", cf["u5"], OP.is_equal, n=64)
    ms("pat", T.pat[:, :], -1.0, 132)
    ts("pat", T.pat[:, 0:64], T["del"][:, :], "del", -1.0, OP.mult, n=32)
    ts("pat", T.pat[:, 66:130:2], T["del"][:, 0:64:2], "del", 1.0, OP.mult, n=32)
    ts("pat", T.pat[:, 67:130:2], T["del"][:, 1:64:2], "del", -1.0, OP.mult, n=32)
    ms("b2", T.b4[:, 2:3], BIG + SHIFT - 2047.5, 1)
    ms("b3", T.b4[:, 3:4], BIG + SHIFT, 1)
    for j in range(4):
        ts("bi%d" % j, T.bi[:, j:j + 1], ci["pc"], "pc", 3 - j, OP.arith_shift_right, 1, OP.bitwise_and, n=1)
    bik = " ".join("bi%d" % j for j in range(4))
    ms("nf", T.nf[:, :], 2048.0, 5)
    ts("nf", T.nf[:, 1:5], T.bi[:, :], bik, 4096.0, OP.mult, -4096.0, OP.add, n=4)
    ms("one5", T.one5[:, :], 1.0, 5)
    const("V", lambda: V.tensor_tensor_scan(T.cum[:, :], T.one5[:, :], T.nf[:, :], 0.0, OP.mult, OP.add), ["nf", "one5"], "cum", vd(5))
    ts("bf", T.bf[:, :], T.bi[:, :], bik, -4096.0, OP.mult, n=4)
    tt("dc", T.dc[:, 0:4], T.cum[:, 0:4], T.bf[:, :], "cum bf", OP.add, n=8)
    for t in range(1, 5):
        sc("dg%d" % t, kb["dg%d" % t], kb["idd"], "idd dc", T.dc[:, t - 1:t])
    ts("wc", T.wc[:, :], T.bi[:, :], bik, -8192.0, OP.mult, 4096.0, OP.add, n=4)

    def round_consts(k):
        K, m = str(k), MS[k]
        tc("bit" + K, "pc", "", (6, 5)[k], OP.arith_shift_right, 1, OP.bitwise_and)
        tc("mu" + K, "bit" + K, "", -2.0, OP.mult, 1.0, OP.add)
        tc("lam" + K, "mu" + K, "", float(-sgn[k]), OP.mult)
        tc("px" + K, "mu" + K, "pcf", 32.0 * m, OP.mult, cf["pcf"], OP.add)
        tc("psx" + K, "mu" + K, "ps", 2.0 * m, OP.mult, cf["ps"], OP.add)
        tc("s2_" + K, "lam" + K, "fc", -2.0, OP.add, cf["fc"], OP.mult)
        tc("s1_" + K, "s2_" + K, "", 2.0, OP.add, 0.5, OP.mult)
        tc("s2_" + K, "s2_" + K, "", 2.0, OP.add)
        hit("pm" + K, "mrow", "px" + K, 64.0)
        hit("dm" + K, "mrow", "px" + K, 1.0)
        hit("op" + K, "sm", "psx" + K, 1.0)
        tt("tp" + K, kb["tp" + K], kb["op" + K], kb["le"], "le op" + K, OP.mult)
        if k == 0:
            tc("sbi", "psi", "", 3, OP.bitwise_and)
            tc("spc0", "sbi", "", 1.0, OP.mult)
            iota("rb0", kb["rb0"], [[0, 2], [1, 2], [0, 32]], 0, 0, 128)
        else:
            tc("spc1", "bit0", "sa", 2.0, OP.mult, cf["sa"], OP.add)
            iota("rb1", kb["rb1"], [[1, 2], [0, 64]], 0, 0, 128)
            iota("sg81", T.sg8[0:1, 8:16], [[0, 2], [-2 * sgn[1], 2], [0, 2]], sgn[1], 0, 8)
        ts("wsp" + K, T.wsp[:, 8 * k:8 * k + 4], T.row8[:, 0:4], "row8 spc%s lam%s" % (K, K), cf["spc" + K], OP.is_equal, cf["lam" + K], OP.mult, n=4)
        ts("wsn" + K, T.wsp[:, 8 * k + 4:8 * k + 8], T.wsp[:, 8 * k:8 * k + 4], "wsp" + K, -1.0, OP.mult, n=4)
        x = "x" + K
        hit(x, "rb" + K, "kv", 1.0)
        sc("xw1", T.xw[:, 0:128], kb[x], x, -4096.0)
        for t in range(2, 6):
            sc("xw%d" % t, T.xw[:, 128 * t - 128:128 * t], kb[x], x + " wc", T.wc[:, t - 2:t - 1])
        for b in range(4):
            sc("xw6%d" % b, T.xw[:, 640 + 32 * b:672 + 32 * b], block(x, b), x, 4096.0 if low(k, b) else -4096.0)
        for t, keys in ((1, "xw1 xw2 xw3"), (4, "xw4 xw5 xw60 xw61 xw62 xw63")):
            const("V", (lambda t: lambda: V.transpose(part(T.kb, B16M, "w%d_%d" % (k, t), 0, 384), T.xw[:, 128 * t - 128:128 * t + 256]))(t), keys.split(),
                  "w%d_%d" % (k, t), vd(192))
            for u in (t + 1, t + 2):
                lastw["w%d_%d" % (k, u)] = len(tasks) - 1
        tc("d5_" + K, "lam" + K, "cum", -2048.0, OP.mult, T.cum[:, 4:5], OP.add)
        tc("d5_" + K, "d5_" + K, "", -2048.0, OP.add)
        sc("dg%d" % (5 + k), kb["dg%d" % (5 + k)], kb["idd"], "idd d5_" + K, cf["d5_" + K])
    round_consts(0)
    tc("s32", "s1_0", "", 32.0, OP.mult)
    tc("ad3", "ad2", "", 32.0, OP.mult, 31.0, OP.add)

    dkeys = ["dd%d" % c for c in range(NC)]
    i = send(dkeys, (1, 2, 3), eng_of, lambda b: T.dd[:, :], lambda b: T.dl[:, big(b)], "ad", "dl", CFG["LATD"], True)
    left = add("R", "lod", None, (), ["left"], dur=0.0, n=0, extra=[i])
    send(["st%d" % off[1], "st%d" % near[0]], off[1:] + near, {off[1]: offe, near[0]: neare}, lambda b: T.st[big(b), :], lambda b: T.lsh[big(b), :],
         "ash", "lsh", CFG["LATS"], True, i)
    for b, key in ((off[0], "lsh"), (near[0], "lshn"), (off[1], "lshf")):
        add("Y", "dbo", (lambda b: lambda: [Y.dma_start(T.sh0[rows(b), :], T.lsh[big(b), :])])(b), [key, "left"], ["sh%d" % b], dur=100, lat=2500, inc=16)
    add("P", "pq", lambda: [P.matmul(T.pa0[rows(0), 128 * e:128 * e + 128], block("idd", 0), T.xo[:, e:256:2], True, True) for e in (0, 1)]
        + [P.matmul(T.pa0[rows(b), 128 * e + 32 * a:128 * e + 32 * a + 32], block("idd", a), T.lx[:, 64 * b - 64 + e:64 * b:2], True, True)
           for b in (1, 2, 3) for a in range(4) for e in (0, 1)], ["lx", "idd"] + xok, (), ["pa0"], dur=pe(18), n=26)
    add("S", "sq_", lambda: [S.activation(T.src[:, 0:256], T.pa0[:, 0:256], AF.Copy)], (), ["srcA", "srcB"], ["pa0"], dur=sd(256))

    keyrow = ["pa0", "pa1", "pb1", "pb2"]

    def order(k):
        K, po, cb = str(k), 24 * k, "pa3" if k else "pa2"
        cnt = T[cb][:, 448:456]
        dq = [T.dd[:, :] if b == 0 or k else T.dl[:, big(b)] for b in range(4)]
        dk = [["du"] if k else (["dln" if b in near else "dlf"] if b else dkeys) for b in range(4)]
        keycol = ["pa2", "pa2", "pa2", "pb0"] if k else ["pa2", "pb3", "pa3", "pb0"]
        spans = ((0, 3), (3, 4)) if k else ((0, 1), (1, 2), (2, 3), (3, 4))
        add("P", "pk", lambda: [P.matmul(T[keyrow[b]][:, 256:512], onesrow, T.neg[0:1, :] if low(k, b) else T.kb[0:1, mo:mo + 256], True, False)
                                for b in range(4)]
            + [P.matmul(T[keycol[a]][:, 384 + 2 * a:384 + 2 * z], T.kb[0:1, mo:mo + 128], T.sg8[0:1, 8 * k + 2 * a:8 * k + 2 * z], True, False) for a, z in spans],
            ["neg", "ones", "sg8" + K], (), keyrow + [keycol[a] for a, _ in spans], dur=pe(16 + len(spans)), n=4 + len(spans))

        def column(a, z):
            col = T[keycol[a]][:, 384 + 2 * a:384 + 2 * z]
            add("P", "pc_%d" % a, lambda: [P.matmul(col, dq[a], T.r2[:, 2 * a:2 * z], False, True)], dk[a] + ["r2"], (), [keycol[a]], dur=pe(1))
            if a == 3:
                add("S", "kc", lambda: [S.activation(T.kc[:, :], col, AF.Copy)], (), ["kc"], [keycol[a]], dur=sd(2))
            return len(tasks) - (2 if a == 3 else 1)

        def keys(b):
            B, row = str(b), T[keyrow[b]]
            return add("P", "pr" + B, lambda: [P.matmul(row[:, 256 + 128 * j:384 + 128 * j], kb["lk%d" % (2 * b + j)], dq[b], False, j == 1) for j in (0, 1)],
                dk[b] + ["lk%d" % (2 * b), "lk%d" % (2 * b + 1)], (), [keyrow[b]], dur=pe(4), n=2)

        def compare(b):
            B, row, col = str(b), T[keyrow[b]], T[keycol[b]]
            io_ = [(T.cc[:, :, 32 * b + 16 * j:32 * b + 16 * j + 16], row[:, 256 + 128 * j:384 + 128 * j]) for j in (0, 1)]
            if b == 3:
                add("S", "cv" + B, lambda: [S.activation(out, src, AF.Sign, bias=T.kc[:, j:j + 1], scale=-1.0) for j, (out, src) in enumerate(io_)],
                    ["kc"], ["cc" + B], [keyrow[b]], dur=2 * sd(128), n=2)
            else:
                add("V", "cv" + B, lambda: [V.tensor_scalar(out, src, col[:, 384 + 2 * b + j:385 + 2 * b + j], None, OP.is_lt if low(k, b) else OP.is_gt)
                                            for j, (out, src) in enumerate(io_)], (), ["cc" + B], [keyrow[b], keycol[b]], dur=2 * vd(128), n=2)

        if k:
            turn_ = [column(3, 4), column(0, 3), keys(0), keys(3), keys(1), keys(2)]
        else:
            turn_ = [column(0, 1), keys(0), column(1, 2), keys(1), column(3, 4), column(2, 3), keys(2), keys(3)]
        for a, z in zip(turn_, turn_[1:]):
            tasks[z]["soft"].add(a)
        for b in (0, 1, 3, 2):
            compare(b)
        add("P", "pl", lambda: [P.matmul(T[cb][:, 448 + j:449 + j], T.cc[:, j, :], ones1, True, True) for j in range(8)],
            ["cc0", "cc1", "cc2", "cc3", "ones"], (), [cb], dur=pe(8), n=8)
        qr = T.pb0[:, 256:384]
        if k:
            add("P", "pq", lambda: [P.matmul(qr, kb["same"], T.dd[:, :], True, True)], ["du"], (), ["pb0"], dur=pe(2))
        else:
            add("P", "pq", lambda: [P.matmul(T.pb0[rows(b), 256:384], block("same", b), dq[b], True, True) for b in range(4)],
                dkeys + ["dln", "dlf"], (), ["pb0"], dur=pe(8), n=4)
        add("S", "sq_", lambda: [S.activation(T.src[:, 256:384], qr, AF.Identity, bias=-2048.0)], (), ["srcq"], ["pb0"], dur=sd(128))
        if k:
            add("S", "sq_", lambda: [S.activation(T.qo[:, 0:128], qr, AF.Copy)], (), ["qo"], ["pb0"], dur=sd(128))

        def lists(sem, key, out, ab):
            add("V", sem, lambda: [V.tensor_scalar(out(j), cnt, cf[a], cf[b], OP.mult, OP.add) for j, (a, b) in enumerate(ab)],
                [x for y in ab for x in y], [key], [cb], dur=len(ab) * vd(8), n=len(ab))
        both = [("s2_" + K, "ad0"), ("s2_" + K, "ad1")]
        lists("po", "po" + K, lambda j: T.po[:, po + 8 * j:po + 8 * j + 8], both)
        add("V", "scat", lambda: [V.tensor_copy(T.win[:, 0:256].indirect(T.po[:, po:po + 16]), T.src[:, 0:256])], ["po" + K, "srcA", "srcB"], ["win"],
            dur=50 + vd(256, 3.5))
        for c in range(NC):
            cast("V" if c < CFG["VW"] else "G", "mi%d" % c, T.wh[:, 64 * c:64 * c + 64], T.win[:, 64 * c:64 * c + 64], 64, ["win"], ["wh%d" % c], "-")
        lists("poq", "poq" + K, lambda j: T.po[:, po + 16:po + 24], [("s1_" + K, "ad2")])
        add("V", "scq", lambda: [V.tensor_copy(T.win[:, 256:384].indirect(T.po[:, po + 16:po + 24]), T.src[:, 256:384])], ["poq" + K, "srcq"], ["winq"],
            dur=50 + vd(128, 3.5))
        cast(CFG["VQ"], "scq", T.wh[:, 256:384], T.win[:, 256:384], 128, ["winq"], ["whq"])
        if k:
            lists("poq", "qp", lambda j: T.qo[:, 128 + 8 * j:136 + 8 * j], [("s2_1", "ad4"), ("s2_1", "ad5")])
        else:
            lists("poq", "pend", lambda j: T.po[:, 48:56], [("s32", "ad3")])

    def dec(c, t, a=0, z=64):
        o = 66 * (5 * c + t - 1)
        return T.de[:, o + a:o + z]

    def half(col):
        return P.matmul(col, T.cl[0:1, :], T.cr[0:1, 192:193], True, False)

    def pairs(col, c, data, w, last):
        return [P.matmul(T["pa%d" % c][rows(s), col:col + 1], data, T.wsp[:, w + s:w + s + 1], False, last) for s in range(4)]

    def before(k, c):
        a, bk, o, W, C, K = T["pa%d" % c], ["pa%d" % c], 64 * c, T.wh, str(c), str(k)
        w = slice(o, o + 64)
        add("P", "pw" + C, lambda: [half(a[:, 2:3])] + pairs(2, c, W[:, 256 + 32 * c:288 + 32 * c], 8 * k, True)
            + [P.matmul(a[:, 192:256], T.cl[0:1, :], T.cr[0:1, 128:192], True, False), P.matmul(a[:, 192:256], kb["dm" + K], W[:, w], False, False),
               P.matmul(a[:, 192:256], kb["ineg"], W[:, w], False, True), P.matmul(a[:, 256:320], kb["dm" + K], W[:, w], True, False),
               P.matmul(a[:, 256:320], kb["ineg"], W[:, w], False, True), P.matmul(a[:, 320:384], kb["idd"], W[:, w], True, True)],
            ["wh" + C, "whq", "dm" + K, "cr2", "cr3", "wsp" + K, "idd"], (), bk, dur=pe(9.2), n=11, kind="-")
        add("V", "pt" + C, lambda: [V.tensor_scalar(T.pt[:, 132 * c:132 * c + 132], T.pat[:, :], a[:, 2:3], None, OP.mult),
                                    V.tensor_scalar(T.tk[:, w], T["del"][:, :], a[:, 2:3], -1.0, OP.mult, OP.is_lt)],
            ["pat", "del"], ["pt" + C, "tk" + C], bk, dur=2 * vd(66), n=2)
        add("V", "md" + C, lambda: [V.tensor_scalar(T.ea[:, w], a[:, 192:256], 2048.0, -4096.0, OP.is_ge, OP.mult)], (), ["ea" + C], bk, dur=vd(64))
        add("V", "md" + C, lambda: [V.tensor_tensor(T.ee[:, w], T.ea[:, w], a[:, 192:256], OP.add)], ["ea" + C], ["ee" + C], bk, dur=vd(64))

    acol = T["pb%d" % (NC - 1)][:, 64:65]

    def total(c, ts_, last):
        add("P", "pA", lambda: [P.matmul(acol, kb["ah%d" % t], dec(c, t, 64, 65), False, last) for t in ts_],
            ["de%d_%d" % (c, t) for t in ts_] + ["ah%d" % t for t in ts_], (), ["pb%d" % (NC - 1)], dur=pe(len(ts_)), n=len(ts_))

    def trial(k, c, t, bb, bkeys):
        a, b, o, C, K = T["pa%d" % c], T["pb%d" % c], 64 * c, str(c), str(k)
        ak, bk, w, G = ["pa" + C], ["pb" + C], slice(o, o + 64), b[:, 0:64]
        now[0] = CFG["N"][1 + 2 * k] + NC * (t - 1) + c
        kx, kn = measure(c, "mask" if t > 1 else k, T.sh0, slots, bb, bkeys, CFG[{1: "B%d" % c, 5: "C%d" % c}.get(t, "US")],
                         CFG["CUT"], "V" if t == 1 and c < CFG["VB"] else "G")
        if t == 1:
            before(k, c)
        add("P", "pd" + C, lambda: [half(a[:, 0:1])], ["cr3"], (), ak, dur=pe(1), kind="pw")
        dg = "dg%d" % (t + k if t == 5 else t)
        known = [("w%d_%d" % (k, u), dec(c, u), "de%d_%d" % (c, u)) for u in range(1, t)] + ([("w%d_6" % k, T.tk[:, w], "tk" + C)] if t == 5 else [])
        add("P", "pc" + C, lambda: [P.matmul(b[:, 0:65], kb[dg], T.one0[:, :], True, False)] + [P.matmul(G, kb[m], d, False, False) for m, d, _ in known],
            [dg, "one0"] + [x[0] for x in known] + [x[2] for x in known], (), bk, dur=pe(1 + len(known)), n=1 + len(known), kind="pg")
        counts = k == 0 and t == 5 and c == NC - 1
        if counts:
            for d in range(NC):
                total(d, range(1, 6 if d < c else 5), False)
        add("P", "pd" + C, lambda: pairs(0, c, ext(T.mx, c), 8 * k, False), kx + ["wsp" + K], (), ak, dur=pe(2.2), n=4)
        add("P", "pd" + C, lambda: pairs(0, c, ext(T.mn, c), 8 * k + 4, True), kn + ["wsn" + K], (), ak, dur=pe(2.2), n=4, kind="pe")
        p = 132 * c + (66 if t == 1 else 0)
        add("V", "de" + C, lambda: [V.tensor_scalar(dec(c, t, 0, 65), T.pt[:, p:p + 65], a[:, 0:1], 0.0, OP.mult, OP.is_gt)], ["pt" + C],
            ["de%d_%d" % (c, t)], ak, dur=vd(64))
        add("P", "pc" + C, lambda: [P.matmul(G, kb["w%d_%d" % (k, t)], dec(c, t), False, not counts)], ["de%d_%d" % (c, t), "w%d_%d" % (k, t)], (), bk, dur=pe(1))
        if counts:
            total(c, (5,), True)
        if t < 5 or k == 0:
            add("P", "px" + C, lambda: sums(c, a, 64, T.wh, True, False), ["wh" + C], (), ak, dur=pe(2), n=2, kind="pw2")
            if not counts:
                masked(c)

    def masked(c):
        C, w = str(c), slice(64 * c, 64 * c + 64)
        add("V", "mi" + C, lambda: [V.tensor_tensor(T.mi[:, w], T["pb" + C][:, 0:64], T.ee[:, w], OP.min)], ["ee" + C], ["mi" + C], ["pb" + C], dur=vd(64))

    def after_sum():
        add("V", "nb", lambda: [V.tensor_scalar(T.nb[:, :], T.bf[:, :], acol, None, OP.add)], ["b4a"], ["nb"], ["pb%d" % (NC - 1)], dur=vd(4))
        masked(NC - 1)

    def taken(c, eng):
        b, C, w = T["pb%d" % c], str(c), slice(64 * c, 64 * c + 64)
        if eng == "V":
            add("V", "md" + C, lambda: [V.tensor_scalar(T.mk[:, w], b[:, 0:64], 0.0, None, OP.is_gt)], (), ["mk" + C], ["pb" + C], dur=vd(64))
        else:
            add("S", "md" + C, lambda: [S.activation(T.mk[:, w], b[:, 0:64], AF.Relu, scale=1.0 / 2048)], (), ["mk" + C], ["pb" + C], dur=sd(64))

    def changed(c):
        a, C, w = T["pa%d" % c], str(c), slice(64 * c, 64 * c + 64)
        add("V", "md" + C, lambda: [V.tensor_tensor(T.md[:, w], T.mk[:, w], a[:, 256:320], OP.mult)], ["mk" + C], ["md" + C], ["pa" + C], dur=vd(64))
        add("V", "md" + C, lambda: [V.tensor_tensor(T.nw[:, w], T.md[:, w], a[:, 320:384], OP.add)], ["md" + C], ["new" + C], ["pa" + C], dur=vd(64))

    def trials(k, bb, bkeys):
        for t in range(1, 6):
            for c in range(NC):
                if k == 0 and t == 5 and c == NC - 1:
                    continue
                trial(k, c, t, bb, bkeys)
    order(0)
    trials(0, T.b4, ["b0", "b1", "b2", "b3"])
    round_consts(1)
    tc("ad4", "k5i", "ad0", 256.0, OP.mult, cf["ad0"], OP.add)
    tc("ad5", "k5i", "ad1", 256.0, OP.mult, cf["ad1"], OP.add)
    for t in range(1, 6):
        sc("ah%d" % t, kb["ah%d" % t], kb["w0_1"], "w0_1", HS[t - 1] / 4096.0)
    ts("b4a", T.bf[:, :], T.b4[:, :], "b0 b1 b2 b3 dc", 3968.0, OP.add, n=4)
    trial(0, NC - 1, 5, T.b4, ["b0", "b1", "b2", "b3"])
    kx, kn = [], []
    for c in range(NC):
        now[0] = CFG["N"][2] + c
        taken(c, CFG["MK"])
        keys = measure(c, "mask", T.sh0, slots, T.nb, ["nb"], CFG["D%d" % c], CFG["CUT"] if c >= CFG["DC"] else 0,
                       "V" if c < CFG["VD"] else "G", True)
        kx, kn = kx + keys[0], kn + keys[1]
        changed(c)
    nwk = ["new%d" % c for c in range(NC)]
    add("S", "un1", lambda: [S.activation(T.src[:, 0:128], T.nw[:, 0:256].indirect(T.po[:, 0:8]), AF.Copy)], nwk + ["po0"], ["srcA"], dur=65 + 106 * GR)
    add("V", "un2", lambda: [V.tensor_copy(T.src[:, 128:256], T.nw[:, 0:256].indirect(T.po[:, 8:16]))], nwk + ["po0"], ["srcB"], dur=50 + 106 * GR)
    add("S", "un1", lambda: [S.activation(T.ds[:, :], T.mn[:, :].indirect(T.po[:, 48:56]), AF.Identity, scale=-1.0)], kx + ["pend"], ["ds"], dur=65 + 106 * GR)
    add("V", "un2", lambda: [V.tensor_tensor(T.dd[:, :], T.mx[:, :].indirect(T.po[:, 48:56]), T.ds[:, :], OP.add)], kn + ["pend", "ds"], ["du"] + dkeys,
        dur=50 + 106 * GR)
    order(1)
    send(["qo", "qp"], (1, 2, 3), eng_of, lambda b: T.qo[:, :], lambda b: T.lq[:, 144 * b:144 * b + 144], "aq", "lq", 4000.0)

    def home(b, p, a, z):
        return T.lq[p, 144 * b + a:144 * b + z] if b else T.qo[p, a:z]
    add("Y", "douq", lambda: [Y.dma_start(T.yq[2 * (b ^ r) + j:2 * (b ^ r) + j + 1, :], home(b, slice(32 * b + 16 * j, 32 * b + 16 * j + 1), 0, 128))
                              for b in range(4) for j in (0, 1)], ["qo", "lq"], ["yq"], dur=800, lat=2000, n=8, inc=16)
    for b in range(4):
        cast("V", "ho", T.ho[rows(b), :], home(b, rows(b), 128, 144), 16, ["qp", "lq"], ["ho%d" % b])
    trials(1, T.nb, ["nb"])
    for c in range(NC):
        taken(c, "V" if c == NC - 1 else CFG["MK"])
        changed(c)

    i = None
    for a, z in CFG["HOME"]:
        for bs in ((off, near) if z == NC and CFG["APART"] else ((1, 2, 3),)):
            i = send(nwk[a:z], bs, eng_of, (lambda a, z: lambda b: T.nw[:, 64 * a:64 * z])(a, z),
                     (lambda a, z: lambda b: T.nw[:, 256 * b + 64 * a:256 * b + 64 * z])(a, z), "al", "ln", 3000.0, False, i)
    hk = nwk + ["ln", "ho0", "ho1", "ho2", "ho3"]
    add("S", "un1", lambda: [S.activation(T.ou[:, 0:256:2], T.nw[:, :].indirect(T.ho[:, 0:8]), AF.Identity, bias=2048.0)], hk, ["ouA"], dur=65 + 106 * GR)
    add("V", "un2", lambda: [V.tensor_scalar(T.ou[:, 1:256:2], T.nw[:, :].indirect(T.ho[:, 8:16]), 2048.0, None, OP.add)], hk, ["ouB"], dur=50 + 106 * GR)
    both("dou", lambda a, b: T.yu[b, :], lambda a, b: T.ou[a, :], ["ouA", "ouB"], "yu", 2000)
    return emit(T, dict(V=V, S=S, P=P, G=g, Y=Y), tasks, count)


def place(tasks, pred, succ, key, back):
    n, wake = len(tasks), CFG["WAKE"]
    need, st, busy = [len(p) for p in pred], [0.0] * n, {}
    pool = set(i for i in range(n) if need[i] == 0)
    while pool:
        i = min(pool, key=lambda j: (key[j], j))
        pool.discard(i)
        t = tasks[i]
        s, d = 0.0, t["dur"]
        for p, hard in pred[i]:
            s = max(s, st[p] + tasks[p]["dur"] + ((t if back else tasks[p])["lat"] + wake if hard else 0.0))
        if t["eng"] != "R":
            iv = busy.setdefault(t["eng"], [])
            j = len(iv)
            while j and iv[j - 1][1] > s:
                j -= 1
            while j < len(iv) and iv[j][0] < s + d - 0.001:
                s = max(s, iv[j][1])
                j += 1
            iv.insert(j, (s, s + d))
        st[i] = s
        for q, _ in succ[i]:
            need[q] -= 1
            if need[q] == 0:
                pool.add(q)
    return st


def emit(T, E, tasks, count):
    n, wake = len(tasks), CFG["WAKE"]
    pred, succ, before = [[] for _ in range(n)], [[] for _ in range(n)], {}
    for i in sorted((i for i in range(n) if tasks[i]["fixed"]), key=lambda i: tasks[i]["plan"]):
        if tasks[i]["eng"] in before:
            tasks[i]["soft"].add(before[tasks[i]["eng"]])
        before[tasks[i]["eng"]] = i
    for i, t in enumerate(tasks):
        p = before.get(t["sem"])
        if p is not None and t["eng"] != "R" and "spare" not in t:
            if t["sem"] not in FREE:
                t["deps"].add(p)
            elif tasks[p]["eng"] == t["eng"]:
                t["soft"].add(p)
        before[t["sem"]] = i
        for hard, ds in ((1, t["deps"]), (0, t["soft"] - t["deps"])):
            for d in ds:
                pred[i].append((d, hard))
                succ[d].append((i, hard))
    key = [0.0] * n
    for i in range(n - 1, -1, -1):
        t = tasks[i]
        late = min([key[j] - (wake + t["lat"] if h else 0.0) for j, h in succ[i] if j > i] or [CFG["N"][4] * CFG["Q"]]) - t["dur"]
        key[i] = late if t["plan"] is None else t["plan"]
        if t.get("spare"):
            key[i] = max(key[i] - CFG["AHEAD"], CFG["EARLY"] * CFG["Q"] + 1e-3 * key[i])
        if t["eng"] == "G" and "spare" not in t:
            key[i] -= 3 * CFG["Q"]
    st = place(tasks, pred, succ, key, False)
    best = (1e18, None)
    for k in range(CFG["ITERS"] + 1):
        end = max(s + t["dur"] + t["lat"] for s, t in zip(st, tasks))
        if end < best[0]:
            best = (end, st)
        if k < CFG["ITERS"]:
            sb = place(tasks, succ, pred, [-(s + t["dur"]) for s, t in zip(st, tasks)], True)
            st = place(tasks, pred, succ, [-(s + t["dur"]) for s, t in zip(sb, tasks)], False)
    st, seq = best[1], {}
    for i in sorted(range(n), key=lambda i: (st[i], i)):
        seq.setdefault(tasks[i]["eng"], []).append(i)
    for e, m in TURNS.items():
        mine = [i for i in seq[e] if "spare" in tasks[i]]
        count.pop(e, None)
        for j, i in enumerate(mine):
            tasks[i]["sem"], tasks[i]["val"] = "%sk%d" % (e.lower(), j % m), j // m + 1
            count[tasks[i]["sem"]] = j // m + 1
            if j >= m:
                tasks[i]["deps"].add(mine[j - m])
    clocks, after = {e: {} for e in E}, [None] * n
    pos, left = {e: 0 for e in seq}, n
    while left:
        was = left
        for e in seq:
            while pos[e] < len(seq[e]):
                i = seq[e][pos[e]]
                t = tasks[i]
                if any(after[d] is None for d in t["deps"]):
                    break
                ck = clocks.get(e, {})
                if e != "R":
                    for d in sorted(t["deps"], key=lambda d: (-st[d], -d) if tasks[d]["sem"] not in FREE else (-1e12 - d, 0)):
                        sem, val = tasks[d]["sem"], tasks[d]["val"]
                        if ck.get(sem, 0) < val:
                            E[e].wait_ge(T.sem[sem], int(val))
                            for s, v in after[d].items():
                                ck[s] = max(ck.get(s, 0), v)
                    for ins in t["fn"]():
                        ins.then_inc(T.sem[t["sem"]], t["inc"])
                after[i] = dict(ck) if e != "R" else {}
                after[i][t["sem"]] = max(ck.get(t["sem"], 0), t["val"])
                pos[e] += 1
                left -= 1
        assert left < was
    last = {t["sem"]: s + t["dur"] + t["lat"] for s, t in zip(st, tasks)}
    for s in sorted(count, key=lambda s: (last[s], s)):
        E["P"].wait_ge(T.sem[s], int(count[s]))
    return seq, st, tasks
